import numpy as np
import ml_dtypes


def mxq(x, axis, fmt="e4m3"):
    dtype, down = {"e4m3": (ml_dtypes.float8_e4m3fn, 7), "e5m2": (ml_dtypes.float8_e5m2, 14)}[fmt]
    v = np.moveaxis(np.asarray(x, np.float32).astype(ml_dtypes.bfloat16).astype(np.float64), axis, -1)
    blocks = v.reshape(v.shape[:-1] + (-1, 32))
    amax = np.abs(blocks).max(-1, keepdims=True)
    byte = np.maximum(np.where(amax > 0, np.frexp(amax)[1] - 1 + 127, 0) - down, 1)
    scale = np.exp2(byte - 127.0)
    codes = (blocks / scale).astype(np.float32).astype(dtype).astype(np.float64)
    return np.moveaxis((codes * scale).reshape(v.shape), -1, axis)


WIDE = False


def mx_kscale(k):
    if not WIDE:
        return np.ones(k)
    levels = np.array([10, -10, 5, -5, 0])
    if k % 512:
        return np.exp2(np.random.permutation(np.resize(levels, k // 32))).repeat(32)
    a = np.empty((k // 512, 16))
    for p in range(k // 512):
        a[p, :8] = np.random.permutation(np.resize(levels, 8))
        for g in range(8):
            far = levels[np.abs(levels - a[p, g]) >= 10]
            a[p, g + 8] = far[np.random.randint(len(far))]
    return np.exp2(a.ravel()).repeat(32)


def f64(x):
    return np.asarray(x).astype(np.float64)


def striped(idx):
    return np.tile(idx.reshape(-1, 16).T, (8, 1)).astype(np.uint16)


def unstriped(offs):
    return offs[:16].T.reshape(-1).astype(np.int64)


E2M1 = np.array([0.0, 0.5, 1.0, 1.5, 2.0, 3.0, 4.0, 6.0, -0.0, -0.5, -1.0, -1.5, -2.0, -3.0, -4.0, -6.0])


def pack_weight(w, fmt):
    k, n = w.shape
    w = f64(np.asarray(w, np.float32).astype(ml_dtypes.bfloat16)).reshape(k // 32, 32, n)
    amax = np.abs(w).max(1)
    if fmt == "e4m3":
        byte = np.frexp(amax)[1] - 1 + 127 - 7
    else:
        mant, ex = np.frexp(amax / 6.0)
        byte = np.where(mant > 0.5, ex, ex - 1) + 127
    byte = np.clip(np.where(amax > 0, byte, 1), 1, 254)
    scaled = (w * np.exp2(127.0 - byte)[:, None, :]).reshape(k, n).astype(np.float32)
    by_word = np.ascontiguousarray(scaled.reshape(k // 512, 128, 4, n).transpose(0, 1, 3, 2))
    if fmt == "e4m3":
        words = by_word.astype(ml_dtypes.float8_e4m3fn).view(np.uint8)
    else:
        c = by_word.astype(ml_dtypes.float4_e2m1fn).view(np.uint8) & 0xF
        words = (c[..., 0::2] | (c[..., 1::2] << 4)).reshape(k // 512, 128, 2 * n)
    return np.ascontiguousarray(words), np.ascontiguousarray(byte.astype(np.uint8).reshape(k // 512, 16, n))


def unpack_weight(words, scales, fmt):
    g, _, n = scales.shape
    words = np.ascontiguousarray(words).reshape(g, 128, n, -1)
    if fmt == "e4m3":
        vals = words.view(ml_dtypes.float8_e4m3fn).astype(np.float64)
    else:
        nib = np.empty((g, 128, n, 4), np.uint8)
        nib[..., 0::2] = words & 0xF
        nib[..., 1::2] = words >> 4
        vals = E2M1[nib]
    vals = vals * np.repeat(np.exp2(scales.astype(np.float64) - 127.0), 8, axis=1)[..., None]
    return vals.transpose(0, 1, 3, 2).reshape(g * 512, n)


def gelu(v):
    return 0.5 * v * (1.0 + np.tanh(np.sqrt(2.0 / np.pi) * (v + 0.044715 * v**3)))


def often(T, S):
    return np.random.permutation(T)[(T * np.random.uniform(0, 1, S) ** 4).astype(np.int64)]


K, K2, T, S, H, F = 1024, 512, 4096, 1024, 768, 512

def setup_inputs():
    n = np.random.standard_normal
    s = mx_kscale(K)[:, None]
    s2 = mx_kscale(K2)[:, None]
    u = mx_kscale(S)[:, None]
    tab_words, tab_scales = pack_weight(n((K, T)) * s, "e4m3")
    tab2 = np.abs(n((K2, T))) * np.exp(0.5 * n((1, T))) * s2
    tab2_words, tab2_scales = pack_weight(tab2, "e2m1")
    w1_words, w1_scales = pack_weight(n((K, H)) / np.sqrt(K) / s, "e2m1")
    w2 = 1.5 * np.abs(n((K2, H))) * np.exp(0.4 * n((1, H))) / K2 / s2
    w2_words, w2_scales = pack_weight(w2, "e4m3")
    return {
        "tab_words": tab_words, "tab_scales": tab_scales,
        "tab2_words": tab2_words, "tab2_scales": tab2_scales,
        "offs": striped(often(T, S)), "offs2": striped(often(T, S)),
        "w1_words": w1_words, "w1_scales": w1_scales,
        "w2_words": w2_words, "w2_scales": w2_scales,
        "w3": (0.7 * n((K2, H)) / np.sqrt(K2) / s2).astype(np.float32),
        "const": (0.5 * np.exp(0.3 * n(H))).astype(np.float32),
        "trust": (np.exp(0.3 * n(S)) * u[:, 0]).astype(np.float32),
        "grid": (n((S, F)) / np.sqrt(S) / u).astype(np.float32),
    }

def reference(tab_words, tab_scales, tab2_words, tab2_scales, offs, offs2, w1_words, w1_scales,
              w2_words, w2_scales, w3, const, trust, grid):
    v = unpack_weight(tab_words, tab_scales, "e4m3")[:, unstriped(offs)]
    v2 = unpack_weight(tab2_words, tab2_scales, "e2m1")[:, unstriped(offs2)]
    w1 = unpack_weight(w1_words, w1_scales, "e2m1")
    w2 = unpack_weight(w2_words, w2_scales, "e4m3")
    a = v.T @ w1 + v2.T @ mxq(f64(w3), 0, "e4m3")
    b = v2.T @ w2
    z = (a - b) / (np.abs(a) + (b + f64(const)[None, :]))
    z = z * f64(trust)[:, None]
    return mxq(z, 0, "e4m3").T @ mxq(f64(grid), 0, "e4m3")

@@ -1,0 +1,281 @@
+from contextlib import ExitStack
+
+import concourse.mybir as mybir
+from concourse.masks import make_identity
+
+K, K2, T, S, H, F = 1024, 512, 4096, 1024, 768, 512
+FLOPS = 2 * S * H * (K + 2 * K2) + 2 * S * H * F
+
+F32 = mybir.dt.float32
+BF16 = mybir.dt.bfloat16
+I32 = mybir.dt.int32
+U32 = mybir.dt.uint32
+U16 = mybir.dt.uint16
+U8 = mybir.dt.uint8
+FP8X4 = mybir.dt.float8_e4m3fn_x4
+FP4X4 = mybir.dt.float4_e2m1fn_x4
+ALU = mybir.AluOpType
+ACT = mybir.ActivationFunctionType
+
+P = 128
+PACK = 4
+HALF = P * PACK
+HALVES = S // HALF
+R_TILES = H // P
+W3_COLS = 256
+GRID_COLS = 256
+
+
+def weave(grouped, planes):
+    return (
+        grouped.rearrange("p (c i) t -> p c t i", i=2),
+        planes.rearrange("p t (c i) -> p c t i", i=2),
+    )
+
+
+def tile_list_moisture_downscaling_kernel(
+    tc, tab_words, tab_scales, tab2_words, tab2_scales, offs, offs2, w1_words, w1_scales,
+    w2_words, w2_scales, w3, const, trust, grid, out,
+):
+    nc = tc.nc
+    with ExitStack() as ctx:
+        keep = ctx.enter_context(tc.tile_pool(name="keep", bufs=1))
+        ring = ctx.enter_context(tc.tile_pool(name="ring", bufs=3))
+        psum_mm = ctx.enter_context(tc.psum_pool(name="psum_mm", bufs=3))
+        psum_t = ctx.enter_context(tc.psum_pool(name="psum_t", bufs=2))
+        psum_o = ctx.enter_context(tc.psum_pool(name="psum_o", bufs=1))
+
+        def held(name, shape, dtype):
+            return keep.tile(shape, dtype, name=name, align_bytes=64)
+
+        list1 = held("list1", [P, S // 16], U16)
+        list2 = held("list2", [P, S // 16], U16)
+        tab_w = [held("tab_w0", [P, T], I32)]
+        w3_first = held("w3_first", [P, PACK, W3_COLS], F32)
+        w3_raw = {0: w3_first[:]}
+        tab2_w = held("tab2_w", [P, T], U16)
+        tab_s = held("tab_s", [P, T], U8)
+        tab2_s = held("tab2_s", [P, T], U8)
+        v_w = [[held("v_w%d%d" % (a, h), [P, HALF], U32) for h in range(HALVES)] for a in range(2)]
+        v2_w = [held("v2_w%d" % h, [P, HALF], U16) for h in range(HALVES)]
+        v_rows = held("v_rows", [P, S], U8)
+        v_s = [held("v_s%d" % a, [P, S], U8) for a in range(2)]
+        v2_s = [held("v2_s%d" % h, [P, HALF], U8) for h in range(HALVES)]
+        w1_s = held("w1_s", [P, 2, H], U8)
+        w2_w = held("w2_w", [P, H], I32)
+        w2_s = held("w2_s", [P, H], U8)
+        w3_w = [held("w3_w%d" % c, [P, W3_COLS], U32) for c in range(H // W3_COLS)]
+        w3_s = [held("w3_s%d" % c, [P, W3_COLS], U8) for c in range(H // W3_COLS)]
+        grid_w = [held("grid_w%d" % h, [P, F], U32) for h in range(HALVES)]
+        grid_s = [held("grid_s%d" % h, [P, F], U8) for h in range(HALVES)]
+        const_rows = held("const_rows", [P, P], F32)
+        half_c = held("half_c", [P, R_TILES], F32)
+        trust_t = held("trust_t", [P, HALVES * PACK], F32)
+        ident = held("ident", [P, P], F32)
+
+        for plane in (tab2_s[:], tab_s[:], w1_s[:].rearrange("p a c -> p (a c)"), v_s[0][:], v_s[1][:]):
+            nc.vector.memset(plane.bitcast(I32), 0)
+        nc.gpsimd.memset(w2_s[:].bitcast(I32), 0)
+        for q in range(4):
+            nc.gpsimd.dma_start(w2_s[32 * q : 32 * q + 4, :].bitcast(I32), w2_scales[0, 4 * q : 4 * q + 4, :].bitcast(I32))
+        for q in range(4):
+            nc.gpsimd.dma_start(w1_s[32 * q : 32 * q + 4, :, :].bitcast(I32),
+                                w1_scales[:, 4 * q : 4 * q + 4, :].rearrange("a r c -> r a c").bitcast(I32))
+        nc.vector.memset(const_rows[0 : P - R_TILES, :], 0.0)
+        make_identity(nc, ident[:])
+
+        def load_tab(a, cols):
+            nc.sync.dma_start(tab_w[a][:, cols], tab_words[a].rearrange("p t i -> p (t i)").bitcast(I32)[:, cols])
+
+        def load_w3(c):
+            nc.sync.dma_start(w3_raw[c], w3[:, c * W3_COLS : (c + 1) * W3_COLS].rearrange("(p j) r -> p j r", j=PACK))
+
+        nc.sync.dma_start(list2[:], offs2)
+        nc.sync.dma_start(list1[:], offs)
+        nc.sync.dma_start(trust_t[:].rearrange("p (h t) -> p h t", t=PACK),
+                          trust.rearrange("(h p t) -> p h t", h=HALVES, t=PACK))
+        nc.sync.dma_start(const_rows[P - R_TILES : P, :], const.rearrange("(t p) -> t p", p=P))
+        for c0 in (0, T // 4):
+            nc.sync.dma_start(tab2_w[:].bitcast(I32)[:, c0 : c0 + T // 4], tab2_words[0].bitcast(I32)[:, c0 : c0 + T // 4])
+        nc.sync.dma_start(w2_w[:], w2_words[0].rearrange("p c i -> p (c i)").bitcast(I32))
+        load_tab(0, slice(0, T // 2))
+        for q in range(4):
+            nc.sync.dma_start(tab2_s[32 * q : 32 * q + 4, :].bitcast(I32), tab2_scales[0, 4 * q : 4 * q + 4, :].bitcast(I32))
+        load_tab(0, slice(T // 2, T))
+        load_w3(0)
+        for q in range(4):
+            nc.sync.dma_start(tab_s[32 * q + 4 : 32 * q + 12, :].bitcast(I32), tab_scales[:, 4 * q : 4 * q + 4, :].bitcast(I32))
+
+        rough = held("rough", [P, HALVES * PACK], F32)
+        root0 = held("root0", [P, HALVES * PACK], F32)
+        defect = held("defect", [P, HALVES * PACK], F32)
+        root = held("root", [P, HALVES * PACK], F32)
+        nc.scalar.activation(rough[:], trust_t[:], ACT.Abs_reciprocal_sqrt)
+        nc.vector.tensor_tensor(root0[:], rough[:], trust_t[:], ALU.mult)
+        nc.vector.scalar_tensor_tensor(defect[:], root0[:], -0.5, rough[:], ALU.mult, ALU.mult)
+        nc.vector.scalar_tensor_tensor(root[:], defect[:], 1.5, root0[:], ALU.add, ALU.mult)
+        tab_w.append(held("rough", [P, T], I32))
+        load_tab(1, slice(0, T))
+        w1_w = held("defect", [P, 2, 2 * H], U8)
+        nc.sync.dma_start(w1_w[:].bitcast(I32), w1_words.rearrange("a p c -> p a c").bitcast(I32))
+
+        def half_list(lst, h):
+            return lst[:, h * (HALF // 16) : (h + 1) * (HALF // 16)]
+
+        for h in range(HALVES):
+            nc.vector.tensor_copy(v2_w[h][:], tab2_w[:].indirect(half_list(list2, h)))
+        for h in range(HALVES):
+            nc.vector.tensor_copy(v2_s[h][:], tab2_s[:].indirect(half_list(list2, h)))
+        nc.vector.tensor_copy(v_rows[:], tab_s[:].indirect(list1[:]))
+        for a in range(2):
+            nc.sync.dma_start(v_s[a][0:100, :].bitcast(I32), v_rows[4 + 4 * a : 104 + 4 * a, :].bitcast(I32))
+
+        units = [(2 * pair + i, h) for pair in range(R_TILES // 2) for h in range(HALVES) for i in range(2)]
+
+        def by_slot(bank):
+            return bank[:].rearrange("p (q t) -> p t q", t=PACK)
+
+        half_b = {}
+
+        def make_b(u):
+            rt, h = units[u]
+            bank = psum_mm.tile([P, HALF], F32, name="mm")
+            nc.tensor.matmul_mx(bank[:], lhsT=w2_w[:, rt * P : (rt + 1) * P].bitcast(FP8X4),
+                                lhsT_scale=w2_s[:, rt * P : (rt + 1) * P],
+                                rhs=v2_w[h][:].bitcast(FP4X4), rhs_scale=v2_s[h][:],
+                                start=True, stop=True)
+            half_b[u] = held("half_b%d" % u, [P, PACK, P], F32)
+            nc.scalar.activation(half_b[u][:], by_slot(bank), ACT.Copy, scale=0.5)
+
+        def gather_tab(a, h):
+            nc.vector.tensor_copy(v_w[a][h][:], tab_w[a][:].bitcast(U32).indirect(half_list(list1, h)))
+
+        def round_cols(raw, cols, name):
+            grouped = ring.tile([P, cols.stop - cols.start, PACK], BF16, name=name, align_bytes=64)
+            dst, src = weave(grouped[:], raw[:, :, cols])
+            nc.scalar.copy(dst, src)
+            return grouped
+
+        def quantize(codes, scales, grouped):
+            nc.vector.quantize_mx(out=codes.bitcast(FP8X4), scales=scales, in_=grouped[:].rearrange("p c t -> p (c t)"))
+
+        for u in range(4):
+            make_b(u)
+        gather_tab(0, 0)
+        gather_tab(0, 1)
+        w3_rest = held("v_rows", [P, 2 * PACK * W3_COLS], F32)
+        for c in (1, 2):
+            w3_raw[c] = w3_rest[:, (c - 1) * PACK * W3_COLS : c * PACK * W3_COLS].rearrange("p (j r) -> p j r", j=PACK)
+            load_w3(c)
+        for u in range(4, 8):
+            make_b(u)
+        const_t = psum_o.tile([P, F], F32, name="o")
+        nc.tensor.transpose(const_t[:, 0:P], const_rows[:], ident[:])
+        nc.scalar.activation(half_c[:], const_t[:, P - R_TILES : P], ACT.Copy, scale=0.5)
+        grouped = round_cols(w3_raw[0], slice(0, W3_COLS), "grouped")
+        quantize(w3_w[0][:], w3_s[0][:], grouped)
+        for u in range(8, 12):
+            make_b(u)
+        gather_tab(1, 0)
+        gather_tab(1, 1)
+        grid_rows = held("rough", [P, HALVES * PACK * F], F32)
+        grid_raw = [grid_rows[:, h * PACK * F : (h + 1) * PACK * F].rearrange("p (j n) -> p j n", j=PACK) for h in range(HALVES)]
+        for h in range(HALVES):
+            nc.sync.dma_start(grid_raw[h], grid[h * HALF : (h + 1) * HALF, :].rearrange("(p j) n -> p j n", j=PACK))
+
+        a_bank, num, den, rsq, num_t, rsq_t, factor, z_bf, z_w, z_s = ({} for i in range(10))
+
+        def make_a(u):
+            rt, h = units[u]
+            bank = psum_mm.tile([P, HALF], F32, name="mm")
+            c, off = divmod(rt * P, W3_COLS)
+            nc.tensor.matmul_mx(bank[:], lhsT=w3_w[c][:, off : off + P].bitcast(FP8X4), lhsT_scale=w3_s[c][:, off : off + P],
+                                rhs=v2_w[h][:].bitcast(FP4X4), rhs_scale=v2_s[h][:],
+                                start=True, stop=False)
+            for a in range(2):
+                nc.tensor.matmul_mx(bank[:], lhsT=w1_w[:, a, 2 * rt * P : 2 * (rt + 1) * P].bitcast(FP4X4),
+                                    lhsT_scale=w1_s[:, a, rt * P : (rt + 1) * P],
+                                    rhs=v_w[a][h][:].bitcast(FP8X4), rhs_scale=v_s[a][:, h * HALF : (h + 1) * HALF],
+                                    start=False, stop=(a == 1))
+            a_bank[u] = bank
+
+        def make_num(u):
+            num[u] = ring.tile([P, PACK, P], F32, name="num")
+            nc.vector.scalar_tensor_tensor(num[u][:], by_slot(a_bank[u]), 0.5, half_b[u][:], ALU.mult, ALU.subtract)
+
+        def make_den(u):
+            den[u] = ring.tile([P, PACK, P], F32, name="den")
+            nc.vector.scalar_tensor_tensor(den[u][:], by_slot(a_bank[u]), 0.0, num[u][:], ALU.max, ALU.subtract)
+
+        def make_rsq(u):
+            rt, h = units[u]
+            rsq[u] = ring.tile([P, PACK, P], F32, name="rsq")
+            nc.scalar.activation(rsq[u][:], den[u][:], ACT.Abs_reciprocal_sqrt, bias=half_c[:, rt : rt + 1])
+
+        def turn(u):
+            num_t[u] = psum_t.tile([P, PACK, P], F32, name="num_t")
+            rsq_t[u] = psum_t.tile([P, PACK, P], F32, name="rsq_t")
+            for src, dst in ((num[u], num_t[u]), (rsq[u], rsq_t[u])):
+                for t in range(PACK):
+                    nc.tensor.transpose(dst[:, t, :], src[:, t, :], ident[:])
+
+        def make_factor(u):
+            rt, h = units[u]
+            factor[u] = ring.tile([P, PACK, P], F32, name="factor")
+            for t in range(PACK):
+                nc.scalar.activation(factor[u][:, t, :], rsq_t[u][:, t, :], ACT.Square,
+                                     scale=root[:, h * PACK + t : h * PACK + t + 1])
+
+        def make_z(u):
+            z_bf[u] = ring.tile([P, P, PACK], BF16, name="z_bf", align_bytes=64)
+            dst, src = weave(z_bf[u][:], num_t[u][:])
+            nc.vector.tensor_tensor(dst, src, weave(z_bf[u][:], factor[u][:])[1], ALU.mult)
+
+        def quantize_z(u):
+            z_w[u] = held("z_w%d" % u, [P, P], U32)
+            z_s[u] = held("z_s%d" % u, [P, P], U8)
+            quantize(z_w[u][:], z_s[u][:], z_bf[u])
+
+        def make_out(rt):
+            bank = psum_o.tile([P, F], F32, name="o")
+            for h in range(HALVES):
+                u = units.index((rt, h))
+                nc.tensor.matmul_mx(bank[:], lhsT=z_w[u][:].bitcast(FP8X4), lhsT_scale=z_s[u][:],
+                                    rhs=grid_w[h][:].bitcast(FP8X4), rhs_scale=grid_s[h][:],
+                                    start=(h == 0), stop=(h == HALVES - 1))
+            result = ring.tile([P, F], F32, name="result")
+            nc.scalar.copy(result[:], bank[:])
+            nc.sync.dma_start(out[rt * P : (rt + 1) * P, :], result[:])
+
+        side = [(w3_raw[c], slice(0, W3_COLS), w3_w[c][:], w3_s[c][:]) for c in (1, 2)]
+        for h in range(HALVES):
+            for n0 in range(0, F, GRID_COLS):
+                cols = slice(n0, n0 + GRID_COLS)
+                side.append((grid_raw[h], cols, grid_w[h][:, cols], grid_s[h][:, cols]))
+        side = dict(zip((0, 1, 3, 4, 5, 6), side))
+        rounded = {}
+        outs = {7: 0, 8: 1, 9: 2, 10: 3, 12: 4, 13: 5}
+
+        n = len(units)
+        make_a(0)
+        for i in range(n + 2):
+            if i + 1 < n:
+                make_a(i + 1)
+            if 1 <= i <= n:
+                turn(i - 1)
+                make_factor(i - 1)
+            if i < n:
+                make_num(i)
+            if 2 <= i < n + 2:
+                make_z(i - 2)
+            if i < n:
+                make_den(i)
+                make_rsq(i)
+            if 2 <= i < n + 2:
+                quantize_z(i - 2)
+            if i in side:
+                rounded[i] = round_cols(side[i][0], side[i][1], "grouped")
+            if i - 1 in side:
+                quantize(side[i - 1][2], side[i - 1][3], rounded[i - 1])
+            if i in outs:
+                make_out(outs[i])

@@ -50,16 +50,16 @@ def tile_list_moisture_downscaling_kernel(
 
         list1 = held("list1", [P, S // 16], U16)
         list2 = held("list2", [P, S // 16], U16)
-        tab_w = [held("tab_w0", [P, T], I32)]
+        tab_w = [held("tab_w%d" % a, [P, T], I32) for a in range(2)]
+        w1_w = held("w1_w", [P, 2, 2 * H], U8)
         w3_first = held("w3_first", [P, PACK, W3_COLS], F32)
         w3_raw = {0: w3_first[:]}
         tab2_w = held("tab2_w", [P, T], U16)
         tab_s = held("tab_s", [P, T], U8)
         tab2_s = held("tab2_s", [P, T], U8)
-        v_w = [[held("v_w%d%d" % (a, h), [P, HALF], U32) for h in range(HALVES)] for a in range(2)]
         v2_w = [held("v2_w%d" % h, [P, HALF], U16) for h in range(HALVES)]
         v_rows = held("v_rows", [P, S], U8)
-        v_s = [held("v_s%d" % a, [P, S], U8) for a in range(2)]
+        v_s = [v_rows, held("v_s1", [P, S], U8)]
         v2_s = [held("v2_s%d" % h, [P, HALF], U8) for h in range(HALVES)]
         w1_s = held("w1_s", [P, 2, H], U8)
         w2_w = held("w2_w", [P, H], I32)
@@ -73,18 +73,23 @@ def tile_list_moisture_downscaling_kernel(
         trust_t = held("trust_t", [P, HALVES * PACK], F32)
         ident = held("ident", [P, P], F32)
 
-        for plane in (tab2_s[:], tab_s[:], w1_s[:].rearrange("p a c -> p (a c)"), v_s[0][:], v_s[1][:]):
+        for plane in (tab2_s[:], tab_s[:], w1_s[:].rearrange("p a c -> p (a c)"), v_s[1][:]):
             nc.vector.memset(plane.bitcast(I32), 0)
         nc.gpsimd.memset(w2_s[:].bitcast(I32), 0)
-        for q in range(4):
-            nc.gpsimd.dma_start(w2_s[32 * q : 32 * q + 4, :].bitcast(I32), w2_scales[0, 4 * q : 4 * q + 4, :].bitcast(I32))
+
+        def load_w2_scales(queue, q):
+            queue.dma_start(w2_s[32 * q : 32 * q + 4, :].bitcast(I32), w2_scales[0, 4 * q : 4 * q + 4, :].bitcast(I32))
+
+        for q in range(2, 4):
+            load_w2_scales(nc.gpsimd, q)
+        nc.gpsimd.memset(const_rows[0 : P - R_TILES, :], 0.0)
+        make_identity(nc, ident[:])
         for q in range(4):
             nc.gpsimd.dma_start(w1_s[32 * q : 32 * q + 4, :, :].bitcast(I32),
                                 w1_scales[:, 4 * q : 4 * q + 4, :].rearrange("a r c -> r a c").bitcast(I32))
-        nc.vector.memset(const_rows[0 : P - R_TILES, :], 0.0)
-        make_identity(nc, ident[:])
 
-        def load_tab(a, cols):
+        def load_tab(a, part):
+            cols = slice(part * T // 2, (part + 1) * T // 2)
             nc.sync.dma_start(tab_w[a][:, cols], tab_words[a].rearrange("p t i -> p (t i)").bitcast(I32)[:, cols])
 
         def load_w3(c):
@@ -94,17 +99,23 @@ def tile_list_moisture_downscaling_kernel(
         nc.sync.dma_start(list1[:], offs)
         nc.sync.dma_start(trust_t[:].rearrange("p (h t) -> p h t", t=PACK),
                           trust.rearrange("(h p t) -> p h t", h=HALVES, t=PACK))
-        nc.sync.dma_start(const_rows[P - R_TILES : P, :], const.rearrange("(t p) -> t p", p=P))
-        for c0 in (0, T // 4):
-            nc.sync.dma_start(tab2_w[:].bitcast(I32)[:, c0 : c0 + T // 4], tab2_words[0].bitcast(I32)[:, c0 : c0 + T // 4])
+        for c0 in range(0, T // 2, T // 8):
+            nc.sync.dma_start(tab2_w[:].bitcast(I32)[:, c0 : c0 + T // 8], tab2_words[0].bitcast(I32)[:, c0 : c0 + T // 8])
         nc.sync.dma_start(w2_w[:], w2_words[0].rearrange("p c i -> p (c i)").bitcast(I32))
-        load_tab(0, slice(0, T // 2))
+        load_tab(0, 0)
         for q in range(4):
             nc.sync.dma_start(tab2_s[32 * q : 32 * q + 4, :].bitcast(I32), tab2_scales[0, 4 * q : 4 * q + 4, :].bitcast(I32))
-        load_tab(0, slice(T // 2, T))
+        for q in range(2):
+            load_w2_scales(nc.sync, q)
+        load_tab(0, 1)
+        for r in range(4):
+            nc.sync.dma_start(tab_s[r:P:16, :].bitcast(I32),
+                              tab_scales.rearrange("a (q r) t -> r q a t", r=4)[r].bitcast(I32))
         load_w3(0)
-        for q in range(4):
-            nc.sync.dma_start(tab_s[32 * q + 4 : 32 * q + 12, :].bitcast(I32), tab_scales[:, 4 * q : 4 * q + 4, :].bitcast(I32))
+        load_tab(1, 0)
+        load_tab(1, 1)
+        nc.sync.dma_start(w1_w[:].bitcast(I32), w1_words.rearrange("a p c -> p a c").bitcast(I32))
+        nc.sync.dma_start(const_rows[P - R_TILES : P, :], const.rearrange("(t p) -> t p", p=P))
 
         rough = held("rough", [P, HALVES * PACK], F32)
         root0 = held("root0", [P, HALVES * PACK], F32)
@@ -114,10 +125,6 @@ def tile_list_moisture_downscaling_kernel(
         nc.vector.tensor_tensor(root0[:], rough[:], trust_t[:], ALU.mult)
         nc.vector.scalar_tensor_tensor(defect[:], root0[:], -0.5, rough[:], ALU.mult, ALU.mult)
         nc.vector.scalar_tensor_tensor(root[:], defect[:], 1.5, root0[:], ALU.add, ALU.mult)
-        tab_w.append(held("rough", [P, T], I32))
-        load_tab(1, slice(0, T))
-        w1_w = held("defect", [P, 2, 2 * H], U8)
-        nc.sync.dma_start(w1_w[:].bitcast(I32), w1_words.rearrange("a p c -> p a c").bitcast(I32))
 
         def half_list(lst, h):
             return lst[:, h * (HALF // 16) : (h + 1) * (HALF // 16)]
@@ -127,8 +134,7 @@ def tile_list_moisture_downscaling_kernel(
         for h in range(HALVES):
             nc.vector.tensor_copy(v2_s[h][:], tab2_s[:].indirect(half_list(list2, h)))
         nc.vector.tensor_copy(v_rows[:], tab_s[:].indirect(list1[:]))
-        for a in range(2):
-            nc.sync.dma_start(v_s[a][0:100, :].bitcast(I32), v_rows[4 + 4 * a : 104 + 4 * a, :].bitcast(I32))
+        nc.gpsimd.dma_start(v_s[1][0:100, :].bitcast(I32), v_rows[16:116, :].bitcast(I32))
 
         units = [(2 * pair + i, h) for pair in range(R_TILES // 2) for h in range(HALVES) for i in range(2)]
 
@@ -147,11 +153,9 @@ def tile_list_moisture_downscaling_kernel(
             half_b[u] = held("half_b%d" % u, [P, PACK, P], F32)
             nc.scalar.activation(half_b[u][:], by_slot(bank), ACT.Copy, scale=0.5)
 
-        def gather_tab(a, h):
-            nc.vector.tensor_copy(v_w[a][h][:], tab_w[a][:].bitcast(U32).indirect(half_list(list1, h)))
 
         def round_cols(raw, cols, name):
-            grouped = ring.tile([P, cols.stop - cols.start, PACK], BF16, name=name, align_bytes=64)
+            grouped = held(name, [P, cols.stop - cols.start, PACK], BF16)
             dst, src = weave(grouped[:], raw[:, :, cols])
             nc.scalar.copy(dst, src)
             return grouped
@@ -161,28 +165,30 @@ def tile_list_moisture_downscaling_kernel(
 
         for u in range(4):
             make_b(u)
-        gather_tab(0, 0)
-        gather_tab(0, 1)
-        w3_rest = held("v_rows", [P, 2 * PACK * W3_COLS], F32)
+        v0_w = held("tab_s", [P, S], U32)
+        nc.vector.tensor_copy(v0_w[:], tab_w[0][:].bitcast(U32).indirect(list1[:]))
+        w3_rest = held("tab_w0", [P, 2 * PACK * W3_COLS], F32)
         for c in (1, 2):
             w3_raw[c] = w3_rest[:, (c - 1) * PACK * W3_COLS : c * PACK * W3_COLS].rearrange("p (j r) -> p j r", j=PACK)
             load_w3(c)
         for u in range(4, 8):
             make_b(u)
-        const_t = psum_o.tile([P, F], F32, name="o")
-        nc.tensor.transpose(const_t[:, 0:P], const_rows[:], ident[:])
-        nc.scalar.activation(half_c[:], const_t[:, P - R_TILES : P], ACT.Copy, scale=0.5)
         grouped = round_cols(w3_raw[0], slice(0, W3_COLS), "grouped")
         quantize(w3_w[0][:], w3_s[0][:], grouped)
+        v1_w = held("grouped", [P, S], U32)
         for u in range(8, 12):
             make_b(u)
-        gather_tab(1, 0)
-        gather_tab(1, 1)
-        grid_rows = held("rough", [P, HALVES * PACK * F], F32)
+        const_t = psum_mm.tile([P, HALF], F32, name="mm")
+        nc.tensor.transpose(const_t[:, 0:P], const_rows[:], ident[:])
+        nc.scalar.activation(half_c[:], const_t[:, P - R_TILES : P], ACT.Copy, scale=0.5)
+        for h in range(HALVES):
+            nc.vector.tensor_copy(v1_w[:, h * HALF : (h + 1) * HALF], tab_w[1][:].bitcast(U32).indirect(half_list(list1, h)))
+        grid_rows = held("tab_w1", [P, HALVES * PACK * F], F32)
         grid_raw = [grid_rows[:, h * PACK * F : (h + 1) * PACK * F].rearrange("p (j n) -> p j n", j=PACK) for h in range(HALVES)]
         for h in range(HALVES):
             nc.sync.dma_start(grid_raw[h], grid[h * HALF : (h + 1) * HALF, :].rearrange("(p j) n -> p j n", j=PACK))
 
+        v_w = [[words[:, h * HALF : (h + 1) * HALF] for h in range(HALVES)] for words in (v0_w, v1_w)]
         a_bank, num, den, rsq, num_t, rsq_t, factor, z_bf, z_w, z_s = ({} for i in range(10))
 
         def make_a(u):
@@ -195,7 +201,7 @@ def tile_list_moisture_downscaling_kernel(
             for a in range(2):
                 nc.tensor.matmul_mx(bank[:], lhsT=w1_w[:, a, 2 * rt * P : 2 * (rt + 1) * P].bitcast(FP4X4),
                                     lhsT_scale=w1_s[:, a, rt * P : (rt + 1) * P],
-                                    rhs=v_w[a][h][:].bitcast(FP8X4), rhs_scale=v_s[a][:, h * HALF : (h + 1) * HALF],
+                                    rhs=v_w[a][h].bitcast(FP8X4), rhs_scale=v_s[a][:, h * HALF : (h + 1) * HALF],
                                     start=False, stop=(a == 1))
             a_bank[u] = bank
 
@@ -252,9 +258,9 @@ def tile_list_moisture_downscaling_kernel(
             for n0 in range(0, F, GRID_COLS):
                 cols = slice(n0, n0 + GRID_COLS)
                 side.append((grid_raw[h], cols, grid_w[h][:, cols], grid_s[h][:, cols]))
-        side = dict(zip((0, 1, 3, 4, 5, 6), side))
+        side = dict(zip(range(1, 7), side))
         rounded = {}
-        outs = {7: 0, 8: 1, 9: 2, 10: 3, 12: 4, 13: 5}
+        outs = {8: 0, 9: 1, 10: 2, 11: 3, 12: 4, 13: 5}
 
         n = len(units)
         make_a(0)
@@ -274,7 +280,7 @@ def tile_list_moisture_downscaling_kernel(
             if 2 <= i < n + 2:
                 quantize_z(i - 2)
             if i in side:
-                rounded[i] = round_cols(side[i][0], side[i][1], "grouped")
+                rounded[i] = round_cols(side[i][0], side[i][1], "half_b%d" % i)
             if i - 1 in side:
                 quantize(side[i - 1][2], side[i - 1][3], rounded[i - 1])
             if i in outs:

@@ -50,10 +50,7 @@ def tile_list_moisture_downscaling_kernel(
 
         list1 = held("list1", [P, S // 16], U16)
         list2 = held("list2", [P, S // 16], U16)
-        tab_w = [held("tab_w%d" % a, [P, T], I32) for a in range(2)]
-        w1_w = held("w1_w", [P, 2, 2 * H], U8)
-        w3_first = held("w3_first", [P, PACK, W3_COLS], F32)
-        w3_raw = {0: w3_first[:]}
+        tab_w = [held("tab_w0", [P, T], I32)]
         tab2_w = held("tab2_w", [P, T], U16)
         tab_s = held("tab_s", [P, T], U8)
         tab2_s = held("tab2_s", [P, T], U8)
@@ -73,20 +70,19 @@ def tile_list_moisture_downscaling_kernel(
         trust_t = held("trust_t", [P, HALVES * PACK], F32)
         ident = held("ident", [P, P], F32)
 
-        for plane in (tab2_s[:], tab_s[:], w1_s[:].rearrange("p a c -> p (a c)"), v_s[1][:]):
+        for plane in (tab2_s[:], w2_s[:], tab_s[:], w1_s[:].rearrange("p a c -> p (a c)"), v_s[1][:]):
             nc.vector.memset(plane.bitcast(I32), 0)
-        nc.gpsimd.memset(w2_s[:].bitcast(I32), 0)
 
-        def load_w2_scales(queue, q):
-            queue.dma_start(w2_s[32 * q : 32 * q + 4, :].bitcast(I32), w2_scales[0, 4 * q : 4 * q + 4, :].bitcast(I32))
+        def load_w2_scales(queue, r):
+            queue.dma_start(w2_s[r:P:32, :].bitcast(I32), w2_scales[0, r:16:4, :].bitcast(I32))
 
         for q in range(2, 4):
             load_w2_scales(nc.gpsimd, q)
         nc.gpsimd.memset(const_rows[0 : P - R_TILES, :], 0.0)
         make_identity(nc, ident[:])
-        for q in range(4):
-            nc.gpsimd.dma_start(w1_s[32 * q : 32 * q + 4, :, :].bitcast(I32),
-                                w1_scales[:, 4 * q : 4 * q + 4, :].rearrange("a r c -> r a c").bitcast(I32))
+        for r in range(4):
+            nc.gpsimd.dma_start(w1_s[r:P:32, :, :].bitcast(I32),
+                                w1_scales[:, r:16:4, :].rearrange("a q c -> q a c").bitcast(I32))
 
         def load_tab(a, part):
             cols = slice(part * T // 2, (part + 1) * T // 2)
@@ -103,19 +99,15 @@ def tile_list_moisture_downscaling_kernel(
             nc.sync.dma_start(tab2_w[:].bitcast(I32)[:, c0 : c0 + T // 8], tab2_words[0].bitcast(I32)[:, c0 : c0 + T // 8])
         nc.sync.dma_start(w2_w[:], w2_words[0].rearrange("p c i -> p (c i)").bitcast(I32))
         load_tab(0, 0)
-        for q in range(4):
-            nc.sync.dma_start(tab2_s[32 * q : 32 * q + 4, :].bitcast(I32), tab2_scales[0, 4 * q : 4 * q + 4, :].bitcast(I32))
+        for r in range(4):
+            nc.sync.dma_start(tab2_s[r:P:32, :].bitcast(I32), tab2_scales[0, r:16:4, :].bitcast(I32))
         for q in range(2):
             load_w2_scales(nc.sync, q)
         load_tab(0, 1)
+        nc.sync.dma_start(const_rows[P - R_TILES : P, :], const.rearrange("(t p) -> t p", p=P))
         for r in range(4):
             nc.sync.dma_start(tab_s[r:P:16, :].bitcast(I32),
                               tab_scales.rearrange("a (q r) t -> r q a t", r=4)[r].bitcast(I32))
-        load_w3(0)
-        load_tab(1, 0)
-        load_tab(1, 1)
-        nc.sync.dma_start(w1_w[:].bitcast(I32), w1_words.rearrange("a p c -> p a c").bitcast(I32))
-        nc.sync.dma_start(const_rows[P - R_TILES : P, :], const.rearrange("(t p) -> t p", p=P))
 
         rough = held("rough", [P, HALVES * PACK], F32)
         root0 = held("root0", [P, HALVES * PACK], F32)
@@ -125,6 +117,14 @@ def tile_list_moisture_downscaling_kernel(
         nc.vector.tensor_tensor(root0[:], rough[:], trust_t[:], ALU.mult)
         nc.vector.scalar_tensor_tensor(defect[:], root0[:], -0.5, rough[:], ALU.mult, ALU.mult)
         nc.vector.scalar_tensor_tensor(root[:], defect[:], 1.5, root0[:], ALU.add, ALU.mult)
+        w3_first = held("rough", [P, PACK, W3_COLS], F32)
+        w3_raw = {0: w3_first[:]}
+        load_w3(0)
+        tab_w.append(held("root0", [P, T], I32))
+        load_tab(1, 0)
+        load_tab(1, 1)
+        w1_w = held("defect", [P, 2, 2 * H], U8)
+        nc.sync.dma_start(w1_w[:].bitcast(I32), w1_words.rearrange("a p c -> p a c").bitcast(I32))
 
         def half_list(lst, h):
             return lst[:, h * (HALF // 16) : (h + 1) * (HALF // 16)]
@@ -158,10 +158,10 @@ def tile_list_moisture_downscaling_kernel(
             grouped = held(name, [P, cols.stop - cols.start, PACK], BF16)
             dst, src = weave(grouped[:], raw[:, :, cols])
             nc.scalar.copy(dst, src)
-            return grouped
+            return grouped[:]
 
         def quantize(codes, scales, grouped):
-            nc.vector.quantize_mx(out=codes.bitcast(FP8X4), scales=scales, in_=grouped[:].rearrange("p c t -> p (c t)"))
+            nc.vector.quantize_mx(out=codes.bitcast(FP8X4), scales=scales, in_=grouped.rearrange("p c t -> p (c t)"))
 
         for u in range(4):
             make_b(u)
@@ -183,7 +183,7 @@ def tile_list_moisture_downscaling_kernel(
         nc.scalar.activation(half_c[:], const_t[:, P - R_TILES : P], ACT.Copy, scale=0.5)
         for h in range(HALVES):
             nc.vector.tensor_copy(v1_w[:, h * HALF : (h + 1) * HALF], tab_w[1][:].bitcast(U32).indirect(half_list(list1, h)))
-        grid_rows = held("tab_w1", [P, HALVES * PACK * F], F32)
+        grid_rows = held("root0", [P, HALVES * PACK * F], F32)
         grid_raw = [grid_rows[:, h * PACK * F : (h + 1) * PACK * F].rearrange("p (j n) -> p j n", j=PACK) for h in range(HALVES)]
         for h in range(HALVES):
             nc.sync.dma_start(grid_raw[h], grid[h * HALF : (h + 1) * HALF, :].rearrange("(p j) n -> p j n", j=PACK))
@@ -233,25 +233,43 @@ def tile_list_moisture_downscaling_kernel(
                                      scale=root[:, h * PACK + t : h * PACK + t + 1])
 
         def make_z(u):
-            z_bf[u] = ring.tile([P, P, PACK], BF16, name="z_bf", align_bytes=64)
-            dst, src = weave(z_bf[u][:], num_t[u][:])
-            nc.vector.tensor_tensor(dst, src, weave(z_bf[u][:], factor[u][:])[1], ALU.mult)
+            if u % 2 == 0:
+                z_bf[u // 2] = ring.tile([P, 2 * P, PACK], BF16, name="z_bf", align_bytes=64)
+            mine = z_bf[u // 2][:, (u % 2) * P : (u % 2 + 1) * P, :]
+            dst, src = weave(mine, num_t[u][:])
+            nc.vector.tensor_tensor(dst, src, weave(mine, factor[u][:])[1], ALU.mult)
 
-        def quantize_z(u):
-            z_w[u] = held("z_w%d" % u, [P, P], U32)
-            z_s[u] = held("z_s%d" % u, [P, P], U8)
-            quantize(z_w[u][:], z_s[u][:], z_bf[u])
+        def quantize_z(first, count):
+            codes = held("z_w%d" % first, [P, count * P], U32)
+            scales = held("z_s%d" % first, [P, count * P], U8)
+            start = (first % 2) * P
+            quantize(codes[:], scales[:], z_bf[first // 2][:, start : start + count * P, :])
+            for i in range(count):
+                z_w[first + i] = codes[:, i * P : (i + 1) * P]
+                z_s[first + i] = scales[:, i * P : (i + 1) * P]
 
         def make_out(rt):
             bank = psum_o.tile([P, F], F32, name="o")
             for h in range(HALVES):
                 u = units.index((rt, h))
-                nc.tensor.matmul_mx(bank[:], lhsT=z_w[u][:].bitcast(FP8X4), lhsT_scale=z_s[u][:],
+                nc.tensor.matmul_mx(bank[:], lhsT=z_w[u].bitcast(FP8X4), lhsT_scale=z_s[u],
                                     rhs=grid_w[h][:].bitcast(FP8X4), rhs_scale=grid_s[h][:],
                                     start=(h == 0), stop=(h == HALVES - 1))
             result = ring.tile([P, F], F32, name="result")
             nc.scalar.copy(result[:], bank[:])
             nc.sync.dma_start(out[rt * P : (rt + 1) * P, :], result[:])
+
+        last_banks = []
+
+        def last_pass(h):
+            u = units.index((R_TILES - 1, h))
+            for half in range(2):
+                if h == 0:
+                    last_banks.append(psum_mm.tile([P, HALF], F32, name="mm"))
+                cols = slice(half * F // 2, (half + 1) * F // 2)
+                nc.tensor.matmul_mx(last_banks[half][:, 0 : F // 2], lhsT=z_w[u].bitcast(FP8X4), lhsT_scale=z_s[u],
+                                    rhs=grid_w[h][:, cols].bitcast(FP8X4), rhs_scale=grid_s[h][:, cols],
+                                    start=(h == 0), stop=(h == HALVES - 1))
 
         side = [(w3_raw[c], slice(0, W3_COLS), w3_w[c][:], w3_s[c][:]) for c in (1, 2)]
         for h in range(HALVES):
@@ -260,7 +278,7 @@ def tile_list_moisture_downscaling_kernel(
                 side.append((grid_raw[h], cols, grid_w[h][:, cols], grid_s[h][:, cols]))
         side = dict(zip(range(1, 7), side))
         rounded = {}
-        outs = {8: 0, 9: 1, 10: 2, 11: 3, 12: 4, 13: 5}
+        outs = {8: 0, 9: 1, 10: 2, 11: 3, 12: 4}
 
         n = len(units)
         make_a(0)
@@ -277,11 +295,20 @@ def tile_list_moisture_downscaling_kernel(
             if i < n:
                 make_den(i)
                 make_rsq(i)
-            if 2 <= i < n + 2:
-                quantize_z(i - 2)
+            if i - 2 >= n - 2:
+                quantize_z(i - 2, 1)
+            elif i >= 3 and i % 2 == 1:
+                quantize_z(i - 3, 2)
+            if i == n:
+                last_pass(0)
             if i in side:
                 rounded[i] = round_cols(side[i][0], side[i][1], "half_b%d" % i)
             if i - 1 in side:
                 quantize(side[i - 1][2], side[i - 1][3], rounded[i - 1])
             if i in outs:
                 make_out(outs[i])
+        last_pass(1)
+        for half, copy in enumerate((nc.scalar.copy, nc.vector.tensor_copy)):
+            part = ring.tile([P, F // 2], F32, name="part")
+            copy(part[:], last_banks[half][:, 0 : F // 2])
+            nc.sync.dma_start(out[H - P : H, half * F // 2 : (half + 1) * F // 2], part[:])

@@ -22,14 +22,16 @@ PACK = 4
 HALF = P * PACK
 HALVES = S // HALF
 R_TILES = H // P
-W3_COLS = 256
-GRID_COLS = 256
+SCALE_ROWS = 16
+PIECE = 256
+PASS1_ROW = 16
+LIVE_ROWS = 100
 
 
-def weave(grouped, planes):
+def weave(grouped, slots):
     return (
         grouped.rearrange("p (c i) t -> p c t i", i=2),
-        planes.rearrange("p t (c i) -> p c t i", i=2),
+        slots.rearrange("p t (c i) -> p c t i", i=2),
     )
 
 
@@ -55,14 +57,14 @@ def tile_list_moisture_downscaling_kernel(
         tab_s = held("tab_s", [P, T], U8)
         tab2_s = held("tab2_s", [P, T], U8)
         v2_w = [held("v2_w%d" % h, [P, HALF], U16) for h in range(HALVES)]
-        v_rows = held("v_rows", [P, S], U8)
-        v_s = [v_rows, held("v_s1", [P, S], U8)]
+        v_s0 = held("v_s0", [P, S], U8)
+        v_s = [v_s0, held("v_s1", [P, S], U8)]
         v2_s = [held("v2_s%d" % h, [P, HALF], U8) for h in range(HALVES)]
         w1_s = held("w1_s", [P, 2, H], U8)
         w2_w = held("w2_w", [P, H], I32)
         w2_s = held("w2_s", [P, H], U8)
-        w3_w = [held("w3_w%d" % c, [P, W3_COLS], U32) for c in range(H // W3_COLS)]
-        w3_s = [held("w3_s%d" % c, [P, W3_COLS], U8) for c in range(H // W3_COLS)]
+        w3_w = [held("w3_w%d" % c, [P, PIECE], U32) for c in range(H // PIECE)]
+        w3_s = [held("w3_s%d" % c, [P, PIECE], U8) for c in range(H // PIECE)]
         grid_w = [held("grid_w%d" % h, [P, F], U32) for h in range(HALVES)]
         grid_s = [held("grid_s%d" % h, [P, F], U8) for h in range(HALVES)]
         const_rows = held("const_rows", [P, P], F32)
@@ -70,26 +72,26 @@ def tile_list_moisture_downscaling_kernel(
         trust_t = held("trust_t", [P, HALVES * PACK], F32)
         ident = held("ident", [P, P], F32)
 
-        for plane in (tab2_s[:], w2_s[:], tab_s[:], w1_s[:].rearrange("p a c -> p (a c)"), v_s[1][:]):
-            nc.vector.memset(plane.bitcast(I32), 0)
+        for scale_tile in (tab2_s[:], w2_s[:], tab_s[:], w1_s[:].rearrange("p a c -> p (a c)"), v_s[1][:]):
+            nc.vector.memset(scale_tile.bitcast(I32), 0)
 
         def load_w2_scales(queue, r):
-            queue.dma_start(w2_s[r:P:32, :].bitcast(I32), w2_scales[0, r:16:4, :].bitcast(I32))
+            queue.dma_start(w2_s[r:P:32, :].bitcast(I32), w2_scales[0, r:SCALE_ROWS:4, :].bitcast(I32))
 
-        for q in range(2, 4):
-            load_w2_scales(nc.gpsimd, q)
+        for r in range(2, 4):
+            load_w2_scales(nc.gpsimd, r)
         nc.gpsimd.memset(const_rows[0 : P - R_TILES, :], 0.0)
         make_identity(nc, ident[:])
         for r in range(4):
             nc.gpsimd.dma_start(w1_s[r:P:32, :, :].bitcast(I32),
-                                w1_scales[:, r:16:4, :].rearrange("a q c -> q a c").bitcast(I32))
+                                w1_scales[:, r:SCALE_ROWS:4, :].rearrange("a q c -> q a c").bitcast(I32))
 
         def load_tab(a, part):
             cols = slice(part * T // 2, (part + 1) * T // 2)
             nc.sync.dma_start(tab_w[a][:, cols], tab_words[a].rearrange("p t i -> p (t i)").bitcast(I32)[:, cols])
 
         def load_w3(c):
-            nc.sync.dma_start(w3_raw[c], w3[:, c * W3_COLS : (c + 1) * W3_COLS].rearrange("(p j) r -> p j r", j=PACK))
+            nc.sync.dma_start(w3_raw[c], w3[:, c * PIECE : (c + 1) * PIECE].rearrange("(p j) r -> p j r", j=PACK))
 
         nc.sync.dma_start(list2[:], offs2)
         nc.sync.dma_start(list1[:], offs)
@@ -100,13 +102,13 @@ def tile_list_moisture_downscaling_kernel(
         nc.sync.dma_start(w2_w[:], w2_words[0].rearrange("p c i -> p (c i)").bitcast(I32))
         load_tab(0, 0)
         for r in range(4):
-            nc.sync.dma_start(tab2_s[r:P:32, :].bitcast(I32), tab2_scales[0, r:16:4, :].bitcast(I32))
-        for q in range(2):
-            load_w2_scales(nc.sync, q)
+            nc.sync.dma_start(tab2_s[r:P:32, :].bitcast(I32), tab2_scales[0, r:SCALE_ROWS:4, :].bitcast(I32))
+        for r in range(2):
+            load_w2_scales(nc.sync, r)
         load_tab(0, 1)
         nc.sync.dma_start(const_rows[P - R_TILES : P, :], const.rearrange("(t p) -> t p", p=P))
         for r in range(4):
-            nc.sync.dma_start(tab_s[r:P:16, :].bitcast(I32),
+            nc.sync.dma_start(tab_s[r:P:PASS1_ROW, :].bitcast(I32),
                               tab_scales.rearrange("a (q r) t -> r q a t", r=4)[r].bitcast(I32))
 
         rough = held("rough", [P, HALVES * PACK], F32)
@@ -117,7 +119,8 @@ def tile_list_moisture_downscaling_kernel(
         nc.vector.tensor_tensor(root0[:], rough[:], trust_t[:], ALU.mult)
         nc.vector.scalar_tensor_tensor(defect[:], root0[:], -0.5, rough[:], ALU.mult, ALU.mult)
         nc.vector.scalar_tensor_tensor(root[:], defect[:], 1.5, root0[:], ALU.add, ALU.mult)
-        w3_first = held("rough", [P, PACK, W3_COLS], F32)
+
+        w3_first = held("rough", [P, PACK, PIECE], F32)
         w3_raw = {0: w3_first[:]}
         load_w3(0)
         tab_w.append(held("root0", [P, T], I32))
@@ -126,17 +129,19 @@ def tile_list_moisture_downscaling_kernel(
         w1_w = held("defect", [P, 2, 2 * H], U8)
         nc.sync.dma_start(w1_w[:].bitcast(I32), w1_words.rearrange("a p c -> p a c").bitcast(I32))
 
-        def half_list(lst, h):
-            return lst[:, h * (HALF // 16) : (h + 1) * (HALF // 16)]
+        def half_list(offsets, h):
+            return offsets[:, h * (HALF // 16) : (h + 1) * (HALF // 16)]
 
         for h in range(HALVES):
             nc.vector.tensor_copy(v2_w[h][:], tab2_w[:].indirect(half_list(list2, h)))
         for h in range(HALVES):
             nc.vector.tensor_copy(v2_s[h][:], tab2_s[:].indirect(half_list(list2, h)))
-        nc.vector.tensor_copy(v_rows[:], tab_s[:].indirect(list1[:]))
-        nc.gpsimd.dma_start(v_s[1][0:100, :].bitcast(I32), v_rows[16:116, :].bitcast(I32))
+        nc.vector.tensor_copy(v_s0[:], tab_s[:].indirect(list1[:]))
+        nc.gpsimd.dma_start(v_s[1][0:LIVE_ROWS, :].bitcast(I32),
+                            v_s0[PASS1_ROW : PASS1_ROW + LIVE_ROWS, :].bitcast(I32))
 
         units = [(2 * pair + i, h) for pair in range(R_TILES // 2) for h in range(HALVES) for i in range(2)]
+        count = len(units)
 
         def by_slot(bank):
             return bank[:].rearrange("p (q t) -> p t q", t=PACK)
@@ -153,9 +158,8 @@ def tile_list_moisture_downscaling_kernel(
             half_b[u] = held("half_b%d" % u, [P, PACK, P], F32)
             nc.scalar.activation(half_b[u][:], by_slot(bank), ACT.Copy, scale=0.5)
 
-
         def round_cols(raw, cols, name):
-            grouped = held(name, [P, cols.stop - cols.start, PACK], BF16)
+            grouped = held(name, [P, PIECE, PACK], BF16)
             dst, src = weave(grouped[:], raw[:, :, cols])
             nc.scalar.copy(dst, src)
             return grouped[:]
@@ -163,20 +167,20 @@ def tile_list_moisture_downscaling_kernel(
         def quantize(codes, scales, grouped):
             nc.vector.quantize_mx(out=codes.bitcast(FP8X4), scales=scales, in_=grouped.rearrange("p c t -> p (c t)"))
 
-        for u in range(4):
+        third = count // 3
+        for u in range(third):
             make_b(u)
         v0_w = held("tab_s", [P, S], U32)
         nc.vector.tensor_copy(v0_w[:], tab_w[0][:].bitcast(U32).indirect(list1[:]))
-        w3_rest = held("tab_w0", [P, 2 * PACK * W3_COLS], F32)
+        w3_rest = held("tab_w0", [P, 2 * PACK * PIECE], F32)
         for c in (1, 2):
-            w3_raw[c] = w3_rest[:, (c - 1) * PACK * W3_COLS : c * PACK * W3_COLS].rearrange("p (j r) -> p j r", j=PACK)
+            w3_raw[c] = w3_rest[:, (c - 1) * PACK * PIECE : c * PACK * PIECE].rearrange("p (j r) -> p j r", j=PACK)
             load_w3(c)
-        for u in range(4, 8):
+        for u in range(third, 2 * third):
             make_b(u)
-        grouped = round_cols(w3_raw[0], slice(0, W3_COLS), "grouped")
-        quantize(w3_w[0][:], w3_s[0][:], grouped)
-        v1_w = held("grouped", [P, S], U32)
-        for u in range(8, 12):
+        quantize(w3_w[0][:], w3_s[0][:], round_cols(w3_raw[0], slice(0, PIECE), "w3_rounded"))
+        v1_w = held("w3_rounded", [P, S], U32)
+        for u in range(2 * third, count):
             make_b(u)
         const_t = psum_mm.tile([P, HALF], F32, name="mm")
         nc.tensor.transpose(const_t[:, 0:P], const_rows[:], ident[:])
@@ -189,12 +193,12 @@ def tile_list_moisture_downscaling_kernel(
             nc.sync.dma_start(grid_raw[h], grid[h * HALF : (h + 1) * HALF, :].rearrange("(p j) n -> p j n", j=PACK))
 
         v_w = [[words[:, h * HALF : (h + 1) * HALF] for h in range(HALVES)] for words in (v0_w, v1_w)]
-        a_bank, num, den, rsq, num_t, rsq_t, factor, z_bf, z_w, z_s = ({} for i in range(10))
+        a_bank, num, den, rsq, num_t, factor, z_bf, z_w, z_s = ({} for i in range(9))
 
         def make_a(u):
             rt, h = units[u]
             bank = psum_mm.tile([P, HALF], F32, name="mm")
-            c, off = divmod(rt * P, W3_COLS)
+            c, off = divmod(rt * P, PIECE)
             nc.tensor.matmul_mx(bank[:], lhsT=w3_w[c][:, off : off + P].bitcast(FP8X4), lhsT_scale=w3_s[c][:, off : off + P],
                                 rhs=v2_w[h][:].bitcast(FP4X4), rhs_scale=v2_s[h][:],
                                 start=True, stop=False)
@@ -209,28 +213,32 @@ def tile_list_moisture_downscaling_kernel(
             num[u] = ring.tile([P, PACK, P], F32, name="num")
             nc.vector.scalar_tensor_tensor(num[u][:], by_slot(a_bank[u]), 0.5, half_b[u][:], ALU.mult, ALU.subtract)
 
-        def make_den(u):
-            den[u] = ring.tile([P, PACK, P], F32, name="den")
-            nc.vector.scalar_tensor_tensor(den[u][:], by_slot(a_bank[u]), 0.0, num[u][:], ALU.max, ALU.subtract)
+        def slot_groups(u):
+            return [slice(0, PACK // 2), slice(PACK // 2, PACK)] if u == count - 1 else [slice(0, PACK)]
 
-        def make_rsq(u):
+        def make_root(u):
             rt, h = units[u]
+            den[u] = ring.tile([P, PACK, P], F32, name="den")
             rsq[u] = ring.tile([P, PACK, P], F32, name="rsq")
-            nc.scalar.activation(rsq[u][:], den[u][:], ACT.Abs_reciprocal_sqrt, bias=half_c[:, rt : rt + 1])
+            for slots in slot_groups(u):
+                nc.vector.scalar_tensor_tensor(den[u][:, slots, :], by_slot(a_bank[u])[:, slots, :], 0.0,
+                                               num[u][:, slots, :], ALU.max, ALU.subtract)
+                nc.scalar.activation(rsq[u][:, slots, :], den[u][:, slots, :], ACT.Abs_reciprocal_sqrt,
+                                     bias=half_c[:, rt : rt + 1])
 
         def turn(u):
-            num_t[u] = psum_t.tile([P, PACK, P], F32, name="num_t")
-            rsq_t[u] = psum_t.tile([P, PACK, P], F32, name="rsq_t")
-            for src, dst in ((num[u], num_t[u]), (rsq[u], rsq_t[u])):
-                for t in range(PACK):
-                    nc.tensor.transpose(dst[:, t, :], src[:, t, :], ident[:])
-
-        def make_factor(u):
             rt, h = units[u]
-            factor[u] = ring.tile([P, PACK, P], F32, name="factor")
+            num_t[u] = psum_t.tile([P, PACK, P], F32, name="num_t")
             for t in range(PACK):
-                nc.scalar.activation(factor[u][:, t, :], rsq_t[u][:, t, :], ACT.Square,
-                                     scale=root[:, h * PACK + t : h * PACK + t + 1])
+                nc.tensor.transpose(num_t[u][:, t, :], num[u][:, t, :], ident[:])
+            factor[u] = ring.tile([P, PACK, P], F32, name="factor")
+            for slots in slot_groups(u):
+                rsq_t = psum_t.tile([P, PACK, P], F32, name="rsq_t")
+                for t in range(slots.start, slots.stop):
+                    nc.tensor.transpose(rsq_t[:, t, :], rsq[u][:, t, :], ident[:])
+                for t in range(slots.start, slots.stop):
+                    nc.scalar.activation(factor[u][:, t, :], rsq_t[:, t, :], ACT.Square,
+                                         scale=root[:, h * PACK + t : h * PACK + t + 1])
 
         def make_z(u):
             if u % 2 == 0:
@@ -239,12 +247,12 @@ def tile_list_moisture_downscaling_kernel(
             dst, src = weave(mine, num_t[u][:])
             nc.vector.tensor_tensor(dst, src, weave(mine, factor[u][:])[1], ALU.mult)
 
-        def quantize_z(first, count):
-            codes = held("z_w%d" % first, [P, count * P], U32)
-            scales = held("z_s%d" % first, [P, count * P], U8)
-            start = (first % 2) * P
-            quantize(codes[:], scales[:], z_bf[first // 2][:, start : start + count * P, :])
-            for i in range(count):
+        def quantize_z(first, together):
+            codes = held("z_w%d" % first, [P, together * P], U32)
+            scales = held("z_s%d" % first, [P, together * P], U8)
+            col = (first % 2) * P
+            quantize(codes[:], scales[:], z_bf[first // 2][:, col : col + together * P, :])
+            for i in range(together):
                 z_w[first + i] = codes[:, i * P : (i + 1) * P]
                 z_s[first + i] = scales[:, i * P : (i + 1) * P]
 
@@ -263,52 +271,49 @@ def tile_list_moisture_downscaling_kernel(
 
         def last_pass(h):
             u = units.index((R_TILES - 1, h))
-            for half in range(2):
+            for side in range(2):
                 if h == 0:
                     last_banks.append(psum_mm.tile([P, HALF], F32, name="mm"))
-                cols = slice(half * F // 2, (half + 1) * F // 2)
-                nc.tensor.matmul_mx(last_banks[half][:, 0 : F // 2], lhsT=z_w[u].bitcast(FP8X4), lhsT_scale=z_s[u],
+                cols = slice(side * F // 2, (side + 1) * F // 2)
+                nc.tensor.matmul_mx(last_banks[side][:, 0 : F // 2], lhsT=z_w[u].bitcast(FP8X4), lhsT_scale=z_s[u],
                                     rhs=grid_w[h][:, cols].bitcast(FP8X4), rhs_scale=grid_s[h][:, cols],
                                     start=(h == 0), stop=(h == HALVES - 1))
 
-        side = [(w3_raw[c], slice(0, W3_COLS), w3_w[c][:], w3_s[c][:]) for c in (1, 2)]
+        pieces = [(w3_raw[c], slice(0, PIECE), w3_w[c][:], w3_s[c][:]) for c in (1, 2)]
         for h in range(HALVES):
-            for n0 in range(0, F, GRID_COLS):
-                cols = slice(n0, n0 + GRID_COLS)
-                side.append((grid_raw[h], cols, grid_w[h][:, cols], grid_s[h][:, cols]))
-        side = dict(zip(range(1, 7), side))
+            for n0 in range(0, F, PIECE):
+                cols = slice(n0, n0 + PIECE)
+                pieces.append((grid_raw[h], cols, grid_w[h][:, cols], grid_s[h][:, cols]))
+        piece_at = dict(zip((0, 1, 3, 4, 5, 6), pieces))
+        first_out = max(piece_at) + 2
         rounded = {}
-        outs = {8: 0, 9: 1, 10: 2, 11: 3, 12: 4}
 
-        n = len(units)
         make_a(0)
-        for i in range(n + 2):
-            if i + 1 < n:
+        for i in range(count + 2):
+            if i + 1 < count:
                 make_a(i + 1)
-            if 1 <= i <= n:
+            if 1 <= i <= count:
                 turn(i - 1)
-                make_factor(i - 1)
-            if i < n:
+            if i < count:
                 make_num(i)
-            if 2 <= i < n + 2:
+            if i >= 2:
                 make_z(i - 2)
-            if i < n:
-                make_den(i)
-                make_rsq(i)
-            if i - 2 >= n - 2:
+            if i < count:
+                make_root(i)
+            if i >= count:
                 quantize_z(i - 2, 1)
             elif i >= 3 and i % 2 == 1:
                 quantize_z(i - 3, 2)
-            if i == n:
+            if i == count:
                 last_pass(0)
-            if i in side:
-                rounded[i] = round_cols(side[i][0], side[i][1], "half_b%d" % i)
-            if i - 1 in side:
-                quantize(side[i - 1][2], side[i - 1][3], rounded[i - 1])
-            if i in outs:
-                make_out(outs[i])
+            if i in piece_at:
+                rounded[i] = round_cols(piece_at[i][0], piece_at[i][1], "half_b%d" % i)
+            if i - 1 in piece_at:
+                quantize(piece_at[i - 1][2], piece_at[i - 1][3], rounded[i - 1])
+            if first_out <= i < first_out + R_TILES - 1:
+                make_out(i - first_out)
         last_pass(1)
-        for half, copy in enumerate((nc.scalar.copy, nc.vector.tensor_copy)):
+        for side, empty in enumerate((nc.scalar.copy, nc.vector.tensor_copy)):
             part = ring.tile([P, F // 2], F32, name="part")
-            copy(part[:], last_banks[half][:, 0 : F // 2])
-            nc.sync.dma_start(out[H - P : H, half * F // 2 : (half + 1) * F // 2], part[:])
+            empty(part[:], last_banks[side][:, 0 : F // 2])
+            nc.sync.dma_start(out[H - P : H, side * F // 2 : (side + 1) * F // 2], part[:])

@@ -1,3 +1,4 @@
+import math
 from contextlib import ExitStack
 
 import concourse.mybir as mybir
@@ -24,7 +25,7 @@ HALVES = S // HALF
 R_TILES = H // P
 SCALE_ROWS = 16
 PIECE = 256
-PASS1_ROW = 16
+PASS_ROWS = (8, 24)
 LIVE_ROWS = 100
 
 
@@ -42,24 +43,38 @@ def tile_list_moisture_downscaling_kernel(
     nc = tc.nc
     with ExitStack() as ctx:
         keep = ctx.enter_context(tc.tile_pool(name="keep", bufs=1))
+        loads = ctx.enter_context(tc.tile_pool(name="loads", bufs=1))
         ring = ctx.enter_context(tc.tile_pool(name="ring", bufs=3))
-        psum_mm = ctx.enter_context(tc.psum_pool(name="psum_mm", bufs=3))
-        psum_t = ctx.enter_context(tc.psum_pool(name="psum_t", bufs=2))
-        psum_o = ctx.enter_context(tc.psum_pool(name="psum_o", bufs=1))
+        psum = ctx.enter_context(tc.psum_pool(name="psum", bufs=1))
 
         def held(name, shape, dtype):
             return keep.tile(shape, dtype, name=name, align_bytes=64)
 
+        def placed(name, shape, dtype, offset):
+            return loads.tile(shape, dtype, name=name, align_bytes=64, offset=offset)
+
+        def bank(name, shape):
+            return psum.tile(shape, F32, name=name)
+
+        A_BANKS = ("a0", "a1", "a2")
+        NUM_BANKS = ("num0", "num1")
+        ROOT_BANKS = ("root0", "root1")
+        OUT_BANK = "o"
+
         list1 = held("list1", [P, S // 16], U16)
         list2 = held("list2", [P, S // 16], U16)
-        tab_w = [held("tab_w0", [P, T], I32)]
-        tab2_w = held("tab2_w", [P, T], U16)
+        tab2_w = placed("tab2_w", [P, T], U16, 0)
+        tab_w = [placed("tab_w%d" % a, [P, T], I32, 2 * T + a * 4 * T) for a in range(2)]
+        w1_w = placed("w1_w", [P, 2, 2 * H], U8, 0)
+        w3_raw = [held("w3_raw0", [P, PACK, PIECE], F32), placed("w3_raw1", [P, PACK, PIECE], F32, T),
+                  placed("w3_raw2", [P, PACK, PIECE], F32, 6 * T)]
+        grid_raw = [placed("grid_raw%d" % h, [P, PACK, F], F32, 2 * T + h * 2 * T) for h in range(HALVES)]
         tab_s = held("tab_s", [P, T], U8)
         tab2_s = held("tab2_s", [P, T], U8)
         v2_w = [held("v2_w%d" % h, [P, HALF], U16) for h in range(HALVES)]
-        v_s0 = held("v_s0", [P, S], U8)
-        v_s = [v_s0, held("v_s1", [P, S], U8)]
         v2_s = [held("v2_s%d" % h, [P, HALF], U8) for h in range(HALVES)]
+        picked_s = held("picked_s", [P, S], U8)
+        v_s = held("v_s", [P, 2, S], U8)
         w1_s = held("w1_s", [P, 2, H], U8)
         w2_w = held("w2_w", [P, H], I32)
         w2_s = held("w2_s", [P, H], U8)
@@ -67,147 +82,126 @@ def tile_list_moisture_downscaling_kernel(
         w3_s = [held("w3_s%d" % c, [P, PIECE], U8) for c in range(H // PIECE)]
         grid_w = [held("grid_w%d" % h, [P, F], U32) for h in range(HALVES)]
         grid_s = [held("grid_s%d" % h, [P, F], U8) for h in range(HALVES)]
-        const_rows = held("const_rows", [P, P], F32)
-        half_c = held("half_c", [P, R_TILES], F32)
+        const_t = held("const_t", [P, R_TILES], F32)
         trust_t = held("trust_t", [P, HALVES * PACK], F32)
         ident = held("ident", [P, P], F32)
 
-        for scale_tile in (tab2_s[:], w2_s[:], tab_s[:], w1_s[:].rearrange("p a c -> p (a c)"), v_s[1][:]):
-            nc.vector.memset(scale_tile.bitcast(I32), 0)
-
-        def load_w2_scales(queue, r):
-            queue.dma_start(w2_s[r:P:32, :].bitcast(I32), w2_scales[0, r:SCALE_ROWS:4, :].bitcast(I32))
-
-        for r in range(2, 4):
-            load_w2_scales(nc.gpsimd, r)
-        nc.gpsimd.memset(const_rows[0 : P - R_TILES, :], 0.0)
-        make_identity(nc, ident[:])
-        for r in range(4):
-            nc.gpsimd.dma_start(w1_s[r:P:32, :, :].bitcast(I32),
-                                w1_scales[:, r:SCALE_ROWS:4, :].rearrange("a q c -> q a c").bitcast(I32))
-
-        def load_tab(a, part):
-            cols = slice(part * T // 2, (part + 1) * T // 2)
-            nc.sync.dma_start(tab_w[a][:, cols], tab_words[a].rearrange("p t i -> p (t i)").bitcast(I32)[:, cols])
-
         def load_w3(c):
-            nc.sync.dma_start(w3_raw[c], w3[:, c * PIECE : (c + 1) * PIECE].rearrange("(p j) r -> p j r", j=PACK))
+            nc.sync.dma_start(w3_raw[c][:], w3[:, c * PIECE : (c + 1) * PIECE].rearrange("(p j) r -> p j r", j=PACK))
+
+        def load_tab(a):
+            nc.sync.dma_start(tab_w[a][:], tab_words[a].rearrange("p t i -> p (t i)").bitcast(I32))
 
         nc.sync.dma_start(list2[:], offs2)
         nc.sync.dma_start(list1[:], offs)
-        nc.sync.dma_start(trust_t[:].rearrange("p (h t) -> p h t", t=PACK),
-                          trust.rearrange("(h p t) -> p h t", h=HALVES, t=PACK))
-        for c0 in range(0, T // 2, T // 8):
-            nc.sync.dma_start(tab2_w[:].bitcast(I32)[:, c0 : c0 + T // 8], tab2_words[0].bitcast(I32)[:, c0 : c0 + T // 8])
+        nc.sync.dma_start(tab2_w[:].bitcast(I32), tab2_words[0].bitcast(I32))
         nc.sync.dma_start(w2_w[:], w2_words[0].rearrange("p c i -> p (c i)").bitcast(I32))
-        load_tab(0, 0)
-        for r in range(4):
-            nc.sync.dma_start(tab2_s[r:P:32, :].bitcast(I32), tab2_scales[0, r:SCALE_ROWS:4, :].bitcast(I32))
-        for r in range(2):
-            load_w2_scales(nc.sync, r)
-        load_tab(0, 1)
-        nc.sync.dma_start(const_rows[P - R_TILES : P, :], const.rearrange("(t p) -> t p", p=P))
-        for r in range(4):
-            nc.sync.dma_start(tab_s[r:P:PASS1_ROW, :].bitcast(I32),
-                              tab_scales.rearrange("a (q r) t -> r q a t", r=4)[r].bitcast(I32))
-
-        rough = held("rough", [P, HALVES * PACK], F32)
-        root0 = held("root0", [P, HALVES * PACK], F32)
-        defect = held("defect", [P, HALVES * PACK], F32)
-        root = held("root", [P, HALVES * PACK], F32)
-        nc.scalar.activation(rough[:], trust_t[:], ACT.Abs_reciprocal_sqrt)
-        nc.vector.tensor_tensor(root0[:], rough[:], trust_t[:], ALU.mult)
-        nc.vector.scalar_tensor_tensor(defect[:], root0[:], -0.5, rough[:], ALU.mult, ALU.mult)
-        nc.vector.scalar_tensor_tensor(root[:], defect[:], 1.5, root0[:], ALU.add, ALU.mult)
-
-        w3_first = held("rough", [P, PACK, PIECE], F32)
-        w3_raw = {0: w3_first[:]}
         load_w3(0)
-        tab_w.append(held("root0", [P, T], I32))
-        load_tab(1, 0)
-        load_tab(1, 1)
-        w1_w = held("defect", [P, 2, 2 * H], U8)
-        nc.sync.dma_start(w1_w[:].bitcast(I32), w1_words.rearrange("a p c -> p a c").bitcast(I32))
+        load_tab(0)
+        load_tab(1)
+        nc.scalar.dma_start(trust_t[:].rearrange("p (h t) -> p h t", t=PACK),
+                            trust.rearrange("(h p t) -> p h t", h=HALVES, t=PACK))
+        with nc.allow_non_contiguous_dma(reason="one value of const a partition and row tile"):
+            nc.scalar.dma_start(const_t[:], const.rearrange("(t p) -> p t", p=P))
+
+        nc.vector.memset(tab2_s[:].bitcast(I32), 0)
+        nc.vector.memset(tab_s[:].bitcast(I32), 0)
+        nc.vector.memset(v_s[:].rearrange("p a c -> p (a c)").bitcast(I32), 0)
+        nc.gpsimd.memset(w2_s[:].bitcast(I32), 0)
+        for r in range(4):
+            nc.scalar.dma_start(tab2_s[r:P:32, :].bitcast(I32), tab2_scales[0, r:SCALE_ROWS:4, :].bitcast(I32))
+        for r in range(4):
+            nc.gpsimd.dma_start(w2_s[r:P:32, :].bitcast(I32), w2_scales[0, r:SCALE_ROWS:4, :].bitcast(I32))
+        for r in range(4):
+            nc.gpsimd.dma_start(tab_s[PASS_ROWS[0] + r : P : 16, :].bitcast(I32),
+                                tab_scales.rearrange("a (q r) t -> r q a t", r=4)[r].bitcast(I32))
+        nc.gpsimd.memset(w1_s[:].rearrange("p a c -> p (a c)").bitcast(I32), 0)
+        for r in range(4):
+            nc.gpsimd.dma_start(w1_s[r:P:32, :, :].bitcast(I32),
+                                w1_scales[:, r:SCALE_ROWS:4, :].rearrange("a q c -> q a c").bitcast(I32))
+        make_identity(nc, ident[:])
 
         def half_list(offsets, h):
             return offsets[:, h * (HALF // 16) : (h + 1) * (HALF // 16)]
 
         for h in range(HALVES):
             nc.vector.tensor_copy(v2_w[h][:], tab2_w[:].indirect(half_list(list2, h)))
-        for h in range(HALVES):
             nc.vector.tensor_copy(v2_s[h][:], tab2_s[:].indirect(half_list(list2, h)))
-        nc.vector.tensor_copy(v_s0[:], tab_s[:].indirect(list1[:]))
-        nc.gpsimd.dma_start(v_s[1][0:LIVE_ROWS, :].bitcast(I32),
-                            v_s0[PASS1_ROW : PASS1_ROW + LIVE_ROWS, :].bitcast(I32))
+        nc.sync.dma_start(w1_w[:].bitcast(I32), w1_words.rearrange("a p c -> p a c").bitcast(I32))
+        load_w3(1)
 
-        units = [(2 * pair + i, h) for pair in range(R_TILES // 2) for h in range(HALVES) for i in range(2)]
+        rough = held("rough", [P, HALVES * PACK], F32)
+        root0 = held("tab2_s", [P, HALVES * PACK], F32)
+        defect = held("defect", [P, HALVES * PACK], F32)
+        root = held("root", [P, HALVES * PACK], F32)
+        nc.scalar.activation(rough[:], trust_t[:], ACT.Abs_reciprocal_sqrt)
+        nc.vector.tensor_tensor(root0[:], rough[:], trust_t[:], ALU.mult)
+        nc.vector.scalar_tensor_tensor(defect[:], root0[:], -0.5 * math.sqrt(2.0), rough[:], ALU.mult, ALU.mult)
+        nc.vector.scalar_tensor_tensor(root[:], defect[:], 1.5 * math.sqrt(2.0), root0[:], ALU.add, ALU.mult)
+
+        units = [(rt, h) for rt in range(R_TILES) for h in range(HALVES)]
         count = len(units)
 
-        def by_slot(bank):
-            return bank[:].rearrange("p (q t) -> p t q", t=PACK)
+        def by_slot(tile):
+            return tile[:].rearrange("p (q t) -> p t q", t=PACK)
 
         half_b = {}
 
-        def make_b(u):
+        def make_b(u, name):
             rt, h = units[u]
-            bank = psum_mm.tile([P, HALF], F32, name="mm")
-            nc.tensor.matmul_mx(bank[:], lhsT=w2_w[:, rt * P : (rt + 1) * P].bitcast(FP8X4),
+            acc = bank(name, [P, HALF])
+            nc.tensor.matmul_mx(acc[:], lhsT=w2_w[:, rt * P : (rt + 1) * P].bitcast(FP8X4),
                                 lhsT_scale=w2_s[:, rt * P : (rt + 1) * P],
                                 rhs=v2_w[h][:].bitcast(FP4X4), rhs_scale=v2_s[h][:],
                                 start=True, stop=True)
             half_b[u] = held("half_b%d" % u, [P, PACK, P], F32)
-            nc.scalar.activation(half_b[u][:], by_slot(bank), ACT.Copy, scale=0.5)
+            nc.scalar.activation(half_b[u][:], by_slot(acc), ACT.Copy, scale=0.5)
 
-        def round_cols(raw, cols, name):
+        def round_cols(copy, raw, cols, name):
             grouped = held(name, [P, PIECE, PACK], BF16)
             dst, src = weave(grouped[:], raw[:, :, cols])
-            nc.scalar.copy(dst, src)
+            copy(dst, src)
             return grouped[:]
 
         def quantize(codes, scales, grouped):
             nc.vector.quantize_mx(out=codes.bitcast(FP8X4), scales=scales, in_=grouped.rearrange("p c t -> p (c t)"))
 
-        third = count // 3
-        for u in range(third):
-            make_b(u)
+        all_banks = A_BANKS + (OUT_BANK,) + NUM_BANKS + ROOT_BANKS
+        b_order = [u for h in range(HALVES) for u in range(h, count, HALVES)]
+        for i, u in enumerate(b_order):
+            make_b(u, all_banks[i % len(all_banks)])
+
+        w3_first = round_cols(nc.vector.tensor_copy, w3_raw[0][:], slice(0, PIECE), "w3_rounded")
+        nc.vector.tensor_copy(picked_s[:], tab_s[:].indirect(list1[:]))
+        for a in range(2):
+            nc.gpsimd.dma_start(v_s[0:LIVE_ROWS, a, :].bitcast(I32),
+                                picked_s[PASS_ROWS[a] : PASS_ROWS[a] + LIVE_ROWS, :].bitcast(I32))
+        quantize(w3_w[0][:], w3_s[0][:], w3_first)
         v0_w = held("tab_s", [P, S], U32)
         nc.vector.tensor_copy(v0_w[:], tab_w[0][:].bitcast(U32).indirect(list1[:]))
-        w3_rest = held("tab_w0", [P, 2 * PACK * PIECE], F32)
-        for c in (1, 2):
-            w3_raw[c] = w3_rest[:, (c - 1) * PACK * PIECE : c * PACK * PIECE].rearrange("p (j r) -> p j r", j=PACK)
-            load_w3(c)
-        for u in range(third, 2 * third):
-            make_b(u)
-        quantize(w3_w[0][:], w3_s[0][:], round_cols(w3_raw[0], slice(0, PIECE), "w3_rounded"))
+        for h in range(HALVES):
+            nc.sync.dma_start(grid_raw[h][:], grid[h * HALF : (h + 1) * HALF, :].rearrange("(p j) n -> p j n", j=PACK))
         v1_w = held("w3_rounded", [P, S], U32)
-        for u in range(2 * third, count):
-            make_b(u)
-        const_t = psum_mm.tile([P, HALF], F32, name="mm")
-        nc.tensor.transpose(const_t[:, 0:P], const_rows[:], ident[:])
-        nc.scalar.activation(half_c[:], const_t[:, P - R_TILES : P], ACT.Copy, scale=0.5)
         for h in range(HALVES):
             nc.vector.tensor_copy(v1_w[:, h * HALF : (h + 1) * HALF], tab_w[1][:].bitcast(U32).indirect(half_list(list1, h)))
-        grid_rows = held("root0", [P, HALVES * PACK * F], F32)
-        grid_raw = [grid_rows[:, h * PACK * F : (h + 1) * PACK * F].rearrange("p (j n) -> p j n", j=PACK) for h in range(HALVES)]
-        for h in range(HALVES):
-            nc.sync.dma_start(grid_raw[h], grid[h * HALF : (h + 1) * HALF, :].rearrange("(p j) n -> p j n", j=PACK))
+        load_w3(2)
 
         v_w = [[words[:, h * HALF : (h + 1) * HALF] for h in range(HALVES)] for words in (v0_w, v1_w)]
         a_bank, num, den, rsq, num_t, factor, z_bf, z_w, z_s = ({} for i in range(9))
 
         def make_a(u):
             rt, h = units[u]
-            bank = psum_mm.tile([P, HALF], F32, name="mm")
+            acc = bank(A_BANKS[u % len(A_BANKS)], [P, HALF])
             c, off = divmod(rt * P, PIECE)
-            nc.tensor.matmul_mx(bank[:], lhsT=w3_w[c][:, off : off + P].bitcast(FP8X4), lhsT_scale=w3_s[c][:, off : off + P],
+            nc.tensor.matmul_mx(acc[:], lhsT=w3_w[c][:, off : off + P].bitcast(FP8X4), lhsT_scale=w3_s[c][:, off : off + P],
                                 rhs=v2_w[h][:].bitcast(FP4X4), rhs_scale=v2_s[h][:],
                                 start=True, stop=False)
             for a in range(2):
-                nc.tensor.matmul_mx(bank[:], lhsT=w1_w[:, a, 2 * rt * P : 2 * (rt + 1) * P].bitcast(FP4X4),
+                nc.tensor.matmul_mx(acc[:], lhsT=w1_w[:, a, 2 * rt * P : 2 * (rt + 1) * P].bitcast(FP4X4),
                                     lhsT_scale=w1_s[:, a, rt * P : (rt + 1) * P],
-                                    rhs=v_w[a][h].bitcast(FP8X4), rhs_scale=v_s[a][:, h * HALF : (h + 1) * HALF],
+                                    rhs=v_w[a][h].bitcast(FP8X4), rhs_scale=v_s[:, a, h * HALF : (h + 1) * HALF],
                                     start=False, stop=(a == 1))
-            a_bank[u] = bank
+            a_bank[u] = acc
 
         def make_num(u):
             num[u] = ring.tile([P, PACK, P], F32, name="num")
@@ -224,16 +218,16 @@ def tile_list_moisture_downscaling_kernel(
                 nc.vector.scalar_tensor_tensor(den[u][:, slots, :], by_slot(a_bank[u])[:, slots, :], 0.0,
                                                num[u][:, slots, :], ALU.max, ALU.subtract)
                 nc.scalar.activation(rsq[u][:, slots, :], den[u][:, slots, :], ACT.Abs_reciprocal_sqrt,
-                                     bias=half_c[:, rt : rt + 1])
+                                     bias=const_t[:, rt : rt + 1], scale=2.0)
 
         def turn(u):
             rt, h = units[u]
-            num_t[u] = psum_t.tile([P, PACK, P], F32, name="num_t")
+            num_t[u] = bank(NUM_BANKS[u % 2], [P, PACK, P])
             for t in range(PACK):
                 nc.tensor.transpose(num_t[u][:, t, :], num[u][:, t, :], ident[:])
             factor[u] = ring.tile([P, PACK, P], F32, name="factor")
-            for slots in slot_groups(u):
-                rsq_t = psum_t.tile([P, PACK, P], F32, name="rsq_t")
+            for g, slots in enumerate(slot_groups(u)):
+                rsq_t = bank(ROOT_BANKS[(u + g) % 2], [P, PACK, P])
                 for t in range(slots.start, slots.stop):
                     nc.tensor.transpose(rsq_t[:, t, :], rsq[u][:, t, :], ident[:])
                 for t in range(slots.start, slots.stop):
@@ -241,79 +235,73 @@ def tile_list_moisture_downscaling_kernel(
                                          scale=root[:, h * PACK + t : h * PACK + t + 1])
 
         def make_z(u):
-            if u % 2 == 0:
-                z_bf[u // 2] = ring.tile([P, 2 * P, PACK], BF16, name="z_bf", align_bytes=64)
-            mine = z_bf[u // 2][:, (u % 2) * P : (u % 2 + 1) * P, :]
-            dst, src = weave(mine, num_t[u][:])
-            nc.vector.tensor_tensor(dst, src, weave(mine, factor[u][:])[1], ALU.mult)
+            z_bf[u] = ring.tile([P, P, PACK], BF16, name="z_bf", align_bytes=64)
+            dst, src = weave(z_bf[u][:], num_t[u][:])
+            nc.vector.tensor_tensor(dst, src, weave(z_bf[u][:], factor[u][:])[1], ALU.mult)
 
-        def quantize_z(first, together):
-            codes = held("z_w%d" % first, [P, together * P], U32)
-            scales = held("z_s%d" % first, [P, together * P], U8)
-            col = (first % 2) * P
-            quantize(codes[:], scales[:], z_bf[first // 2][:, col : col + together * P, :])
-            for i in range(together):
-                z_w[first + i] = codes[:, i * P : (i + 1) * P]
-                z_s[first + i] = scales[:, i * P : (i + 1) * P]
+        def quantize_z(u):
+            z_w[u] = held("z_w%d" % u, [P, P], U32)
+            z_s[u] = held("z_s%d" % u, [P, P], U8)
+            quantize(z_w[u][:], z_s[u][:], z_bf[u][:])
+
+        def out_pass(acc, rt, h, cols):
+            u = units.index((rt, h))
+            nc.tensor.matmul_mx(acc, lhsT=z_w[u][:].bitcast(FP8X4), lhsT_scale=z_s[u][:],
+                                rhs=grid_w[h][:, cols].bitcast(FP8X4), rhs_scale=grid_s[h][:, cols],
+                                start=(h == 0), stop=(h == HALVES - 1))
 
         def make_out(rt):
-            bank = psum_o.tile([P, F], F32, name="o")
+            acc = bank(OUT_BANK, [P, F])
             for h in range(HALVES):
-                u = units.index((rt, h))
-                nc.tensor.matmul_mx(bank[:], lhsT=z_w[u].bitcast(FP8X4), lhsT_scale=z_s[u],
-                                    rhs=grid_w[h][:].bitcast(FP8X4), rhs_scale=grid_s[h][:],
-                                    start=(h == 0), stop=(h == HALVES - 1))
+                out_pass(acc[:], rt, h, slice(0, F))
             result = ring.tile([P, F], F32, name="result")
-            nc.scalar.copy(result[:], bank[:])
+            nc.scalar.copy(result[:], acc[:])
             nc.sync.dma_start(out[rt * P : (rt + 1) * P, :], result[:])
 
+        sides = [slice(0, F // 2), slice(F // 2, F)]
         last_banks = []
 
         def last_pass(h):
-            u = units.index((R_TILES - 1, h))
-            for side in range(2):
+            for side, cols in enumerate(sides):
                 if h == 0:
-                    last_banks.append(psum_mm.tile([P, HALF], F32, name="mm"))
-                cols = slice(side * F // 2, (side + 1) * F // 2)
-                nc.tensor.matmul_mx(last_banks[side][:, 0 : F // 2], lhsT=z_w[u].bitcast(FP8X4), lhsT_scale=z_s[u],
-                                    rhs=grid_w[h][:, cols].bitcast(FP8X4), rhs_scale=grid_s[h][:, cols],
-                                    start=(h == 0), stop=(h == HALVES - 1))
+                    last_banks.append(bank(A_BANKS[side], [P, HALF]))
+                out_pass(last_banks[side][:, 0 : F // 2], R_TILES - 1, h, cols)
 
-        pieces = [(w3_raw[c], slice(0, PIECE), w3_w[c][:], w3_s[c][:]) for c in (1, 2)]
+        pieces = []
         for h in range(HALVES):
             for n0 in range(0, F, PIECE):
                 cols = slice(n0, n0 + PIECE)
-                pieces.append((grid_raw[h], cols, grid_w[h][:, cols], grid_s[h][:, cols]))
-        piece_at = dict(zip((0, 1, 3, 4, 5, 6), pieces))
-        first_out = max(piece_at) + 2
-        rounded = {}
+                pieces.append((grid_raw[h][:], cols, grid_w[h][:, cols], grid_s[h][:, cols]))
+        pieces.append((w3_raw[2][:], slice(0, PIECE), w3_w[2][:], w3_s[2][:]))
+        piece_at = {i + 1: piece for i, piece in enumerate(pieces)}
+        rounded = {-1: round_cols(nc.scalar.copy, w3_raw[1][:], slice(0, PIECE), "w3_rounded1")}
+        piece_at[-1] = (None, None, w3_w[1][:], w3_s[1][:])
+        out_at = {6: 0, 7: 1, 8: 2, 10: 3, 12: 4}
 
         make_a(0)
-        for i in range(count + 2):
+        for i in range(count + 3):
             if i + 1 < count:
                 make_a(i + 1)
             if 1 <= i <= count:
                 turn(i - 1)
             if i < count:
                 make_num(i)
-            if i >= 2:
-                make_z(i - 2)
-            if i < count:
-                make_root(i)
-            if i >= count:
-                quantize_z(i - 2, 1)
-            elif i >= 3 and i % 2 == 1:
-                quantize_z(i - 3, 2)
-            if i == count:
-                last_pass(0)
-            if i in piece_at:
-                rounded[i] = round_cols(piece_at[i][0], piece_at[i][1], "half_b%d" % i)
+            if i >= 3:
+                quantize_z(i - 3)
             if i - 1 in piece_at:
                 quantize(piece_at[i - 1][2], piece_at[i - 1][3], rounded[i - 1])
-            if first_out <= i < first_out + R_TILES - 1:
-                make_out(i - first_out)
+            if i < count:
+                make_root(i)
+            if 2 <= i < count + 2:
+                make_z(i - 2)
+            if i in piece_at:
+                rounded[i] = round_cols(nc.scalar.copy, piece_at[i][0], piece_at[i][1], "half_b%d" % i)
+            if i in out_at:
+                make_out(out_at[i])
+            if i == count + 1:
+                last_pass(0)
         last_pass(1)
         for side, empty in enumerate((nc.scalar.copy, nc.vector.tensor_copy)):
             part = ring.tile([P, F // 2], F32, name="part")
             empty(part[:], last_banks[side][:, 0 : F // 2])
-            nc.sync.dma_start(out[H - P : H, side * F // 2 : (side + 1) * F // 2], part[:])
+            nc.sync.dma_start(out[H - P : H, sides[side]], part[:])

@@ -25,7 +25,7 @@ HALVES = S // HALF
 R_TILES = H // P
 SCALE_ROWS = 16
 PIECE = 256
-PASS_ROWS = (8, 24)
+PASS1_ROW = 16
 LIVE_ROWS = 100
 
 
@@ -65,16 +65,17 @@ def tile_list_moisture_downscaling_kernel(
         list2 = held("list2", [P, S // 16], U16)
         tab2_w = placed("tab2_w", [P, T], U16, 0)
         tab_w = [placed("tab_w%d" % a, [P, T], I32, 2 * T + a * 4 * T) for a in range(2)]
-        w1_w = placed("w1_w", [P, 2, 2 * H], U8, 0)
-        w3_raw = [held("w3_raw0", [P, PACK, PIECE], F32), placed("w3_raw1", [P, PACK, PIECE], F32, T),
+        w1_first = held("w1_first", [P, 2, 2 * PIECE], U8)
+        w1_rest = placed("w1_rest", [P, 2, 2 * (H - PIECE)], U8, 11 * T + 1536)
+        w3_raw = [held("w3_raw0", [P, PACK, PIECE], F32), placed("w3_raw1", [P, PACK, PIECE], F32, 11 * T + 3584),
                   placed("w3_raw2", [P, PACK, PIECE], F32, 6 * T)]
         grid_raw = [placed("grid_raw%d" % h, [P, PACK, F], F32, 2 * T + h * 2 * T) for h in range(HALVES)]
-        tab_s = held("tab_s", [P, T], U8)
+        tab_s = placed("tab_s", [P, T], U8, 11 * T)
         tab2_s = held("tab2_s", [P, T], U8)
         v2_w = [held("v2_w%d" % h, [P, HALF], U16) for h in range(HALVES)]
-        v2_s = [held("v2_s%d" % h, [P, HALF], U8) for h in range(HALVES)]
-        picked_s = held("picked_s", [P, S], U8)
-        v_s = held("v_s", [P, 2, S], U8)
+        v2_s = [held("v2_s0", [P, HALF], U8), held("v2_s1", [P, HALF], U8)]
+        w1_rows = w1_words.rearrange("a p c -> p a c").bitcast(I32)
+        lifted_s = held("lifted_s", [P, S], U8)
         w1_s = held("w1_s", [P, 2, H], U8)
         w2_w = held("w2_w", [P, H], I32)
         w2_s = held("w2_s", [P, H], U8)
@@ -92,34 +93,36 @@ def tile_list_moisture_downscaling_kernel(
         def load_tab(a):
             nc.sync.dma_start(tab_w[a][:], tab_words[a].rearrange("p t i -> p (t i)").bitcast(I32))
 
+        nc.vector.memset(tab2_s[:].bitcast(I32), 0)
+        nc.gpsimd.memset(tab_s[:].bitcast(I32), 0)
+        for scale_tile in (w2_s[:], w1_s[:].rearrange("p a c -> p (a c)"), lifted_s[:]):
+            nc.vector.memset(scale_tile.bitcast(I32), 0)
+        for r in range(4):
+            nc.gpsimd.dma_start(tab_s[r:P:PASS1_ROW, :].bitcast(I32),
+                                tab_scales.rearrange("a (q r) t -> r q a t", r=4)[r].bitcast(I32))
+        make_identity(nc, ident[:])
+
         nc.sync.dma_start(list2[:], offs2)
         nc.sync.dma_start(list1[:], offs)
-        nc.sync.dma_start(tab2_w[:].bitcast(I32), tab2_words[0].bitcast(I32))
-        nc.sync.dma_start(w2_w[:], w2_words[0].rearrange("p c i -> p (c i)").bitcast(I32))
-        load_w3(0)
-        load_tab(0)
-        load_tab(1)
-        nc.scalar.dma_start(trust_t[:].rearrange("p (h t) -> p h t", t=PACK),
-                            trust.rearrange("(h p t) -> p h t", h=HALVES, t=PACK))
+        nc.sync.dma_start(trust_t[:].rearrange("p (h t) -> p h t", t=PACK),
+                          trust.rearrange("(h p t) -> p h t", h=HALVES, t=PACK))
         with nc.allow_non_contiguous_dma(reason="one value of const a partition and row tile"):
-            nc.scalar.dma_start(const_t[:], const.rearrange("(t p) -> p t", p=P))
-
-        nc.vector.memset(tab2_s[:].bitcast(I32), 0)
-        nc.vector.memset(tab_s[:].bitcast(I32), 0)
-        nc.vector.memset(v_s[:].rearrange("p a c -> p (a c)").bitcast(I32), 0)
-        nc.gpsimd.memset(w2_s[:].bitcast(I32), 0)
+            nc.sync.dma_start(const_t[:], const.rearrange("(t p) -> p t", p=P))
+        for c0 in range(0, T // 2, T // 8):
+            nc.sync.dma_start(tab2_w[:].bitcast(I32)[:, c0 : c0 + T // 8], tab2_words[0].bitcast(I32)[:, c0 : c0 + T // 8])
+        for c0 in range(0, H, H // 2):
+            nc.sync.dma_start(w2_w[:, c0 : c0 + H // 2], w2_words[0].rearrange("p c i -> p (c i)").bitcast(I32)[:, c0 : c0 + H // 2])
         for r in range(4):
-            nc.scalar.dma_start(tab2_s[r:P:32, :].bitcast(I32), tab2_scales[0, r:SCALE_ROWS:4, :].bitcast(I32))
+            nc.sync.dma_start(tab2_s[r:P:32, :].bitcast(I32), tab2_scales[0, r:SCALE_ROWS:4, :].bitcast(I32))
+        load_w3(0)
         for r in range(4):
-            nc.gpsimd.dma_start(w2_s[r:P:32, :].bitcast(I32), w2_scales[0, r:SCALE_ROWS:4, :].bitcast(I32))
+            nc.sync.dma_start(w2_s[r:P:32, :].bitcast(I32), w2_scales[0, r:SCALE_ROWS:4, :].bitcast(I32))
+        nc.sync.dma_start(w1_first[:].bitcast(I32), w1_rows[:, :, 0 : PIECE // 2])
+        load_tab(0)
         for r in range(4):
-            nc.gpsimd.dma_start(tab_s[PASS_ROWS[0] + r : P : 16, :].bitcast(I32),
-                                tab_scales.rearrange("a (q r) t -> r q a t", r=4)[r].bitcast(I32))
-        nc.gpsimd.memset(w1_s[:].rearrange("p a c -> p (a c)").bitcast(I32), 0)
-        for r in range(4):
-            nc.gpsimd.dma_start(w1_s[r:P:32, :, :].bitcast(I32),
-                                w1_scales[:, r:SCALE_ROWS:4, :].rearrange("a q c -> q a c").bitcast(I32))
-        make_identity(nc, ident[:])
+            nc.sync.dma_start(w1_s[r:P:32, :, :].bitcast(I32),
+                              w1_scales[:, r:SCALE_ROWS:4, :].rearrange("a q c -> q a c").bitcast(I32))
+        load_tab(1)
 
         def half_list(offsets, h):
             return offsets[:, h * (HALF // 16) : (h + 1) * (HALF // 16)]
@@ -127,11 +130,15 @@ def tile_list_moisture_downscaling_kernel(
         for h in range(HALVES):
             nc.vector.tensor_copy(v2_w[h][:], tab2_w[:].indirect(half_list(list2, h)))
             nc.vector.tensor_copy(v2_s[h][:], tab2_s[:].indirect(half_list(list2, h)))
-        nc.sync.dma_start(w1_w[:].bitcast(I32), w1_words.rearrange("a p c -> p a c").bitcast(I32))
+        picked_s = held("tab2_s", [P, S], U8)
+        nc.vector.tensor_copy(picked_s[:], tab_s[:].indirect(list1[:]))
+        nc.sync.dma_start(lifted_s[0:LIVE_ROWS, :].bitcast(I32), picked_s[PASS1_ROW : PASS1_ROW + LIVE_ROWS, :].bitcast(I32))
+        nc.sync.dma_start(w1_rest[:].bitcast(I32), w1_rows[:, :, PIECE // 2 : H // 2])
         load_w3(1)
+        v_s = [picked_s, lifted_s]
 
         rough = held("rough", [P, HALVES * PACK], F32)
-        root0 = held("tab2_s", [P, HALVES * PACK], F32)
+        root0 = held("root0", [P, HALVES * PACK], F32)
         defect = held("defect", [P, HALVES * PACK], F32)
         root = held("root", [P, HALVES * PACK], F32)
         nc.scalar.activation(rough[:], trust_t[:], ACT.Abs_reciprocal_sqrt)
@@ -166,18 +173,14 @@ def tile_list_moisture_downscaling_kernel(
         def quantize(codes, scales, grouped):
             nc.vector.quantize_mx(out=codes.bitcast(FP8X4), scales=scales, in_=grouped.rearrange("p c t -> p (c t)"))
 
+        w3_first = round_cols(nc.scalar.copy, w3_raw[0][:], slice(0, PIECE), "w3_rounded")
         all_banks = A_BANKS + (OUT_BANK,) + NUM_BANKS + ROOT_BANKS
         b_order = [u for h in range(HALVES) for u in range(h, count, HALVES)]
         for i, u in enumerate(b_order):
             make_b(u, all_banks[i % len(all_banks)])
 
-        w3_first = round_cols(nc.vector.tensor_copy, w3_raw[0][:], slice(0, PIECE), "w3_rounded")
-        nc.vector.tensor_copy(picked_s[:], tab_s[:].indirect(list1[:]))
-        for a in range(2):
-            nc.gpsimd.dma_start(v_s[0:LIVE_ROWS, a, :].bitcast(I32),
-                                picked_s[PASS_ROWS[a] : PASS_ROWS[a] + LIVE_ROWS, :].bitcast(I32))
         quantize(w3_w[0][:], w3_s[0][:], w3_first)
-        v0_w = held("tab_s", [P, S], U32)
+        v0_w = placed("v0_w", [P, S], U32, 11 * T - 3072)
         nc.vector.tensor_copy(v0_w[:], tab_w[0][:].bitcast(U32).indirect(list1[:]))
         for h in range(HALVES):
             nc.sync.dma_start(grid_raw[h][:], grid[h * HALF : (h + 1) * HALF, :].rearrange("(p j) n -> p j n", j=PACK))
@@ -196,10 +199,11 @@ def tile_list_moisture_downscaling_kernel(
             nc.tensor.matmul_mx(acc[:], lhsT=w3_w[c][:, off : off + P].bitcast(FP8X4), lhsT_scale=w3_s[c][:, off : off + P],
                                 rhs=v2_w[h][:].bitcast(FP4X4), rhs_scale=v2_s[h][:],
                                 start=True, stop=False)
+            w1_cols = w1_first[:, :, 2 * off : 2 * (off + P)] if c == 0 else w1_rest[:, :, 2 * (rt * P - PIECE) : 2 * (rt * P - PIECE + P)]
             for a in range(2):
-                nc.tensor.matmul_mx(acc[:], lhsT=w1_w[:, a, 2 * rt * P : 2 * (rt + 1) * P].bitcast(FP4X4),
+                nc.tensor.matmul_mx(acc[:], lhsT=w1_cols[:, a, :].bitcast(FP4X4),
                                     lhsT_scale=w1_s[:, a, rt * P : (rt + 1) * P],
-                                    rhs=v_w[a][h].bitcast(FP8X4), rhs_scale=v_s[:, a, h * HALF : (h + 1) * HALF],
+                                    rhs=v_w[a][h].bitcast(FP8X4), rhs_scale=v_s[a][:, h * HALF : (h + 1) * HALF],
                                     start=False, stop=(a == 1))
             a_bank[u] = acc
 
@@ -222,7 +226,7 @@ def tile_list_moisture_downscaling_kernel(
 
         def turn(u):
             rt, h = units[u]
-            num_t[u] = bank(NUM_BANKS[u % 2], [P, PACK, P])
+            num_t[u] = bank(NUM_BANKS[u % 2] if u < count - 1 else A_BANKS[0], [P, PACK, P])
             for t in range(PACK):
                 nc.tensor.transpose(num_t[u][:, t, :], num[u][:, t, :], ident[:])
             factor[u] = ring.tile([P, PACK, P], F32, name="factor")
@@ -251,7 +255,7 @@ def tile_list_moisture_downscaling_kernel(
                                 start=(h == 0), stop=(h == HALVES - 1))
 
         def make_out(rt):
-            acc = bank(OUT_BANK, [P, F])
+            acc = bank(OUT_BANK if rt < R_TILES - 2 else ROOT_BANKS[(count - 1) % 2], [P, F])
             for h in range(HALVES):
                 out_pass(acc[:], rt, h, slice(0, F))
             result = ring.tile([P, F], F32, name="result")
@@ -264,18 +268,17 @@ def tile_list_moisture_downscaling_kernel(
         def last_pass(h):
             for side, cols in enumerate(sides):
                 if h == 0:
-                    last_banks.append(bank(A_BANKS[side], [P, HALF]))
+                    last_banks.append(bank((A_BANKS[1], OUT_BANK)[side], [P, HALF]))
                 out_pass(last_banks[side][:, 0 : F // 2], R_TILES - 1, h, cols)
 
-        pieces = []
+        pieces = [(w3_raw[1][:], slice(0, PIECE), w3_w[1][:], w3_s[1][:])]
         for h in range(HALVES):
             for n0 in range(0, F, PIECE):
                 cols = slice(n0, n0 + PIECE)
                 pieces.append((grid_raw[h][:], cols, grid_w[h][:, cols], grid_s[h][:, cols]))
         pieces.append((w3_raw[2][:], slice(0, PIECE), w3_w[2][:], w3_s[2][:]))
-        piece_at = {i + 1: piece for i, piece in enumerate(pieces)}
-        rounded = {-1: round_cols(nc.scalar.copy, w3_raw[1][:], slice(0, PIECE), "w3_rounded1")}
-        piece_at[-1] = (None, None, w3_w[1][:], w3_s[1][:])
+        piece_at = dict(enumerate(pieces))
+        rounded = {}
         out_at = {6: 0, 7: 1, 8: 2, 10: 3, 12: 4}
 
         make_a(0)

@@ -61,30 +61,37 @@ def tile_list_moisture_downscaling_kernel(
         ROOT_BANKS = ("root0", "root1")
         OUT_BANK = "o"
 
+        TAB2, TAB0, TAB1, W3A, W1A, WIN2, WIN = 0, 2 * T, 6 * T, 10 * T, 11 * T, 13 * T, 16 * T
         list1 = held("list1", [P, S // 16], U16)
         list2 = held("list2", [P, S // 16], U16)
-        tab2_w = placed("tab2_w", [P, T], U16, 0)
-        tab_w = [placed("tab_w%d" % a, [P, T], I32, 2 * T + a * 4 * T) for a in range(2)]
-        w1_first = held("w1_first", [P, 2, 2 * PIECE], U8)
-        w1_rest = placed("w1_rest", [P, 2, 2 * (H - PIECE)], U8, 11 * T + 1536)
-        w3_raw = [held("w3_raw0", [P, PACK, PIECE], F32), placed("w3_raw1", [P, PACK, PIECE], F32, 11 * T + 3584),
-                  placed("w3_raw2", [P, PACK, PIECE], F32, 6 * T)]
-        grid_raw = [placed("grid_raw%d" % h, [P, PACK, F], F32, 2 * T + h * 2 * T) for h in range(HALVES)]
-        tab_s = placed("tab_s", [P, T], U8, 11 * T)
-        tab2_s = held("tab2_s", [P, T], U8)
-        v2_w = [held("v2_w%d" % h, [P, HALF], U16) for h in range(HALVES)]
-        v2_s = [held("v2_s0", [P, HALF], U8), held("v2_s1", [P, HALF], U8)]
+        tab2_w = placed("tab2_w", [P, T], U16, TAB2)
+        tab_w = [placed("tab_w0", [P, T], I32, TAB0), placed("tab_w1", [P, T], I32, TAB1)]
+        tab_s = placed("tab_s", [P, T], U8, WIN)
+        tab2_s = placed("tab2_s", [P, T], U8, WIN2)
+        w1_first = placed("w1_first", [P, 2, 2 * PIECE], U8, W1A)
+        w1_rest = placed("w1_rest", [P, 2, 2 * (H - PIECE)], U8, WIN + 1024)
+        w3_raw = [placed("w3_raw0", [P, PACK, PIECE], F32, W3A), placed("w3_raw1", [P, PACK, PIECE], F32, WIN + 3072),
+                  placed("w3_raw2", [P, PACK, PIECE], F32, TAB1)]
+        grid_raw = [placed("grid_raw%d" % h, [P, PACK, F], F32, TAB0 + h * 2 * T) for h in range(HALVES)]
+        v2_w = [placed("v2_w%d" % h, [P, HALF], U16, WIN2 + h * 1024) for h in range(HALVES)]
+        w1_s = placed("w1_s", [P, 2, H], U8, WIN2 + 2048)
+        lifted_s = placed("lifted_s", [P, S], U8, WIN2 + 3584)
+        picked_s = placed("picked_s", [P, S], U8, TAB2)
+        const_t = placed("const_t", [P, R_TILES], F32, TAB2 + 1024)
+        v0_w = placed("v0_w", [P, S], U32, WIN - 3072)
+        trust_t = placed("trust_t", [P, HALVES * PACK], F32, TAB0)
+        rough = placed("rough", [P, HALVES * PACK], F32, W3A)
+        defect = placed("defect", [P, HALVES * PACK], F32, W1A)
+        root0 = placed("root0", [P, HALVES * PACK], F32, TAB1)
+        root = held("root", [P, HALVES * PACK], F32)
+        v2_s = held("v2_s", [P, S], U8)
         w1_rows = w1_words.rearrange("a p c -> p a c").bitcast(I32)
-        lifted_s = held("lifted_s", [P, S], U8)
-        w1_s = held("w1_s", [P, 2, H], U8)
         w2_w = held("w2_w", [P, H], I32)
         w2_s = held("w2_s", [P, H], U8)
         w3_w = [held("w3_w%d" % c, [P, PIECE], U32) for c in range(H // PIECE)]
         w3_s = [held("w3_s%d" % c, [P, PIECE], U8) for c in range(H // PIECE)]
         grid_w = [held("grid_w%d" % h, [P, F], U32) for h in range(HALVES)]
         grid_s = [held("grid_s%d" % h, [P, F], U8) for h in range(HALVES)]
-        const_t = held("const_t", [P, R_TILES], F32)
-        trust_t = held("trust_t", [P, HALVES * PACK], F32)
         ident = held("ident", [P, P], F32)
 
         def load_w3(c):
@@ -93,10 +100,11 @@ def tile_list_moisture_downscaling_kernel(
         def load_tab(a):
             nc.sync.dma_start(tab_w[a][:], tab_words[a].rearrange("p t i -> p (t i)").bitcast(I32))
 
-        nc.vector.memset(tab2_s[:].bitcast(I32), 0)
-        nc.gpsimd.memset(tab_s[:].bitcast(I32), 0)
-        for scale_tile in (w2_s[:], w1_s[:].rearrange("p a c -> p (a c)"), lifted_s[:]):
-            nc.vector.memset(scale_tile.bitcast(I32), 0)
+        def half_list(offsets, h):
+            return offsets[:, h * (HALF // 16) : (h + 1) * (HALF // 16)]
+
+        for scale_tile in (tab_s, tab2_s, w2_s):
+            nc.vector.memset(scale_tile[:].bitcast(I32), 0)
         for r in range(4):
             nc.gpsimd.dma_start(tab_s[r:P:PASS1_ROW, :].bitcast(I32),
                                 tab_scales.rearrange("a (q r) t -> r q a t", r=4)[r].bitcast(I32))
@@ -106,45 +114,38 @@ def tile_list_moisture_downscaling_kernel(
         nc.sync.dma_start(list1[:], offs)
         nc.sync.dma_start(trust_t[:].rearrange("p (h t) -> p h t", t=PACK),
                           trust.rearrange("(h p t) -> p h t", h=HALVES, t=PACK))
-        with nc.allow_non_contiguous_dma(reason="one value of const a partition and row tile"):
-            nc.sync.dma_start(const_t[:], const.rearrange("(t p) -> p t", p=P))
-        for c0 in range(0, T // 2, T // 8):
-            nc.sync.dma_start(tab2_w[:].bitcast(I32)[:, c0 : c0 + T // 8], tab2_words[0].bitcast(I32)[:, c0 : c0 + T // 8])
-        for c0 in range(0, H, H // 2):
-            nc.sync.dma_start(w2_w[:, c0 : c0 + H // 2], w2_words[0].rearrange("p c i -> p (c i)").bitcast(I32)[:, c0 : c0 + H // 2])
+        nc.sync.dma_start(tab2_w[:].bitcast(I32), tab2_words[0].bitcast(I32))
+        nc.sync.dma_start(w2_w[:], w2_words[0].rearrange("p c i -> p (c i)").bitcast(I32))
         for r in range(4):
             nc.sync.dma_start(tab2_s[r:P:32, :].bitcast(I32), tab2_scales[0, r:SCALE_ROWS:4, :].bitcast(I32))
-        load_w3(0)
+
+        nc.scalar.activation(rough[:], trust_t[:], ACT.Abs_reciprocal_sqrt)
+        nc.vector.tensor_tensor(root0[:], rough[:], trust_t[:], ALU.mult)
+        nc.vector.scalar_tensor_tensor(defect[:], root0[:], -0.5 * math.sqrt(2.0), rough[:], ALU.mult, ALU.mult)
+        nc.vector.scalar_tensor_tensor(root[:], defect[:], 1.5 * math.sqrt(2.0), root0[:], ALU.add, ALU.mult)
+
+        load_tab(0)
         for r in range(4):
             nc.sync.dma_start(w2_s[r:P:32, :].bitcast(I32), w2_scales[0, r:SCALE_ROWS:4, :].bitcast(I32))
+        load_w3(0)
         nc.sync.dma_start(w1_first[:].bitcast(I32), w1_rows[:, :, 0 : PIECE // 2])
-        load_tab(0)
+        load_tab(1)
+
+        nc.vector.tensor_copy(v2_s[:], tab2_s[:].indirect(list2[:]))
+        nc.vector.tensor_copy(v2_w[0][:], tab2_w[:].indirect(half_list(list2, 0)))
+        for scale_tile in (w1_s[:].rearrange("p a c -> p (a c)"), lifted_s[:]):
+            nc.vector.memset(scale_tile.bitcast(I32), 0)
         for r in range(4):
             nc.sync.dma_start(w1_s[r:P:32, :, :].bitcast(I32),
                               w1_scales[:, r:SCALE_ROWS:4, :].rearrange("a q c -> q a c").bitcast(I32))
-        load_tab(1)
-
-        def half_list(offsets, h):
-            return offsets[:, h * (HALF // 16) : (h + 1) * (HALF // 16)]
-
-        for h in range(HALVES):
-            nc.vector.tensor_copy(v2_w[h][:], tab2_w[:].indirect(half_list(list2, h)))
-            nc.vector.tensor_copy(v2_s[h][:], tab2_s[:].indirect(half_list(list2, h)))
-        picked_s = held("tab2_s", [P, S], U8)
+        nc.vector.tensor_copy(v2_w[1][:], tab2_w[:].indirect(half_list(list2, 1)))
+        with nc.allow_non_contiguous_dma(reason="one value of const a partition and row tile"):
+            nc.sync.dma_start(const_t[:], const.rearrange("(t p) -> p t", p=P))
         nc.vector.tensor_copy(picked_s[:], tab_s[:].indirect(list1[:]))
         nc.sync.dma_start(lifted_s[0:LIVE_ROWS, :].bitcast(I32), picked_s[PASS1_ROW : PASS1_ROW + LIVE_ROWS, :].bitcast(I32))
         nc.sync.dma_start(w1_rest[:].bitcast(I32), w1_rows[:, :, PIECE // 2 : H // 2])
         load_w3(1)
         v_s = [picked_s, lifted_s]
-
-        rough = held("rough", [P, HALVES * PACK], F32)
-        root0 = held("root0", [P, HALVES * PACK], F32)
-        defect = held("defect", [P, HALVES * PACK], F32)
-        root = held("root", [P, HALVES * PACK], F32)
-        nc.scalar.activation(rough[:], trust_t[:], ACT.Abs_reciprocal_sqrt)
-        nc.vector.tensor_tensor(root0[:], rough[:], trust_t[:], ALU.mult)
-        nc.vector.scalar_tensor_tensor(defect[:], root0[:], -0.5 * math.sqrt(2.0), rough[:], ALU.mult, ALU.mult)
-        nc.vector.scalar_tensor_tensor(root[:], defect[:], 1.5 * math.sqrt(2.0), root0[:], ALU.add, ALU.mult)
 
         units = [(rt, h) for rt in range(R_TILES) for h in range(HALVES)]
         count = len(units)
@@ -159,7 +160,7 @@ def tile_list_moisture_downscaling_kernel(
             acc = bank(name, [P, HALF])
             nc.tensor.matmul_mx(acc[:], lhsT=w2_w[:, rt * P : (rt + 1) * P].bitcast(FP8X4),
                                 lhsT_scale=w2_s[:, rt * P : (rt + 1) * P],
-                                rhs=v2_w[h][:].bitcast(FP4X4), rhs_scale=v2_s[h][:],
+                                rhs=v2_w[h][:].bitcast(FP4X4), rhs_scale=v2_s[:, h * HALF : (h + 1) * HALF],
                                 start=True, stop=True)
             half_b[u] = held("half_b%d" % u, [P, PACK, P], F32)
             nc.scalar.activation(half_b[u][:], by_slot(acc), ACT.Copy, scale=0.5)
@@ -180,7 +181,6 @@ def tile_list_moisture_downscaling_kernel(
             make_b(u, all_banks[i % len(all_banks)])
 
         quantize(w3_w[0][:], w3_s[0][:], w3_first)
-        v0_w = placed("v0_w", [P, S], U32, 11 * T - 3072)
         nc.vector.tensor_copy(v0_w[:], tab_w[0][:].bitcast(U32).indirect(list1[:]))
         for h in range(HALVES):
             nc.sync.dma_start(grid_raw[h][:], grid[h * HALF : (h + 1) * HALF, :].rearrange("(p j) n -> p j n", j=PACK))
@@ -197,7 +197,7 @@ def tile_list_moisture_downscaling_kernel(
             acc = bank(A_BANKS[u % len(A_BANKS)], [P, HALF])
             c, off = divmod(rt * P, PIECE)
             nc.tensor.matmul_mx(acc[:], lhsT=w3_w[c][:, off : off + P].bitcast(FP8X4), lhsT_scale=w3_s[c][:, off : off + P],
-                                rhs=v2_w[h][:].bitcast(FP4X4), rhs_scale=v2_s[h][:],
+                                rhs=v2_w[h][:].bitcast(FP4X4), rhs_scale=v2_s[:, h * HALF : (h + 1) * HALF],
                                 start=True, stop=False)
             w1_cols = w1_first[:, :, 2 * off : 2 * (off + P)] if c == 0 else w1_rest[:, :, 2 * (rt * P - PIECE) : 2 * (rt * P - PIECE + P)]
             for a in range(2):

@@ -77,7 +77,8 @@ def tile_list_moisture_downscaling_kernel(
         w1_s = placed("w1_s", [P, 2, H], U8, WIN2 + 2048)
         lifted_s = placed("lifted_s", [P, S], U8, WIN2 + 3584)
         picked_s = placed("picked_s", [P, S], U8, TAB2)
-        const_t = placed("const_t", [P, R_TILES], F32, TAB2 + 1024)
+        const_rows = held("const_rows", [P, P], F32)
+        const_t = held("const_t", [P, R_TILES], F32)
         v0_w = placed("v0_w", [P, S], U32, WIN - 3072)
         trust_t = placed("trust_t", [P, HALVES * PACK], F32, TAB0)
         rough = placed("rough", [P, HALVES * PACK], F32, W3A)
@@ -108,7 +109,9 @@ def tile_list_moisture_downscaling_kernel(
         for r in range(4):
             nc.gpsimd.dma_start(tab_s[r:P:PASS1_ROW, :].bitcast(I32),
                                 tab_scales.rearrange("a (q r) t -> r q a t", r=4)[r].bitcast(I32))
+        nc.gpsimd.memset(const_rows[0 : P - R_TILES, :], 0.0)
         make_identity(nc, ident[:])
+        nc.scalar.dma_start(const_rows[P - R_TILES : P, :], const.rearrange("(t p) -> t p", p=P))
 
         nc.sync.dma_start(list2[:], offs2)
         nc.sync.dma_start(list1[:], offs)
@@ -139,8 +142,6 @@ def tile_list_moisture_downscaling_kernel(
             nc.sync.dma_start(w1_s[r:P:32, :, :].bitcast(I32),
                               w1_scales[:, r:SCALE_ROWS:4, :].rearrange("a q c -> q a c").bitcast(I32))
         nc.vector.tensor_copy(v2_w[1][:], tab2_w[:].indirect(half_list(list2, 1)))
-        with nc.allow_non_contiguous_dma(reason="one value of const a partition and row tile"):
-            nc.sync.dma_start(const_t[:], const.rearrange("(t p) -> p t", p=P))
         nc.vector.tensor_copy(picked_s[:], tab_s[:].indirect(list1[:]))
         nc.sync.dma_start(lifted_s[0:LIVE_ROWS, :].bitcast(I32), picked_s[PASS1_ROW : PASS1_ROW + LIVE_ROWS, :].bitcast(I32))
         nc.sync.dma_start(w1_rest[:].bitcast(I32), w1_rows[:, :, PIECE // 2 : H // 2])
@@ -180,6 +181,9 @@ def tile_list_moisture_downscaling_kernel(
         for i, u in enumerate(b_order):
             make_b(u, all_banks[i % len(all_banks)])
 
+        const_turned = bank(ROOT_BANKS[1], [P, P])
+        nc.tensor.transpose(const_turned[:], const_rows[:], ident[:])
+        nc.scalar.copy(const_t[:], const_turned[:, P - R_TILES : P])
         quantize(w3_w[0][:], w3_s[0][:], w3_first)
         nc.vector.tensor_copy(v0_w[:], tab_w[0][:].bitcast(U32).indirect(list1[:]))
         for h in range(HALVES):

@@ -61,18 +61,20 @@ def tile_list_moisture_downscaling_kernel(
         ROOT_BANKS = ("root0", "root1")
         OUT_BANK = "o"
 
-        TAB2, TAB0, TAB1, W3A, W1A, WIN2, WIN = 0, 2 * T, 6 * T, 10 * T, 11 * T, 13 * T, 16 * T
+        TAB2, TAB0, TAB1, W3A, W1A, WIN2, WIN = 0, 4 * T, 10 * T, 14 * T, 15 * T, 17 * T, 20 * T
         list1 = held("list1", [P, S // 16], U16)
         list2 = held("list2", [P, S // 16], U16)
         tab2_w = placed("tab2_w", [P, T], U16, TAB2)
         tab_w = [placed("tab_w0", [P, T], I32, TAB0), placed("tab_w1", [P, T], I32, TAB1)]
         tab_s = placed("tab_s", [P, T], U8, WIN)
         tab2_s = placed("tab2_s", [P, T], U8, WIN2)
-        w1_first = placed("w1_first", [P, 2, 2 * PIECE], U8, W1A)
-        w1_rest = placed("w1_rest", [P, 2, 2 * (H - PIECE)], U8, WIN + 1024)
-        w3_raw = [placed("w3_raw0", [P, PACK, PIECE], F32, W3A), placed("w3_raw1", [P, PACK, PIECE], F32, WIN + 3072),
-                  placed("w3_raw2", [P, PACK, PIECE], F32, TAB1)]
-        grid_raw = [placed("grid_raw%d" % h, [P, PACK, F], F32, TAB0 + h * 2 * T) for h in range(HALVES)]
+        w1_first = placed("w1_first", [P, 2, 2 * P], U8, W1A)
+        w1_rest = placed("w1_rest", [P, 2, 2 * (H - P)], U8, WIN + 1024)
+        w3_cuts = (0, P, 2 * P, 4 * P, H)
+        w3_cols = [slice(c0, c1) for c0, c1 in zip(w3_cuts, w3_cuts[1:])]
+        w3_at = (W3A, WIN + 3584, TAB0 + 64 - T, TAB0 + 64)
+        w3_raw = [placed("w3_raw%d" % c, [P, PACK, cols.stop - cols.start], F32, w3_at[c]) for c, cols in enumerate(w3_cols)]
+        grid_raw = [placed("grid_raw%d" % h, [P, PACK, F], F32, TAB0 + 64 + T + h * 2 * T) for h in range(HALVES)]
         v2_w = [placed("v2_w%d" % h, [P, HALF], U16, WIN2 + h * 1024) for h in range(HALVES)]
         w1_s = placed("w1_s", [P, 2, H], U8, WIN2 + 2048)
         lifted_s = placed("lifted_s", [P, S], U8, WIN2 + 3584)
@@ -89,14 +91,15 @@ def tile_list_moisture_downscaling_kernel(
         w1_rows = w1_words.rearrange("a p c -> p a c").bitcast(I32)
         w2_w = held("w2_w", [P, H], I32)
         w2_s = held("w2_s", [P, H], U8)
-        w3_w = [held("w3_w%d" % c, [P, PIECE], U32) for c in range(H // PIECE)]
-        w3_s = [held("w3_s%d" % c, [P, PIECE], U8) for c in range(H // PIECE)]
+        w3_w = {0: held("w3_w0", [P, P], U32)}
+        w3_s = [held("w3_s%d" % c, [P, cols.stop - cols.start], U8) if c != 1 else None for c, cols in enumerate(w3_cols)]
+        w3_s[1] = placed("w3_s_second", [P, P], U8, TAB1)
         grid_w = [held("grid_w%d" % h, [P, F], U32) for h in range(HALVES)]
         grid_s = [held("grid_s%d" % h, [P, F], U8) for h in range(HALVES)]
         ident = held("ident", [P, P], F32)
 
         def load_w3(c):
-            nc.sync.dma_start(w3_raw[c][:], w3[:, c * PIECE : (c + 1) * PIECE].rearrange("(p j) r -> p j r", j=PACK))
+            nc.sync.dma_start(w3_raw[c][:], w3[:, w3_cols[c]].rearrange("(p j) r -> p j r", j=PACK))
 
         def load_tab(a):
             nc.sync.dma_start(tab_w[a][:], tab_words[a].rearrange("p t i -> p (t i)").bitcast(I32))
@@ -104,14 +107,13 @@ def tile_list_moisture_downscaling_kernel(
         def half_list(offsets, h):
             return offsets[:, h * (HALF // 16) : (h + 1) * (HALF // 16)]
 
+        make_identity(nc, ident[:])
         for scale_tile in (tab_s, tab2_s, w2_s):
             nc.vector.memset(scale_tile[:].bitcast(I32), 0)
+        nc.vector.memset(const_rows[0 : P - R_TILES, :], 0.0)
         for r in range(4):
             nc.gpsimd.dma_start(tab_s[r:P:PASS1_ROW, :].bitcast(I32),
                                 tab_scales.rearrange("a (q r) t -> r q a t", r=4)[r].bitcast(I32))
-        nc.gpsimd.memset(const_rows[0 : P - R_TILES, :], 0.0)
-        make_identity(nc, ident[:])
-        nc.scalar.dma_start(const_rows[P - R_TILES : P, :], const.rearrange("(t p) -> t p", p=P))
 
         nc.sync.dma_start(list2[:], offs2)
         nc.sync.dma_start(list1[:], offs)
@@ -119,6 +121,7 @@ def tile_list_moisture_downscaling_kernel(
                           trust.rearrange("(h p t) -> p h t", h=HALVES, t=PACK))
         nc.sync.dma_start(tab2_w[:].bitcast(I32), tab2_words[0].bitcast(I32))
         nc.sync.dma_start(w2_w[:], w2_words[0].rearrange("p c i -> p (c i)").bitcast(I32))
+        nc.sync.dma_start(const_rows[P - R_TILES : P, :], const.rearrange("(t p) -> t p", p=P))
         for r in range(4):
             nc.sync.dma_start(tab2_s[r:P:32, :].bitcast(I32), tab2_scales[0, r:SCALE_ROWS:4, :].bitcast(I32))
 
@@ -127,11 +130,11 @@ def tile_list_moisture_downscaling_kernel(
         nc.vector.scalar_tensor_tensor(defect[:], root0[:], -0.5 * math.sqrt(2.0), rough[:], ALU.mult, ALU.mult)
         nc.vector.scalar_tensor_tensor(root[:], defect[:], 1.5 * math.sqrt(2.0), root0[:], ALU.add, ALU.mult)
 
-        load_tab(0)
         for r in range(4):
             nc.sync.dma_start(w2_s[r:P:32, :].bitcast(I32), w2_scales[0, r:SCALE_ROWS:4, :].bitcast(I32))
         load_w3(0)
-        nc.sync.dma_start(w1_first[:].bitcast(I32), w1_rows[:, :, 0 : PIECE // 2])
+        nc.sync.dma_start(w1_first[:].bitcast(I32), w1_rows[:, :, 0 : P // 2])
+        load_tab(0)
         load_tab(1)
 
         nc.vector.tensor_copy(v2_s[:], tab2_s[:].indirect(list2[:]))
@@ -144,8 +147,8 @@ def tile_list_moisture_downscaling_kernel(
         nc.vector.tensor_copy(v2_w[1][:], tab2_w[:].indirect(half_list(list2, 1)))
         nc.vector.tensor_copy(picked_s[:], tab_s[:].indirect(list1[:]))
         nc.sync.dma_start(lifted_s[0:LIVE_ROWS, :].bitcast(I32), picked_s[PASS1_ROW : PASS1_ROW + LIVE_ROWS, :].bitcast(I32))
-        nc.sync.dma_start(w1_rest[:].bitcast(I32), w1_rows[:, :, PIECE // 2 : H // 2])
         load_w3(1)
+        nc.sync.dma_start(w1_rest[:].bitcast(I32), w1_rows[:, :, P // 2 : H // 2])
         v_s = [picked_s, lifted_s]
 
         units = [(rt, h) for rt in range(R_TILES) for h in range(HALVES)]
@@ -166,32 +169,35 @@ def tile_list_moisture_downscaling_kernel(
             half_b[u] = held("half_b%d" % u, [P, PACK, P], F32)
             nc.scalar.activation(half_b[u][:], by_slot(acc), ACT.Copy, scale=0.5)
 
-        def round_cols(copy, raw, cols, name):
-            grouped = held(name, [P, PIECE, PACK], BF16)
-            dst, src = weave(grouped[:], raw[:, :, cols])
-            copy(dst, src)
+        def round_on_scalar(raw, name):
+            grouped = held(name, [P, raw.shape[2], PACK], BF16)
+            dst, src = weave(grouped[:], raw)
+            nc.scalar.copy(dst, src)
             return grouped[:]
+
 
         def quantize(codes, scales, grouped):
             nc.vector.quantize_mx(out=codes.bitcast(FP8X4), scales=scales, in_=grouped.rearrange("p c t -> p (c t)"))
 
-        w3_first = round_cols(nc.scalar.copy, w3_raw[0][:], slice(0, PIECE), "w3_rounded")
+        const_turned = bank(ROOT_BANKS[0], [P, P])
+        nc.tensor.transpose(const_turned[:], const_rows[:], ident[:])
+        nc.scalar.copy(const_t[:], const_turned[:, P - R_TILES : P])
         all_banks = A_BANKS + (OUT_BANK,) + NUM_BANKS + ROOT_BANKS
         b_order = [u for h in range(HALVES) for u in range(h, count, HALVES)]
         for i, u in enumerate(b_order):
             make_b(u, all_banks[i % len(all_banks)])
 
-        const_turned = bank(ROOT_BANKS[1], [P, P])
-        nc.tensor.transpose(const_turned[:], const_rows[:], ident[:])
-        nc.scalar.copy(const_t[:], const_turned[:, P - R_TILES : P])
-        quantize(w3_w[0][:], w3_s[0][:], w3_first)
         nc.vector.tensor_copy(v0_w[:], tab_w[0][:].bitcast(U32).indirect(list1[:]))
+        load_w3(2)
+        load_w3(3)
         for h in range(HALVES):
             nc.sync.dma_start(grid_raw[h][:], grid[h * HALF : (h + 1) * HALF, :].rearrange("(p j) n -> p j n", j=PACK))
-        v1_w = held("w3_rounded", [P, S], U32)
+        w3_first = placed("w3_first", [P, P, PACK], BF16, TAB2 + 2048)
+        nc.vector.tensor_copy(*weave(w3_first[:], w3_raw[0][:]))
+        v1_w = placed("v1_w", [P, S], U32, TAB2 + 2048)
+        quantize(w3_w[0][:], w3_s[0][:], w3_first[:])
         for h in range(HALVES):
             nc.vector.tensor_copy(v1_w[:, h * HALF : (h + 1) * HALF], tab_w[1][:].bitcast(U32).indirect(half_list(list1, h)))
-        load_w3(2)
 
         v_w = [[words[:, h * HALF : (h + 1) * HALF] for h in range(HALVES)] for words in (v0_w, v1_w)]
         a_bank, num, den, rsq, num_t, factor, z_bf, z_w, z_s = ({} for i in range(9))
@@ -199,11 +205,12 @@ def tile_list_moisture_downscaling_kernel(
         def make_a(u):
             rt, h = units[u]
             acc = bank(A_BANKS[u % len(A_BANKS)], [P, HALF])
-            c, off = divmod(rt * P, PIECE)
+            c = max(c for c, cols in enumerate(w3_cols) if cols.start <= rt * P)
+            off = rt * P - w3_cols[c].start
             nc.tensor.matmul_mx(acc[:], lhsT=w3_w[c][:, off : off + P].bitcast(FP8X4), lhsT_scale=w3_s[c][:, off : off + P],
                                 rhs=v2_w[h][:].bitcast(FP4X4), rhs_scale=v2_s[:, h * HALF : (h + 1) * HALF],
                                 start=True, stop=False)
-            w1_cols = w1_first[:, :, 2 * off : 2 * (off + P)] if c == 0 else w1_rest[:, :, 2 * (rt * P - PIECE) : 2 * (rt * P - PIECE + P)]
+            w1_cols = w1_first[:] if rt == 0 else w1_rest[:, :, 2 * (rt - 1) * P : 2 * rt * P]
             for a in range(2):
                 nc.tensor.matmul_mx(acc[:], lhsT=w1_cols[:, a, :].bitcast(FP4X4),
                                     lhsT_scale=w1_s[:, a, rt * P : (rt + 1) * P],
@@ -275,15 +282,21 @@ def tile_list_moisture_downscaling_kernel(
                     last_banks.append(bank((A_BANKS[1], OUT_BANK)[side], [P, HALF]))
                 out_pass(last_banks[side][:, 0 : F // 2], R_TILES - 1, h, cols)
 
-        pieces = [(w3_raw[1][:], slice(0, PIECE), w3_w[1][:], w3_s[1][:])]
-        for h in range(HALVES):
-            for n0 in range(0, F, PIECE):
-                cols = slice(n0, n0 + PIECE)
-                pieces.append((grid_raw[h][:], cols, grid_w[h][:, cols], grid_s[h][:, cols]))
-        pieces.append((w3_raw[2][:], slice(0, PIECE), w3_w[2][:], w3_s[2][:]))
+        w3_w[1] = None
+        pieces = [(w3_raw[2][:], 2), (w3_raw[3][:], 3)] + [(grid_raw[h][:, :, n0 : n0 + PIECE], (h, slice(n0, n0 + PIECE))) for h in range(HALVES) for n0 in range(0, F, PIECE)]
         piece_at = dict(enumerate(pieces))
         rounded = {}
+        w3_second = round_on_scalar(w3_raw[1][:], "w3_rounded1")
         out_at = {6: 0, 7: 1, 8: 2, 10: 3, 12: 4}
+
+        def quantize_piece(i):
+            where = piece_at[i][1]
+            if isinstance(where, int):
+                w3_w[where] = held("w3_w%d" % where, [P, PIECE], U32)
+                quantize(w3_w[where][:], w3_s[where][:], rounded[i])
+            else:
+                h, cols = where
+                quantize(grid_w[h][:, cols], grid_s[h][:, cols], rounded[i])
 
         make_a(0)
         for i in range(count + 3):
@@ -295,14 +308,17 @@ def tile_list_moisture_downscaling_kernel(
                 make_num(i)
             if i >= 3:
                 quantize_z(i - 3)
+            if i == 0:
+                w3_w[1] = held("w3_w1", [P, P], U32)
+                quantize(w3_w[1][:], w3_s[1][:], w3_second)
             if i - 1 in piece_at:
-                quantize(piece_at[i - 1][2], piece_at[i - 1][3], rounded[i - 1])
+                quantize_piece(i - 1)
             if i < count:
                 make_root(i)
             if 2 <= i < count + 2:
                 make_z(i - 2)
             if i in piece_at:
-                rounded[i] = round_cols(nc.scalar.copy, piece_at[i][0], piece_at[i][1], "half_b%d" % i)
+                rounded[i] = round_on_scalar(piece_at[i][0], "half_b%d" % i)
             if i in out_at:
                 make_out(out_at[i])
             if i == count + 1:

@@ -26,6 +26,7 @@ R_TILES = H // P
 SCALE_ROWS = 16
 PIECE = 256
 PASS1_ROW = 16
+LAG = 3
 LIVE_ROWS = 100
 
 
@@ -44,7 +45,7 @@ def tile_list_moisture_downscaling_kernel(
     with ExitStack() as ctx:
         keep = ctx.enter_context(tc.tile_pool(name="keep", bufs=1))
         loads = ctx.enter_context(tc.tile_pool(name="loads", bufs=1))
-        ring = ctx.enter_context(tc.tile_pool(name="ring", bufs=3))
+        ring = ctx.enter_context(tc.tile_pool(name="ring", bufs=4))
         psum = ctx.enter_context(tc.psum_pool(name="psum", bufs=1))
 
         def held(name, shape, dtype):
@@ -225,21 +226,24 @@ def tile_list_moisture_downscaling_kernel(
         def slot_groups(u):
             return [slice(0, PACK // 2), slice(PACK // 2, PACK)] if u == count - 1 else [slice(0, PACK)]
 
+        def make_den(u):
+            den[u] = ring.tile([P, PACK, P], F32, name="den")
+            nc.vector.scalar_tensor_tensor(den[u][:], by_slot(a_bank[u]), 0.0, num[u][:], ALU.max, ALU.subtract)
+
         def make_root(u):
             rt, h = units[u]
-            den[u] = ring.tile([P, PACK, P], F32, name="den")
             rsq[u] = ring.tile([P, PACK, P], F32, name="rsq")
             for slots in slot_groups(u):
-                nc.vector.scalar_tensor_tensor(den[u][:, slots, :], by_slot(a_bank[u])[:, slots, :], 0.0,
-                                               num[u][:, slots, :], ALU.max, ALU.subtract)
                 nc.scalar.activation(rsq[u][:, slots, :], den[u][:, slots, :], ACT.Abs_reciprocal_sqrt,
                                      bias=const_t[:, rt : rt + 1], scale=2.0)
 
-        def turn(u):
-            rt, h = units[u]
+        def turn_num(u):
             num_t[u] = bank(NUM_BANKS[u % 2] if u < count - 1 else A_BANKS[0], [P, PACK, P])
             for t in range(PACK):
                 nc.tensor.transpose(num_t[u][:, t, :], num[u][:, t, :], ident[:])
+
+        def make_factor(u):
+            rt, h = units[u]
             factor[u] = ring.tile([P, PACK, P], F32, name="factor")
             for g, slots in enumerate(slot_groups(u)):
                 rsq_t = bank(ROOT_BANKS[(u + g) % 2], [P, PACK, P])
@@ -265,65 +269,72 @@ def tile_list_moisture_downscaling_kernel(
                                 rhs=grid_w[h][:, cols].bitcast(FP8X4), rhs_scale=grid_s[h][:, cols],
                                 start=(h == 0), stop=(h == HALVES - 1))
 
+        def w3_codes(c):
+            w3_w[c] = held("w3_w%d" % c, [P, w3_cols[c].stop - w3_cols[c].start], U32)
+            return w3_w[c][:]
+
+        out_bank = {}
+
         def make_out(rt):
-            acc = bank(OUT_BANK if rt < R_TILES - 2 else ROOT_BANKS[(count - 1) % 2], [P, F])
+            out_bank[rt] = bank(OUT_BANK, [P, F])
             for h in range(HALVES):
-                out_pass(acc[:], rt, h, slice(0, F))
+                out_pass(out_bank[rt][:], rt, h, slice(0, F))
+
+        def store_out(rt):
             result = ring.tile([P, F], F32, name="result")
-            nc.scalar.copy(result[:], acc[:])
+            nc.scalar.copy(result[:], out_bank[rt][:])
             nc.sync.dma_start(out[rt * P : (rt + 1) * P, :], result[:])
 
-        sides = [slice(0, F // 2), slice(F // 2, F)]
-        last_banks = []
-
-        def last_pass(h):
-            for side, cols in enumerate(sides):
-                if h == 0:
-                    last_banks.append(bank((A_BANKS[1], OUT_BANK)[side], [P, HALF]))
-                out_pass(last_banks[side][:, 0 : F // 2], R_TILES - 1, h, cols)
-
-        w3_w[1] = None
-        pieces = [(w3_raw[2][:], 2), (w3_raw[3][:], 3)] + [(grid_raw[h][:, :, n0 : n0 + PIECE], (h, slice(n0, n0 + PIECE))) for h in range(HALVES) for n0 in range(0, F, PIECE)]
-        piece_at = dict(enumerate(pieces))
+        grid_pieces = [(grid_raw[h][:, :, n0 : n0 + PIECE], grid_w[h][:, n0 : n0 + PIECE], grid_s[h][:, n0 : n0 + PIECE])
+                       for h in range(HALVES) for n0 in range(0, F, PIECE)]
+        w3_pieces = [(w3_raw[c][:], w3_codes(c), w3_s[c][:]) for c in range(1, len(w3_cols))]
+        pieces = w3_pieces + grid_pieces
         rounded = {}
-        w3_second = round_on_scalar(w3_raw[1][:], "w3_rounded1")
-        out_at = {6: 0, 7: 1, 8: 2, 10: 3, 12: 4}
 
-        def quantize_piece(i):
-            where = piece_at[i][1]
-            if isinstance(where, int):
-                w3_w[where] = held("w3_w%d" % where, [P, PIECE], U32)
-                quantize(w3_w[where][:], w3_s[where][:], rounded[i])
-            else:
-                h, cols = where
-                quantize(grid_w[h][:, cols], grid_s[h][:, cols], rounded[i])
+        def round_piece(i):
+            raw = pieces[i][0]
+            rounded[i] = held("half_b%d" % i if i > 0 else "w3_second", [P, raw.shape[2], PACK], BF16)
+            nc.scalar.copy(*weave(rounded[i][:], raw))
+
+        out_made_at = {7: 0, 8: 1, 9: 2, 10: 3}
+        sides = [slice(0, F // 2), slice(F // 2, F)]
 
         make_a(0)
-        for i in range(count + 3):
-            if i + 1 < count:
-                make_a(i + 1)
+        make_a(1)
+        for i in range(count + LAG):
             if 1 <= i <= count:
-                turn(i - 1)
+                make_root(i - 1)
             if i < count:
                 make_num(i)
-            if i >= 3:
-                quantize_z(i - 3)
-            if i == 0:
-                w3_w[1] = held("w3_w1", [P, P], U32)
-                quantize(w3_w[1][:], w3_s[1][:], w3_second)
-            if i - 1 in piece_at:
-                quantize_piece(i - 1)
-            if i < count:
-                make_root(i)
+            if i >= LAG:
+                make_z(i - LAG)
             if 2 <= i < count + 2:
-                make_z(i - 2)
-            if i in piece_at:
-                rounded[i] = round_on_scalar(piece_at[i][0], "half_b%d" % i)
-            if i in out_at:
-                make_out(out_at[i])
-            if i == count + 1:
-                last_pass(0)
-        last_pass(1)
+                turn_num(i - 2)
+            if i < len(pieces):
+                round_piece(i)
+            if i - 1 in out_made_at:
+                store_out(out_made_at[i - 1])
+            if 1 <= i <= count:
+                make_factor(i - 1)
+            if i < count:
+                make_den(i)
+            if i >= LAG:
+                quantize_z(i - LAG)
+            if i == 0:
+                quantize(pieces[0][1], pieces[0][2], rounded[0][:])
+            if 2 <= i <= len(pieces):
+                quantize(pieces[i - 1][1], pieces[i - 1][2], rounded[i - 1][:])
+            if i + 2 < count:
+                make_a(i + 2)
+            if i in out_made_at:
+                make_out(out_made_at[i])
+            if i == count:
+                make_out(R_TILES - 2)
+                store_out(R_TILES - 2)
+        last_banks = [bank(name, [P, HALF]) for name in (A_BANKS[1], A_BANKS[2])]
+        for h in range(HALVES):
+            for side, cols in enumerate(sides):
+                out_pass(last_banks[side][:, 0 : F // 2], R_TILES - 1, h, cols)
         for side, empty in enumerate((nc.scalar.copy, nc.vector.tensor_copy)):
             part = ring.tile([P, F // 2], F32, name="part")
             empty(part[:], last_banks[side][:, 0 : F // 2])

@@ -46,6 +46,7 @@ def tile_list_moisture_downscaling_kernel(
         keep = ctx.enter_context(tc.tile_pool(name="keep", bufs=1))
         loads = ctx.enter_context(tc.tile_pool(name="loads", bufs=1))
         ring = ctx.enter_context(tc.tile_pool(name="ring", bufs=4))
+        stage = ctx.enter_context(tc.tile_pool(name="stage", bufs=1))
         psum = ctx.enter_context(tc.psum_pool(name="psum", bufs=1))
 
         def held(name, shape, dtype):
@@ -201,7 +202,10 @@ def tile_list_moisture_downscaling_kernel(
             nc.vector.tensor_copy(v1_w[:, h * HALF : (h + 1) * HALF], tab_w[1][:].bitcast(U32).indirect(half_list(list1, h)))
 
         v_w = [[words[:, h * HALF : (h + 1) * HALF] for h in range(HALVES)] for words in (v0_w, v1_w)]
-        a_bank, num, den, rsq, num_t, factor, z_bf, z_w, z_s = ({} for i in range(9))
+        a_bank, num, den, rsq, num_t, rsq_t, factor, z_bf, z_w, z_s = ({} for i in range(10))
+
+        def staged(name, shape, dtype, place):
+            return stage.tile(shape, dtype, name=name, align_bytes=64, offset=place * 4 * HALF)
 
         def make_a(u):
             rt, h = units[u]
@@ -223,9 +227,6 @@ def tile_list_moisture_downscaling_kernel(
             num[u] = ring.tile([P, PACK, P], F32, name="num")
             nc.vector.scalar_tensor_tensor(num[u][:], by_slot(a_bank[u]), 0.5, half_b[u][:], ALU.mult, ALU.subtract)
 
-        def slot_groups(u):
-            return [slice(0, PACK // 2), slice(PACK // 2, PACK)] if u == count - 1 else [slice(0, PACK)]
-
         def make_den(u):
             den[u] = ring.tile([P, PACK, P], F32, name="den")
             nc.vector.scalar_tensor_tensor(den[u][:], by_slot(a_bank[u]), 0.0, num[u][:], ALU.max, ALU.subtract)
@@ -233,28 +234,27 @@ def tile_list_moisture_downscaling_kernel(
         def make_root(u):
             rt, h = units[u]
             rsq[u] = ring.tile([P, PACK, P], F32, name="rsq")
-            for slots in slot_groups(u):
-                nc.scalar.activation(rsq[u][:, slots, :], den[u][:, slots, :], ACT.Abs_reciprocal_sqrt,
-                                     bias=const_t[:, rt : rt + 1], scale=2.0)
+            nc.scalar.activation(rsq[u][:], den[u][:], ACT.Abs_reciprocal_sqrt, bias=const_t[:, rt : rt + 1], scale=2.0)
 
         def turn_num(u):
             num_t[u] = bank(NUM_BANKS[u % 2] if u < count - 1 else A_BANKS[0], [P, PACK, P])
             for t in range(PACK):
                 nc.tensor.transpose(num_t[u][:, t, :], num[u][:, t, :], ident[:])
 
+        def turn_root(u):
+            rsq_t[u] = bank(ROOT_BANKS[u % 2], [P, PACK, P])
+            for t in range(PACK):
+                nc.tensor.transpose(rsq_t[u][:, t, :], rsq[u][:, t, :], ident[:])
+
         def make_factor(u):
             rt, h = units[u]
-            factor[u] = ring.tile([P, PACK, P], F32, name="factor")
-            for g, slots in enumerate(slot_groups(u)):
-                rsq_t = bank(ROOT_BANKS[(u + g) % 2], [P, PACK, P])
-                for t in range(slots.start, slots.stop):
-                    nc.tensor.transpose(rsq_t[:, t, :], rsq[u][:, t, :], ident[:])
-                for t in range(slots.start, slots.stop):
-                    nc.scalar.activation(factor[u][:, t, :], rsq_t[:, t, :], ACT.Square,
-                                         scale=root[:, h * PACK + t : h * PACK + t + 1])
+            factor[u] = staged("factor%d" % u, [P, PACK, P], F32, u)
+            for t in range(PACK):
+                nc.scalar.activation(factor[u][:, t, :], rsq_t[u][:, t, :], ACT.Square,
+                                     scale=root[:, h * PACK + t : h * PACK + t + 1])
 
         def make_z(u):
-            z_bf[u] = ring.tile([P, P, PACK], BF16, name="z_bf", align_bytes=64)
+            z_bf[u] = staged("z_bf%d" % u, [P, P, PACK], BF16, u + 2 if u + 2 < count - 2 else count + u % 2)
             dst, src = weave(z_bf[u][:], num_t[u][:])
             nc.vector.tensor_tensor(dst, src, weave(z_bf[u][:], factor[u][:])[1], ALU.mult)
 
@@ -296,7 +296,7 @@ def tile_list_moisture_downscaling_kernel(
             rounded[i] = held("half_b%d" % i if i > 0 else "w3_second", [P, raw.shape[2], PACK], BF16)
             nc.scalar.copy(*weave(rounded[i][:], raw))
 
-        out_made_at = {7: 0, 8: 1, 9: 2, 10: 3}
+        out_made_at = {7: 0, 8: 1, 9: 2, 10: 3, 12: 4}
         sides = [slice(0, F // 2), slice(F // 2, F)]
 
         make_a(0)
@@ -304,18 +304,20 @@ def tile_list_moisture_downscaling_kernel(
         for i in range(count + LAG):
             if 1 <= i <= count:
                 make_root(i - 1)
+            if 2 <= i < count + 2:
+                make_factor(i - 2)
             if i < count:
                 make_num(i)
             if i >= LAG:
                 make_z(i - LAG)
             if 2 <= i < count + 2:
                 turn_num(i - 2)
+            if 1 <= i <= count:
+                turn_root(i - 1)
             if i < len(pieces):
                 round_piece(i)
             if i - 1 in out_made_at:
                 store_out(out_made_at[i - 1])
-            if 1 <= i <= count:
-                make_factor(i - 1)
             if i < count:
                 make_den(i)
             if i >= LAG:
@@ -328,9 +330,6 @@ def tile_list_moisture_downscaling_kernel(
                 make_a(i + 2)
             if i in out_made_at:
                 make_out(out_made_at[i])
-            if i == count:
-                make_out(R_TILES - 2)
-                store_out(R_TILES - 2)
         last_banks = [bank(name, [P, HALF]) for name in (A_BANKS[1], A_BANKS[2])]
         for h in range(HALVES):
             for side, cols in enumerate(sides):

@@ -237,7 +237,7 @@ def tile_list_moisture_downscaling_kernel(
             nc.scalar.activation(rsq[u][:], den[u][:], ACT.Abs_reciprocal_sqrt, bias=const_t[:, rt : rt + 1], scale=2.0)
 
         def turn_num(u):
-            num_t[u] = bank(NUM_BANKS[u % 2] if u < count - 1 else A_BANKS[0], [P, PACK, P])
+            num_t[u] = bank(NUM_BANKS[u % 2], [P, PACK, P])
             for t in range(PACK):
                 nc.tensor.transpose(num_t[u][:, t, :], num[u][:, t, :], ident[:])
 
@@ -254,7 +254,7 @@ def tile_list_moisture_downscaling_kernel(
                                      scale=root[:, h * PACK + t : h * PACK + t + 1])
 
         def make_z(u):
-            z_bf[u] = staged("z_bf%d" % u, [P, P, PACK], BF16, u + 2 if u + 2 < count - 2 else count + u % 2)
+            z_bf[u] = staged("z_bf%d" % u, [P, P, PACK], BF16, u + 2 if u + 2 < count - 3 else count + u % 3)
             dst, src = weave(z_bf[u][:], num_t[u][:])
             nc.vector.tensor_tensor(dst, src, weave(z_bf[u][:], factor[u][:])[1], ALU.mult)
 
@@ -276,7 +276,7 @@ def tile_list_moisture_downscaling_kernel(
         out_bank = {}
 
         def make_out(rt):
-            out_bank[rt] = bank(OUT_BANK, [P, F])
+            out_bank[rt] = bank((OUT_BANK, OUT_BANK, A_BANKS[0], ROOT_BANKS[0], OUT_BANK)[rt], [P, F])
             for h in range(HALVES):
                 out_pass(out_bank[rt][:], rt, h, slice(0, F))
 
@@ -290,17 +290,24 @@ def tile_list_moisture_downscaling_kernel(
         w3_pieces = [(w3_raw[c][:], w3_codes(c), w3_s[c][:]) for c in range(1, len(w3_cols))]
         pieces = w3_pieces + grid_pieces
         rounded = {}
+        rounded_at = {1: 1, 2: 2, 4: 3, 5: 4, 7: 5, 8: 6}
+        on_vector = ()
 
-        def round_piece(i):
-            raw = pieces[i][0]
-            rounded[i] = held("half_b%d" % i if i > 0 else "w3_second", [P, raw.shape[2], PACK], BF16)
-            nc.scalar.copy(*weave(rounded[i][:], raw))
+        def round_piece(k, name):
+            raw = pieces[k][0]
+            rounded[k] = held(name, [P, raw.shape[2], PACK], BF16)
+            (nc.vector.tensor_copy if k in on_vector else nc.scalar.copy)(*weave(rounded[k][:], raw))
 
-        out_made_at = {7: 0, 8: 1, 9: 2, 10: 3, 12: 4}
+        def quantize_piece(k):
+            quantize(pieces[k][1], pieces[k][2], rounded[k][:])
+
+        out_made_at = {9: [0], 10: [1], 11: [2], 12: [3, 4]}
+        out_stored_at = {10: [0], 11: [1], 13: [2, 3, 4]}
         sides = [slice(0, F // 2), slice(F // 2, F)]
 
         make_a(0)
         make_a(1)
+        round_piece(0, "w3_second")
         for i in range(count + LAG):
             if 1 <= i <= count:
                 make_root(i - 1)
@@ -308,28 +315,35 @@ def tile_list_moisture_downscaling_kernel(
                 make_factor(i - 2)
             if i < count:
                 make_num(i)
-            if i >= LAG:
-                make_z(i - LAG)
-            if 2 <= i < count + 2:
-                turn_num(i - 2)
-            if 1 <= i <= count:
-                turn_root(i - 1)
-            if i < len(pieces):
-                round_piece(i)
-            if i - 1 in out_made_at:
-                store_out(out_made_at[i - 1])
-            if i < count:
+            if i == count - 1:
+                quantize_z(i - 1 - LAG)
                 make_den(i)
             if i >= LAG:
+                make_z(i - LAG)
+            if 2 <= i <= count:
+                turn_num(i - 2)
+            if i == count:
+                turn_num(count - 1)
+            if 1 <= i <= count:
+                turn_root(i - 1)
+            if rounded_at.get(i) not in on_vector + (None,):
+                round_piece(rounded_at[i], "half_b%d" % i)
+            for rt in out_stored_at.get(i, []):
+                store_out(rt)
+            if i < count - 1:
+                make_den(i)
+            if i >= LAG and i != count - 2:
                 quantize_z(i - LAG)
             if i == 0:
-                quantize(pieces[0][1], pieces[0][2], rounded[0][:])
-            if 2 <= i <= len(pieces):
-                quantize(pieces[i - 1][1], pieces[i - 1][2], rounded[i - 1][:])
+                quantize_piece(0)
+            if i - 1 in rounded_at:
+                quantize_piece(rounded_at[i - 1])
+            if rounded_at.get(i) in on_vector:
+                round_piece(rounded_at[i], "half_b%d" % i)
             if i + 2 < count:
                 make_a(i + 2)
-            if i in out_made_at:
-                make_out(out_made_at[i])
+            for rt in out_made_at.get(i, []):
+                make_out(rt)
         last_banks = [bank(name, [P, HALF]) for name in (A_BANKS[1], A_BANKS[2])]
         for h in range(HALVES):
             for side, cols in enumerate(sides):

@@ -45,7 +45,7 @@ def tile_list_moisture_downscaling_kernel(
     with ExitStack() as ctx:
         keep = ctx.enter_context(tc.tile_pool(name="keep", bufs=1))
         loads = ctx.enter_context(tc.tile_pool(name="loads", bufs=1))
-        ring = ctx.enter_context(tc.tile_pool(name="ring", bufs=4))
+        ring = ctx.enter_context(tc.tile_pool(name="ring", bufs=5))
         stage = ctx.enter_context(tc.tile_pool(name="stage", bufs=1))
         psum = ctx.enter_context(tc.psum_pool(name="psum", bufs=1))
 
@@ -236,8 +236,8 @@ def tile_list_moisture_downscaling_kernel(
             rsq[u] = ring.tile([P, PACK, P], F32, name="rsq")
             nc.scalar.activation(rsq[u][:], den[u][:], ACT.Abs_reciprocal_sqrt, bias=const_t[:, rt : rt + 1], scale=2.0)
 
-        def turn_num(u):
-            num_t[u] = bank(NUM_BANKS[u % 2], [P, PACK, P])
+        def turn_num(u, name):
+            num_t[u] = bank(name, [P, PACK, P])
             for t in range(PACK):
                 nc.tensor.transpose(num_t[u][:, t, :], num[u][:, t, :], ident[:])
 
@@ -254,18 +254,26 @@ def tile_list_moisture_downscaling_kernel(
                                      scale=root[:, h * PACK + t : h * PACK + t + 1])
 
         def make_z(u):
-            z_bf[u] = staged("z_bf%d" % u, [P, P, PACK], BF16, u + 2 if u + 2 < count - 3 else count + u % 3)
-            dst, src = weave(z_bf[u][:], num_t[u][:])
-            nc.vector.tensor_tensor(dst, src, weave(z_bf[u][:], factor[u][:])[1], ALU.mult)
+            rt, h = units[u]
+            if h == 0:
+                z_bf[rt] = staged("z_bf%d" % rt, [P, HALVES * P, PACK], BF16, u + LAG if u + LAG < count - LAG else count + rt % 2)
+                z_w[rt] = held("z_w%d" % rt, [P, HALVES * P], U32)
+                z_s[rt] = held("z_s%d" % rt, [P, HALVES * P], U8)
+            grouped = z_bf[rt][:, h * P : (h + 1) * P, :]
+            dst, src = weave(grouped, num_t[u][:])
+            nc.vector.tensor_tensor(dst, src, weave(grouped, factor[u][:])[1], ALU.mult)
 
         def quantize_z(u):
-            z_w[u] = held("z_w%d" % u, [P, P], U32)
-            z_s[u] = held("z_s%d" % u, [P, P], U8)
-            quantize(z_w[u][:], z_s[u][:], z_bf[u][:])
+            rt, h = units[u]
+            if rt == R_TILES - 1:
+                cols = slice(h * P, (h + 1) * P)
+                quantize(z_w[rt][:, cols], z_s[rt][:, cols], z_bf[rt][:, cols, :])
+            elif h == HALVES - 1:
+                quantize(z_w[rt][:], z_s[rt][:], z_bf[rt][:])
 
         def out_pass(acc, rt, h, cols):
-            u = units.index((rt, h))
-            nc.tensor.matmul_mx(acc, lhsT=z_w[u][:].bitcast(FP8X4), lhsT_scale=z_s[u][:],
+            nc.tensor.matmul_mx(acc, lhsT=z_w[rt][:, h * P : (h + 1) * P].bitcast(FP8X4),
+                                lhsT_scale=z_s[rt][:, h * P : (h + 1) * P],
                                 rhs=grid_w[h][:, cols].bitcast(FP8X4), rhs_scale=grid_s[h][:, cols],
                                 start=(h == 0), stop=(h == HALVES - 1))
 
@@ -275,8 +283,8 @@ def tile_list_moisture_downscaling_kernel(
 
         out_bank = {}
 
-        def make_out(rt):
-            out_bank[rt] = bank((OUT_BANK, OUT_BANK, A_BANKS[0], ROOT_BANKS[0], OUT_BANK)[rt], [P, F])
+        def make_out(rt, name):
+            out_bank[rt] = bank(name, [P, F])
             for h in range(HALVES):
                 out_pass(out_bank[rt][:], rt, h, slice(0, F))
 
@@ -290,61 +298,80 @@ def tile_list_moisture_downscaling_kernel(
         w3_pieces = [(w3_raw[c][:], w3_codes(c), w3_s[c][:]) for c in range(1, len(w3_cols))]
         pieces = w3_pieces + grid_pieces
         rounded = {}
-        rounded_at = {1: 1, 2: 2, 4: 3, 5: 4, 7: 5, 8: 6}
-        on_vector = ()
+        rounded_at = {1: 1, 2: 2, 3: 3, 5: 4, 6: 5, 7: 6}
 
-        def round_piece(k, name):
+        def round_piece(k, name, step):
             raw = pieces[k][0]
-            rounded[k] = held(name, [P, raw.shape[2], PACK], BF16)
-            (nc.vector.tensor_copy if k in on_vector else nc.scalar.copy)(*weave(rounded[k][:], raw))
+            shape = [P, raw.shape[2], PACK]
+            rounded[k] = held(name, shape, BF16) if step < LAG else staged(name, shape, BF16, step - LAG)
+            nc.scalar.copy(*weave(rounded[k][:], raw))
 
         def quantize_piece(k):
             quantize(pieces[k][1], pieces[k][2], rounded[k][:])
 
-        out_made_at = {9: [0], 10: [1], 11: [2], 12: [3, 4]}
-        out_stored_at = {10: [0], 11: [1], 13: [2, 3, 4]}
         sides = [slice(0, F // 2), slice(F // 2, F)]
+        last, steady = count - 1, count - 2
 
         make_a(0)
         make_a(1)
-        round_piece(0, "w3_second")
-        for i in range(count + LAG):
-            if 1 <= i <= count:
+        round_piece(0, "w3_second", 0)
+        for i in range(steady):
+            if i >= 1:
                 make_root(i - 1)
-            if 2 <= i < count + 2:
+            if i >= 2:
                 make_factor(i - 2)
-            if i < count:
-                make_num(i)
-            if i == count - 1:
-                quantize_z(i - 1 - LAG)
-                make_den(i)
+            make_num(i)
             if i >= LAG:
                 make_z(i - LAG)
-            if 2 <= i <= count:
-                turn_num(i - 2)
-            if i == count:
-                turn_num(count - 1)
-            if 1 <= i <= count:
+            if i >= 2:
+                turn_num(i - 2, NUM_BANKS[i % 2])
+            if i >= 1:
                 turn_root(i - 1)
-            if rounded_at.get(i) not in on_vector + (None,):
-                round_piece(rounded_at[i], "half_b%d" % i)
-            for rt in out_stored_at.get(i, []):
-                store_out(rt)
-            if i < count - 1:
-                make_den(i)
-            if i >= LAG and i != count - 2:
+            if i in rounded_at:
+                round_piece(rounded_at[i], ("half_b%d" if i < LAG else "rounded%d") % i, i)
+            if i == steady - 1:
+                store_out(0)
+            make_den(i)
+            if i >= LAG:
                 quantize_z(i - LAG)
             if i == 0:
                 quantize_piece(0)
             if i - 1 in rounded_at:
                 quantize_piece(rounded_at[i - 1])
-            if rounded_at.get(i) in on_vector:
-                round_piece(rounded_at[i], "half_b%d" % i)
-            if i + 2 < count:
+            if i + 2 < last:
                 make_a(i + 2)
-            for rt in out_made_at.get(i, []):
-                make_out(rt)
-        last_banks = [bank(name, [P, HALF]) for name in (A_BANKS[1], A_BANKS[2])]
+            if i + 3 == last:
+                make_a(last)
+            if i >= steady - 2:
+                make_out(i - (steady - 2), OUT_BANK)
+
+        make_root(last - 2)
+        make_factor(last - 3)
+        make_num(last - 1)
+        make_num(last)
+        turn_num(last - 3, NUM_BANKS[0])
+        turn_root(last - 2)
+        turn_num(last - 2, A_BANKS[0])
+        make_factor(last - 2)
+        for u in (last - 1, last):
+            make_den(u)
+        for u in (last - 1, last):
+            make_root(u)
+            turn_root(u)
+        for u in (last - 1, last):
+            turn_num(u, A_BANKS[u % len(A_BANKS)])
+        store_out(1)
+        for u in (last - 1, last):
+            make_factor(u)
+        for u in range(last - 4, count):
+            make_z(u)
+            if u != last - 4:
+                quantize_z(u - 1)
+        quantize_z(last)
+        for rt, name in ((2, NUM_BANKS[1]), (3, NUM_BANKS[0]), (4, OUT_BANK)):
+            make_out(rt, name)
+            store_out(rt)
+        last_banks = [bank(name, [P, HALF]) for name in (A_BANKS[0], ROOT_BANKS[0])]
         for h in range(HALVES):
             for side, cols in enumerate(sides):
                 out_pass(last_banks[side][:, 0 : F // 2], R_TILES - 1, h, cols)

@@ -78,16 +78,16 @@ def tile_list_moisture_downscaling_kernel(
         w3_raw = [placed("w3_raw%d" % c, [P, PACK, cols.stop - cols.start], F32, w3_at[c]) for c, cols in enumerate(w3_cols)]
         grid_raw = [placed("grid_raw%d" % h, [P, PACK, F], F32, TAB0 + 64 + T + h * 2 * T) for h in range(HALVES)]
         v2_w = [placed("v2_w%d" % h, [P, HALF], U16, WIN2 + h * 1024) for h in range(HALVES)]
-        w1_s = placed("w1_s", [P, 2, H], U8, WIN2 + 2048)
-        lifted_s = placed("lifted_s", [P, S], U8, WIN2 + 3584)
+        w1_s = held("w1_s", [P, 2, H], U8)
+        lifted_s = held("lifted_s", [P, S], U8)
         picked_s = placed("picked_s", [P, S], U8, TAB2)
         const_rows = held("const_rows", [P, P], F32)
         const_t = held("const_t", [P, R_TILES], F32)
         v0_w = placed("v0_w", [P, S], U32, WIN - 3072)
-        trust_t = placed("trust_t", [P, HALVES * PACK], F32, TAB0)
-        rough = placed("rough", [P, HALVES * PACK], F32, W3A)
-        defect = placed("defect", [P, HALVES * PACK], F32, W1A)
-        root0 = placed("root0", [P, HALVES * PACK], F32, TAB1)
+        trust_t = held("trust_t", [P, HALVES * PACK], F32)
+        rough = held("rough", [P, HALVES * PACK], F32)
+        defect = held("defect", [P, HALVES * PACK], F32)
+        root0 = held("root0", [P, HALVES * PACK], F32)
         root = held("root", [P, HALVES * PACK], F32)
         v2_s = held("v2_s", [P, S], U8)
         w1_rows = w1_words.rearrange("a p c -> p a c").bitcast(I32)
@@ -113,17 +113,23 @@ def tile_list_moisture_downscaling_kernel(
         for scale_tile in (tab_s, tab2_s, w2_s):
             nc.vector.memset(scale_tile[:].bitcast(I32), 0)
         nc.vector.memset(const_rows[0 : P - R_TILES, :], 0.0)
-        for r in range(4):
-            nc.gpsimd.dma_start(tab_s[r:P:PASS1_ROW, :].bitcast(I32),
-                                tab_scales.rearrange("a (q r) t -> r q a t", r=4)[r].bitcast(I32))
+        for scale_tile in (w1_s[:].rearrange("p a c -> p (a c)"), lifted_s[:]):
+            nc.vector.memset(scale_tile.bitcast(I32), 0)
+
+        def load_tab_scales(queue, r):
+            queue.dma_start(tab_s[r:P:PASS1_ROW, :].bitcast(I32),
+                            tab_scales.rearrange("a (q r) t -> r q a t", r=4)[r].bitcast(I32))
+
+        for r in range(3):
+            load_tab_scales(nc.gpsimd, r)
+        nc.gpsimd.dma_start(const_rows[P - R_TILES : P, :], const.rearrange("(t p) -> t p", p=P))
 
         nc.sync.dma_start(list2[:], offs2)
         nc.sync.dma_start(list1[:], offs)
         nc.sync.dma_start(trust_t[:].rearrange("p (h t) -> p h t", t=PACK),
                           trust.rearrange("(h p t) -> p h t", h=HALVES, t=PACK))
         nc.sync.dma_start(tab2_w[:].bitcast(I32), tab2_words[0].bitcast(I32))
-        nc.sync.dma_start(w2_w[:], w2_words[0].rearrange("p c i -> p (c i)").bitcast(I32))
-        nc.sync.dma_start(const_rows[P - R_TILES : P, :], const.rearrange("(t p) -> t p", p=P))
+        load_tab_scales(nc.sync, 3)
         for r in range(4):
             nc.sync.dma_start(tab2_s[r:P:32, :].bitcast(I32), tab2_scales[0, r:SCALE_ROWS:4, :].bitcast(I32))
 
@@ -134,18 +140,17 @@ def tile_list_moisture_downscaling_kernel(
 
         for r in range(4):
             nc.sync.dma_start(w2_s[r:P:32, :].bitcast(I32), w2_scales[0, r:SCALE_ROWS:4, :].bitcast(I32))
+        nc.sync.dma_start(w2_w[:], w2_words[0].rearrange("p c i -> p (c i)").bitcast(I32))
         load_w3(0)
-        nc.sync.dma_start(w1_first[:].bitcast(I32), w1_rows[:, :, 0 : P // 2])
         load_tab(0)
         load_tab(1)
-
-        nc.vector.tensor_copy(v2_s[:], tab2_s[:].indirect(list2[:]))
-        nc.vector.tensor_copy(v2_w[0][:], tab2_w[:].indirect(half_list(list2, 0)))
-        for scale_tile in (w1_s[:].rearrange("p a c -> p (a c)"), lifted_s[:]):
-            nc.vector.memset(scale_tile.bitcast(I32), 0)
+        nc.sync.dma_start(w1_first[:].bitcast(I32), w1_rows[:, :, 0 : P // 2])
         for r in range(4):
             nc.sync.dma_start(w1_s[r:P:32, :, :].bitcast(I32),
                               w1_scales[:, r:SCALE_ROWS:4, :].rearrange("a q c -> q a c").bitcast(I32))
+
+        nc.vector.tensor_copy(v2_s[:], tab2_s[:].indirect(list2[:]))
+        nc.vector.tensor_copy(v2_w[0][:], tab2_w[:].indirect(half_list(list2, 0)))
         nc.vector.tensor_copy(v2_w[1][:], tab2_w[:].indirect(half_list(list2, 1)))
         nc.vector.tensor_copy(picked_s[:], tab_s[:].indirect(list1[:]))
         nc.sync.dma_start(lifted_s[0:LIVE_ROWS, :].bitcast(I32), picked_s[PASS1_ROW : PASS1_ROW + LIVE_ROWS, :].bitcast(I32))
@@ -181,9 +186,6 @@ def tile_list_moisture_downscaling_kernel(
         def quantize(codes, scales, grouped):
             nc.vector.quantize_mx(out=codes.bitcast(FP8X4), scales=scales, in_=grouped.rearrange("p c t -> p (c t)"))
 
-        const_turned = bank(ROOT_BANKS[0], [P, P])
-        nc.tensor.transpose(const_turned[:], const_rows[:], ident[:])
-        nc.scalar.copy(const_t[:], const_turned[:, P - R_TILES : P])
         all_banks = A_BANKS + (OUT_BANK,) + NUM_BANKS + ROOT_BANKS
         b_order = [u for h in range(HALVES) for u in range(h, count, HALVES)]
         for i, u in enumerate(b_order):
@@ -314,6 +316,9 @@ def tile_list_moisture_downscaling_kernel(
 
         make_a(0)
         make_a(1)
+        const_turned = bank(OUT_BANK, [P, P])
+        nc.tensor.transpose(const_turned[:], const_rows[:], ident[:])
+        nc.scalar.copy(const_t[:], const_turned[:, P - R_TILES : P])
         round_piece(0, "w3_second", 0)
         for i in range(steady):
             if i >= 1:

@@ -24,7 +24,6 @@ HALF = P * PACK
 HALVES = S // HALF
 R_TILES = H // P
 SCALE_ROWS = 16
-PIECE = 256
 PASS1_ROW = 16
 LAG = 3
 LIVE_ROWS = 100
@@ -45,8 +44,7 @@ def tile_list_moisture_downscaling_kernel(
     with ExitStack() as ctx:
         keep = ctx.enter_context(tc.tile_pool(name="keep", bufs=1))
         loads = ctx.enter_context(tc.tile_pool(name="loads", bufs=1))
-        ring = ctx.enter_context(tc.tile_pool(name="ring", bufs=5))
-        stage = ctx.enter_context(tc.tile_pool(name="stage", bufs=1))
+        ring = ctx.enter_context(tc.tile_pool(name="ring", bufs=1))
         psum = ctx.enter_context(tc.psum_pool(name="psum", bufs=1))
 
         def held(name, shape, dtype):
@@ -72,7 +70,7 @@ def tile_list_moisture_downscaling_kernel(
         tab2_s = placed("tab2_s", [P, T], U8, WIN2)
         w1_first = placed("w1_first", [P, 2, 2 * P], U8, W1A)
         w1_rest = placed("w1_rest", [P, 2, 2 * (H - P)], U8, WIN + 1024)
-        w3_cuts = (0, P, 2 * P, 4 * P, H)
+        w3_cuts = (0, P, 3 * P, 5 * P, H)
         w3_cols = [slice(c0, c1) for c0, c1 in zip(w3_cuts, w3_cuts[1:])]
         w3_at = (W3A, WIN + 3584, TAB0 + 64 - T, TAB0 + 64)
         w3_raw = [placed("w3_raw%d" % c, [P, PACK, cols.stop - cols.start], F32, w3_at[c]) for c, cols in enumerate(w3_cols)]
@@ -95,7 +93,7 @@ def tile_list_moisture_downscaling_kernel(
         w2_s = held("w2_s", [P, H], U8)
         w3_w = {0: held("w3_w0", [P, P], U32)}
         w3_s = [held("w3_s%d" % c, [P, cols.stop - cols.start], U8) if c != 1 else None for c, cols in enumerate(w3_cols)]
-        w3_s[1] = placed("w3_s_second", [P, P], U8, TAB1)
+        w3_s[1] = placed("w3_s_second", [P, 2 * P], U8, TAB1)
         grid_w = [held("grid_w%d" % h, [P, F], U32) for h in range(HALVES)]
         grid_s = [held("grid_s%d" % h, [P, F], U8) for h in range(HALVES)]
         ident = held("ident", [P, P], F32)
@@ -158,8 +156,12 @@ def tile_list_moisture_downscaling_kernel(
         nc.sync.dma_start(w1_rest[:].bitcast(I32), w1_rows[:, :, P // 2 : H // 2])
         v_s = [picked_s, lifted_s]
 
-        units = [(rt, h) for rt in range(R_TILES) for h in range(HALVES)]
-        count = len(units)
+        steps = [((0, 0), (0, 1))]
+        for rt in range(1, R_TILES - 1, 2):
+            steps.extend(((rt, h), (rt + 1, h)) for h in range(HALVES))
+        steps.append(((R_TILES - 1, 0), (R_TILES - 1, 1)))
+        units = [unit for step in steps for unit in step]
+        count, last = len(units), len(steps) - 1
 
         def by_slot(tile):
             return tile[:].rearrange("p (q t) -> p t q", t=PACK)
@@ -176,18 +178,11 @@ def tile_list_moisture_downscaling_kernel(
             half_b[u] = held("half_b%d" % u, [P, PACK, P], F32)
             nc.scalar.activation(half_b[u][:], by_slot(acc), ACT.Copy, scale=0.5)
 
-        def round_on_scalar(raw, name):
-            grouped = held(name, [P, raw.shape[2], PACK], BF16)
-            dst, src = weave(grouped[:], raw)
-            nc.scalar.copy(dst, src)
-            return grouped[:]
-
-
         def quantize(codes, scales, grouped):
             nc.vector.quantize_mx(out=codes.bitcast(FP8X4), scales=scales, in_=grouped.rearrange("p c t -> p (c t)"))
 
-        all_banks = A_BANKS + (OUT_BANK,) + NUM_BANKS + ROOT_BANKS
-        b_order = [u for h in range(HALVES) for u in range(h, count, HALVES)]
+        all_banks = NUM_BANKS + ROOT_BANKS + A_BANKS + (OUT_BANK,)
+        b_order = [u for h in range(HALVES) for u in range(count) if units[u][1] == h]
         for i, u in enumerate(b_order):
             make_b(u, all_banks[i % len(all_banks)])
 
@@ -204,38 +199,40 @@ def tile_list_moisture_downscaling_kernel(
             nc.vector.tensor_copy(v1_w[:, h * HALF : (h + 1) * HALF], tab_w[1][:].bitcast(U32).indirect(half_list(list1, h)))
 
         v_w = [[words[:, h * HALF : (h + 1) * HALF] for h in range(HALVES)] for words in (v0_w, v1_w)]
-        a_bank, num, den, rsq, num_t, rsq_t, factor, z_bf, z_w, z_s = ({} for i in range(10))
+        a_bank, num, den, rsq, num_t, rsq_t, factor, z_bf, z_w, z_s, rounded, out_bank = ({} for i in range(12))
+        for c in range(1, len(w3_cols)):
+            w3_w[c] = held("w3_w%d" % c, [P, w3_cols[c].stop - w3_cols[c].start], U32)
 
-        def staged(name, shape, dtype, place):
-            return stage.tile(shape, dtype, name=name, align_bytes=64, offset=place * 4 * HALF)
+        a_names = list(A_BANKS) + [OUT_BANK] + [A_BANKS[u % len(A_BANKS)] for u in range(count - 4)]
 
         def make_a(u):
             rt, h = units[u]
-            acc = bank(A_BANKS[u % len(A_BANKS)], [P, HALF])
+            acc = bank(a_names[u], [P, HALF])
             c = max(c for c, cols in enumerate(w3_cols) if cols.start <= rt * P)
             off = rt * P - w3_cols[c].start
-            nc.tensor.matmul_mx(acc[:], lhsT=w3_w[c][:, off : off + P].bitcast(FP8X4), lhsT_scale=w3_s[c][:, off : off + P],
-                                rhs=v2_w[h][:].bitcast(FP4X4), rhs_scale=v2_s[:, h * HALF : (h + 1) * HALF],
-                                start=True, stop=False)
+            pixels = slice(h * HALF, (h + 1) * HALF)
             w1_cols = w1_first[:] if rt == 0 else w1_rest[:, :, 2 * (rt - 1) * P : 2 * rt * P]
-            for a in range(2):
-                nc.tensor.matmul_mx(acc[:], lhsT=w1_cols[:, a, :].bitcast(FP4X4),
-                                    lhsT_scale=w1_s[:, a, rt * P : (rt + 1) * P],
-                                    rhs=v_w[a][h].bitcast(FP8X4), rhs_scale=v_s[a][:, h * HALF : (h + 1) * HALF],
-                                    start=False, stop=(a == 1))
+            from_tab = [(w1_cols[:, a, :].bitcast(FP4X4), w1_s[:, a, rt * P : (rt + 1) * P],
+                         v_w[a][h].bitcast(FP8X4), v_s[a][:, pixels]) for a in range(2)]
+            from_tab2 = [(w3_w[c][:, off : off + P].bitcast(FP8X4), w3_s[c][:, off : off + P],
+                          v2_w[h][:].bitcast(FP4X4), v2_s[:, pixels])]
+            passes = from_tab2 + from_tab if rt == 0 else from_tab + from_tab2
+            for k, (weights, weight_scales, moving, moving_scales) in enumerate(passes):
+                nc.tensor.matmul_mx(acc[:], lhsT=weights, lhsT_scale=weight_scales, rhs=moving, rhs_scale=moving_scales,
+                                    start=(k == 0), stop=(k == len(passes) - 1))
             a_bank[u] = acc
 
         def make_num(u):
-            num[u] = ring.tile([P, PACK, P], F32, name="num")
+            num[u] = ring.tile([P, PACK, P], F32, name="num", bufs=6)
             nc.vector.scalar_tensor_tensor(num[u][:], by_slot(a_bank[u]), 0.5, half_b[u][:], ALU.mult, ALU.subtract)
 
         def make_den(u):
-            den[u] = ring.tile([P, PACK, P], F32, name="den")
+            den[u] = held("half_b%d" % u, [P, PACK, P], F32)
             nc.vector.scalar_tensor_tensor(den[u][:], by_slot(a_bank[u]), 0.0, num[u][:], ALU.max, ALU.subtract)
 
         def make_root(u):
             rt, h = units[u]
-            rsq[u] = ring.tile([P, PACK, P], F32, name="rsq")
+            rsq[u] = ring.tile([P, PACK, P], F32, name="rsq", bufs=4)
             nc.scalar.activation(rsq[u][:], den[u][:], ACT.Abs_reciprocal_sqrt, bias=const_t[:, rt : rt + 1], scale=2.0)
 
         def turn_num(u, name):
@@ -243,47 +240,47 @@ def tile_list_moisture_downscaling_kernel(
             for t in range(PACK):
                 nc.tensor.transpose(num_t[u][:, t, :], num[u][:, t, :], ident[:])
 
-        def turn_root(u):
-            rsq_t[u] = bank(ROOT_BANKS[u % 2], [P, PACK, P])
-            for t in range(PACK):
-                nc.tensor.transpose(rsq_t[u][:, t, :], rsq[u][:, t, :], ident[:])
+        def one_half(s):
+            return steps[s][0][1] == steps[s][1][1]
 
-        def make_factor(u):
-            rt, h = units[u]
-            factor[u] = staged("factor%d" % u, [P, PACK, P], F32, u)
-            for t in range(PACK):
-                nc.scalar.activation(factor[u][:, t, :], rsq_t[u][:, t, :], ACT.Square,
-                                     scale=root[:, h * PACK + t : h * PACK + t + 1])
+        def root_blocks(s, k):
+            if one_half(s):
+                return [(e, t) for t in (2 * k, 2 * k + 1) for e in range(2)]
+            return [(k, t) for t in range(PACK)]
 
-        def make_z(u):
-            rt, h = units[u]
-            if h == 0:
-                z_bf[rt] = staged("z_bf%d" % rt, [P, HALVES * P, PACK], BF16, u + LAG if u + LAG < count - LAG else count + rt % 2)
-                z_w[rt] = held("z_w%d" % rt, [P, HALVES * P], U32)
-                z_s[rt] = held("z_s%d" % rt, [P, HALVES * P], U8)
-            grouped = z_bf[rt][:, h * P : (h + 1) * P, :]
-            dst, src = weave(grouped, num_t[u][:])
-            nc.vector.tensor_tensor(dst, src, weave(grouped, factor[u][:])[1], ALU.mult)
+        def turn_roots(s, k):
+            rsq_t[s, k] = bank(ROOT_BANKS[k], [P, PACK, P])
+            for place, (e, t) in enumerate(root_blocks(s, k)):
+                nc.tensor.transpose(rsq_t[s, k][:, place, :], rsq[2 * s + e][:, t, :], ident[:])
 
-        def quantize_z(u):
-            rt, h = units[u]
-            if rt == R_TILES - 1:
-                cols = slice(h * P, (h + 1) * P)
-                quantize(z_w[rt][:, cols], z_s[rt][:, cols], z_bf[rt][:, cols, :])
-            elif h == HALVES - 1:
-                quantize(z_w[rt][:], z_s[rt][:], z_bf[rt][:])
+        def make_factors(s, k):
+            if k == 0:
+                factor[s] = ring.tile([P, PACK, 2, P], F32, name="factor", bufs=3)
+            together = 2 if one_half(s) else 1
+            for place in range(0, PACK, together):
+                e, t = root_blocks(s, k)[place]
+                slot = steps[s][e][1] * PACK + t
+                nc.scalar.activation(factor[s][:, t, e : e + together, :], rsq_t[s, k][:, place : place + together, :],
+                                     ACT.Square, scale=root[:, slot : slot + 1])
+
+        def make_z(s, e):
+            if s not in z_bf:
+                z_bf[s] = held("z_bf%d" % s, [P, 2 * P, PACK], BF16)
+                z_w[s] = held("z_w%d" % s, [P, 2 * P], U32)
+                z_s[s] = held("z_s%d" % s, [P, 2 * P], U8)
+            grouped = z_bf[s][:, e * P : (e + 1) * P, :]
+            dst, src = weave(grouped, num_t[2 * s + e][:])
+            nc.vector.tensor_tensor(dst, src, weave(grouped, factor[s][:, :, e, :])[1], ALU.mult)
+
+        def quantize_z(s, cols):
+            quantize(z_w[s][:, cols], z_s[s][:, cols], z_bf[s][:, cols, :])
 
         def out_pass(acc, rt, h, cols):
-            nc.tensor.matmul_mx(acc, lhsT=z_w[rt][:, h * P : (h + 1) * P].bitcast(FP8X4),
-                                lhsT_scale=z_s[rt][:, h * P : (h + 1) * P],
+            s, e = divmod(units.index((rt, h)), 2)
+            nc.tensor.matmul_mx(acc, lhsT=z_w[s][:, e * P : (e + 1) * P].bitcast(FP8X4),
+                                lhsT_scale=z_s[s][:, e * P : (e + 1) * P],
                                 rhs=grid_w[h][:, cols].bitcast(FP8X4), rhs_scale=grid_s[h][:, cols],
                                 start=(h == 0), stop=(h == HALVES - 1))
-
-        def w3_codes(c):
-            w3_w[c] = held("w3_w%d" % c, [P, w3_cols[c].stop - w3_cols[c].start], U32)
-            return w3_w[c][:]
-
-        out_bank = {}
 
         def make_out(rt, name):
             out_bank[rt] = bank(name, [P, F])
@@ -291,96 +288,112 @@ def tile_list_moisture_downscaling_kernel(
                 out_pass(out_bank[rt][:], rt, h, slice(0, F))
 
         def store_out(rt):
-            result = ring.tile([P, F], F32, name="result")
+            result = ring.tile([P, F], F32, name="result", bufs=5)
             nc.scalar.copy(result[:], out_bank[rt][:])
             nc.sync.dma_start(out[rt * P : (rt + 1) * P, :], result[:])
 
-        grid_pieces = [(grid_raw[h][:, :, n0 : n0 + PIECE], grid_w[h][:, n0 : n0 + PIECE], grid_s[h][:, n0 : n0 + PIECE])
-                       for h in range(HALVES) for n0 in range(0, F, PIECE)]
-        w3_pieces = [(w3_raw[c][:], w3_codes(c), w3_s[c][:]) for c in range(1, len(w3_cols))]
-        pieces = w3_pieces + grid_pieces
-        rounded = {}
-        rounded_at = {1: 1, 2: 2, 3: 3, 5: 4, 6: 5, 7: 6}
+        def round_w3(c, name):
+            rounded["w3", c] = held(name, [P, w3_cols[c].stop - w3_cols[c].start, PACK], BF16)
+            nc.scalar.copy(*weave(rounded["w3", c][:], w3_raw[c][:]))
 
-        def round_piece(k, name, step):
-            raw = pieces[k][0]
-            shape = [P, raw.shape[2], PACK]
-            rounded[k] = held(name, shape, BF16) if step < LAG else staged(name, shape, BF16, step - LAG)
-            nc.scalar.copy(*weave(rounded[k][:], raw))
+        def round_grid(h):
+            rounded["grid", h] = held("in_turn", [P, F, PACK], BF16)
+            nc.gpsimd.tensor_scalar(rounded["grid", h][:], grid_raw[h][:].rearrange("p t c -> p c t"), 1.0, 0.0, ALU.mult, ALU.add)
 
-        def quantize_piece(k):
-            quantize(pieces[k][1], pieces[k][2], rounded[k][:])
+        def quantize_w3(c):
+            quantize(w3_w[c][:], w3_s[c][:], rounded["w3", c][:])
 
-        sides = [slice(0, F // 2), slice(F // 2, F)]
-        last, steady = count - 1, count - 2
+        def quantize_grid(h):
+            quantize(grid_w[h][:], grid_s[h][:], rounded["grid", h][:])
 
         make_a(0)
         make_a(1)
-        const_turned = bank(OUT_BANK, [P, P])
+        const_turned = bank(NUM_BANKS[0], [P, P])
         nc.tensor.transpose(const_turned[:], const_rows[:], ident[:])
         nc.scalar.copy(const_t[:], const_turned[:, P - R_TILES : P])
-        round_piece(0, "w3_second", 0)
-        for i in range(steady):
-            if i >= 1:
-                make_root(i - 1)
-            if i >= 2:
-                make_factor(i - 2)
-            make_num(i)
-            if i >= LAG:
-                make_z(i - LAG)
-            if i >= 2:
-                turn_num(i - 2, NUM_BANKS[i % 2])
-            if i >= 1:
-                turn_root(i - 1)
-            if i in rounded_at:
-                round_piece(rounded_at[i], ("half_b%d" if i < LAG else "rounded%d") % i, i)
-            if i == steady - 1:
-                store_out(0)
-            make_den(i)
-            if i >= LAG:
-                quantize_z(i - LAG)
-            if i == 0:
-                quantize_piece(0)
-            if i - 1 in rounded_at:
-                quantize_piece(rounded_at[i - 1])
-            if i + 2 < last:
-                make_a(i + 2)
-            if i + 3 == last:
-                make_a(last)
-            if i >= steady - 2:
-                make_out(i - (steady - 2), OUT_BANK)
+        round_w3(1, "w3_second")
+        outs_at = {4: (0,), 5: (1,)}
+        for s in range(last + 1):
+            early, late = 2 * s, 2 * s + 1
+            if s >= LAG:
+                make_z(s - LAG, 1)
+                make_z(s - LAG, 0)
+            if s >= 1:
+                make_root(early - 2)
+                make_root(late - 2)
+            if 1 <= s < last:
+                make_a(early + 2)
+            if s == 1:
+                make_a(late + 2)
+            for u in (early, late) if s == 0 else (late, early):
+                make_num(u)
+            if s == 0:
+                round_w3(2, "in_turn")
+            if s == 2:
+                round_w3(3, "w3_second")
+            for rt in outs_at.get(s - 1, ()):
+                store_out(rt)
+            if s >= 1:
+                for k in range(2):
+                    turn_roots(s - 1, k)
+                for k in range(2):
+                    make_factors(s - 1, k)
+            if s >= 2:
+                for e in range(2):
+                    turn_num(early - 4 + e, NUM_BANKS[e])
+            if s >= LAG:
+                quantize_z(s - LAG, slice(0, 2 * P))
+            if s < 2:
+                quantize_w3(s + 1)
+            if s in (3, 4):
+                quantize_grid(s - 3)
+            if s == 3:
+                quantize_w3(3)
+            if s in (1, 3):
+                round_grid(s // 2)
+            if s == 0:
+                make_a(2)
+                make_a(3)
+            for rt in outs_at.get(s, ()):
+                make_out(rt, OUT_BANK)
+            make_den(early)
+            if 2 <= s < last:
+                make_a(late + 2)
+            make_den(late)
 
-        make_root(last - 2)
-        make_factor(last - 3)
-        make_num(last - 1)
-        make_num(last)
-        turn_num(last - 3, NUM_BANKS[0])
-        turn_root(last - 2)
-        turn_num(last - 2, A_BANKS[0])
-        make_factor(last - 2)
-        for u in (last - 1, last):
-            make_den(u)
-        for u in (last - 1, last):
-            make_root(u)
-            turn_root(u)
-        for u in (last - 1, last):
-            turn_num(u, A_BANKS[u % len(A_BANKS)])
+        early, late = 2 * last, 2 * last + 1
+        make_root(early)
+        make_root(late)
+        for e in (1, 0):
+            make_z(last - 2, e)
+        turn_num(early - 2, a_names[early - 1])
+        for k in range(2):
+            turn_roots(last, k)
+        turn_num(late - 2, NUM_BANKS[1])
+        turn_num(early, NUM_BANKS[0])
+        turn_num(late, a_names[early])
         store_out(1)
-        for u in (last - 1, last):
-            make_factor(u)
-        for u in range(last - 4, count):
-            make_z(u)
-            if u != last - 4:
-                quantize_z(u - 1)
-        quantize_z(last)
-        for rt, name in ((2, NUM_BANKS[1]), (3, NUM_BANKS[0]), (4, OUT_BANK)):
+        for k in range(2):
+            make_factors(last, k)
+        quantize_z(last - 2, slice(0, 2 * P))
+        make_out(2, OUT_BANK)
+        store_out(2)
+        for e in range(2):
+            make_z(last - 1, e)
+        make_z(last, 0)
+        quantize_z(last - 1, slice(0, 2 * P))
+        make_z(last, 1)
+        for e in range(2):
+            quantize_z(last, slice(e * P, (e + 1) * P))
+        for rt, name in ((3, ROOT_BANKS[0]), (4, OUT_BANK)):
             make_out(rt, name)
             store_out(rt)
-        last_banks = [bank(name, [P, HALF]) for name in (A_BANKS[0], ROOT_BANKS[0])]
+        sides = [slice(0, F // 2), slice(F // 2, F)]
+        last_banks = [bank(name, [P, HALF]) for name in (a_names[early - 1], a_names[late])]
         for h in range(HALVES):
             for side, cols in enumerate(sides):
                 out_pass(last_banks[side][:, 0 : F // 2], R_TILES - 1, h, cols)
         for side, empty in enumerate((nc.scalar.copy, nc.vector.tensor_copy)):
-            part = ring.tile([P, F // 2], F32, name="part")
+            part = ring.tile([P, F // 2], F32, name="part", bufs=2)
             empty(part[:], last_banks[side][:, 0 : F // 2])
             nc.sync.dma_start(out[H - P : H, sides[side]], part[:])

@@ -24,9 +24,7 @@ HALF = P * PACK
 HALVES = S // HALF
 R_TILES = H // P
 SCALE_ROWS = 16
-PASS1_ROW = 16
 LAG = 3
-LIVE_ROWS = 100
 
 
 def weave(grouped, slots):
@@ -45,6 +43,7 @@ def tile_list_moisture_downscaling_kernel(
         keep = ctx.enter_context(tc.tile_pool(name="keep", bufs=1))
         loads = ctx.enter_context(tc.tile_pool(name="loads", bufs=1))
         ring = ctx.enter_context(tc.tile_pool(name="ring", bufs=1))
+        stage = ctx.enter_context(tc.tile_pool(name="stage", bufs=1))
         psum = ctx.enter_context(tc.psum_pool(name="psum", bufs=1))
 
         def held(name, shape, dtype):
@@ -61,100 +60,101 @@ def tile_list_moisture_downscaling_kernel(
         ROOT_BANKS = ("root0", "root1")
         OUT_BANK = "o"
 
-        TAB2, TAB0, TAB1, W3A, W1A, WIN2, WIN = 0, 4 * T, 10 * T, 14 * T, 15 * T, 17 * T, 20 * T
+        TAB1, V1 = 0, 4 * T
         list1 = held("list1", [P, S // 16], U16)
         list2 = held("list2", [P, S // 16], U16)
-        tab2_w = placed("tab2_w", [P, T], U16, TAB2)
-        tab_w = [placed("tab_w0", [P, T], I32, TAB0), placed("tab_w1", [P, T], I32, TAB1)]
-        tab_s = placed("tab_s", [P, T], U8, WIN)
-        tab2_s = placed("tab2_s", [P, T], U8, WIN2)
-        w1_first = placed("w1_first", [P, 2, 2 * P], U8, W1A)
-        w1_rest = placed("w1_rest", [P, 2, 2 * (H - P)], U8, WIN + 1024)
+        tab2_w = held("tab2_w", [P, T], U16)
+        tab_w = [held("tab_w0", [P, T], I32), placed("tab_w1", [P, T], I32, TAB1)]
+        tab_s = held("tab_s", [P, T], U8)
+        tab2_s = held("tab2_s", [P, T], U8)
+        w1_w = held("w1_w", [P, 2, 2 * H], U8)
         w3_cuts = (0, P, 3 * P, 5 * P, H)
         w3_cols = [slice(c0, c1) for c0, c1 in zip(w3_cuts, w3_cuts[1:])]
-        w3_at = (W3A, WIN + 3584, TAB0 + 64 - T, TAB0 + 64)
-        w3_raw = [placed("w3_raw%d" % c, [P, PACK, cols.stop - cols.start], F32, w3_at[c]) for c, cols in enumerate(w3_cols)]
-        grid_raw = [placed("grid_raw%d" % h, [P, PACK, F], F32, TAB0 + 64 + T + h * 2 * T) for h in range(HALVES)]
-        v2_w = [placed("v2_w%d" % h, [P, HALF], U16, WIN2 + h * 1024) for h in range(HALVES)]
+        w3_raw = [held("w3_raw%d" % c, [P, PACK, cols.stop - cols.start], F32) for c, cols in enumerate(w3_cols)]
+        grid_raw = [held("grid_raw%d" % h, [P, PACK, F], F32) for h in range(HALVES)]
+        v2_w = [held("v2_w%d" % h, [P, HALF], U16) for h in range(HALVES)]
         w1_s = held("w1_s", [P, 2, H], U8)
-        lifted_s = held("lifted_s", [P, S], U8)
-        picked_s = placed("picked_s", [P, S], U8, TAB2)
+        picked_s = held("picked_s", [P, S], U8)
+        picked2_s = held("picked2_s", [P, S], U8)
+        v_both = held("v_both", [P, 2, S], U8)
+        v_s = [v_both[:, a, :] for a in range(2)]
         const_rows = held("const_rows", [P, P], F32)
         const_t = held("const_t", [P, R_TILES], F32)
-        v0_w = placed("v0_w", [P, S], U32, WIN - 3072)
+        v0_w = held("v0_w", [P, S], U32)
         trust_t = held("trust_t", [P, HALVES * PACK], F32)
         rough = held("rough", [P, HALVES * PACK], F32)
         defect = held("defect", [P, HALVES * PACK], F32)
         root0 = held("root0", [P, HALVES * PACK], F32)
         root = held("root", [P, HALVES * PACK], F32)
         v2_s = held("v2_s", [P, S], U8)
-        w1_rows = w1_words.rearrange("a p c -> p a c").bitcast(I32)
         w2_w = held("w2_w", [P, H], I32)
         w2_s = held("w2_s", [P, H], U8)
         w3_w = {0: held("w3_w0", [P, P], U32)}
         w3_s = [held("w3_s%d" % c, [P, cols.stop - cols.start], U8) if c != 1 else None for c, cols in enumerate(w3_cols)]
         w3_s[1] = placed("w3_s_second", [P, 2 * P], U8, TAB1)
-        grid_w = [held("grid_w%d" % h, [P, F], U32) for h in range(HALVES)]
         grid_s = [held("grid_s%d" % h, [P, F], U8) for h in range(HALVES)]
         ident = held("ident", [P, P], F32)
 
         def load_w3(c):
             nc.sync.dma_start(w3_raw[c][:], w3[:, w3_cols[c]].rearrange("(p j) r -> p j r", j=PACK))
 
-        def load_tab(a):
-            nc.sync.dma_start(tab_w[a][:], tab_words[a].rearrange("p t i -> p (t i)").bitcast(I32))
+        def load_part(tile, rows, c0, c1):
+            cols = slice(c0 * rows.shape[1] // 8, c1 * rows.shape[1] // 8)
+            nc.sync.dma_start(tile[:, cols], rows[:, cols])
+
+        def lift(scale_tile, picked, first):
+            for r in range(4):
+                nc.sync.dma_start(scale_tile[r:P:32, :].bitcast(I32), picked[8 * r + first : P : 32, :].bitcast(I32))
 
         def half_list(offsets, h):
             return offsets[:, h * (HALF // 16) : (h + 1) * (HALF // 16)]
 
-        make_identity(nc, ident[:])
-        for scale_tile in (tab_s, tab2_s, w2_s):
-            nc.vector.memset(scale_tile[:].bitcast(I32), 0)
-        nc.vector.memset(const_rows[0 : P - R_TILES, :], 0.0)
-        for scale_tile in (w1_s[:].rearrange("p a c -> p (a c)"), lifted_s[:]):
+        tab_rows = [tab_words[a].rearrange("p t i -> p (t i)").bitcast(I32) for a in range(2)]
+        tab2_rows = tab2_words[0].bitcast(I32)
+
+        for scale_tile in (tab2_s[:], tab_s[:], w2_s[:], v2_s[:], w1_s[:].rearrange("p a c -> p (a c)"),
+                           v_both[:].rearrange("p a c -> p (a c)")):
             nc.vector.memset(scale_tile.bitcast(I32), 0)
 
-        def load_tab_scales(queue, r):
-            queue.dma_start(tab_s[r:P:PASS1_ROW, :].bitcast(I32),
-                            tab_scales.rearrange("a (q r) t -> r q a t", r=4)[r].bitcast(I32))
-
-        for r in range(3):
-            load_tab_scales(nc.gpsimd, r)
+        nc.gpsimd.dma_start(trust_t[:].rearrange("p (h t) -> p h t", t=PACK),
+                            trust.rearrange("(h p t) -> p h t", h=HALVES, t=PACK))
+        nc.gpsimd.memset(const_rows[0 : P - R_TILES, :], 0.0)
         nc.gpsimd.dma_start(const_rows[P - R_TILES : P, :], const.rearrange("(t p) -> t p", p=P))
+        make_identity(nc, ident[:])
 
         nc.sync.dma_start(list2[:], offs2)
+        load_part(tab2_w[:].bitcast(I32), tab2_rows, 0, 4)
+        nc.sync.dma_start(tab2_s[0:P:8, :].bitcast(I32), tab2_scales[0].bitcast(I32))
+        load_part(tab2_w[:].bitcast(I32), tab2_rows, 4, 8)
         nc.sync.dma_start(list1[:], offs)
-        nc.sync.dma_start(trust_t[:].rearrange("p (h t) -> p h t", t=PACK),
-                          trust.rearrange("(h p t) -> p h t", h=HALVES, t=PACK))
-        nc.sync.dma_start(tab2_w[:].bitcast(I32), tab2_words[0].bitcast(I32))
-        load_tab_scales(nc.sync, 3)
+        nc.sync.dma_start(tab_s[0:P:4, :].bitcast(I32), tab_scales.rearrange("a g t -> g a t").bitcast(I32))
+        load_part(tab_w[0][:], tab_rows[0], 0, 4)
         for r in range(4):
-            nc.sync.dma_start(tab2_s[r:P:32, :].bitcast(I32), tab2_scales[0, r:SCALE_ROWS:4, :].bitcast(I32))
+            nc.sync.dma_start(w2_s[r:P:32, :].bitcast(I32), w2_scales[0, r:SCALE_ROWS:4, :].bitcast(I32))
+        load_part(tab_w[0][:], tab_rows[0], 4, 8)
+        nc.sync.dma_start(w2_w[:], w2_words[0].rearrange("p c i -> p (c i)").bitcast(I32))
+
+        nc.vector.tensor_copy(picked2_s[:], tab2_s[:].indirect(list2[:]))
+        lift(v2_s, picked2_s, 0)
+        for h in range(HALVES):
+            nc.vector.tensor_copy(v2_w[h][:], tab2_w[:].indirect(half_list(list2, h)))
+        nc.vector.tensor_copy(picked_s[:], tab_s[:].indirect(list1[:]))
+        load_part(tab_w[1][:], tab_rows[1], 0, 3)
+        for r in range(4):
+            nc.sync.dma_start(w1_s[r:P:32, :, :].bitcast(I32),
+                              w1_scales[:, r:SCALE_ROWS:4, :].rearrange("a q c -> q a c").bitcast(I32))
+        load_part(tab_w[1][:], tab_rows[1], 3, 6)
+        load_w3(0)
+        lift(v_s[0], picked_s, 0)
+        load_part(tab_w[1][:], tab_rows[1], 6, 8)
+        lift(v_s[1], picked_s, 4)
+        nc.sync.dma_start(w1_w[:].bitcast(I32), w1_words.rearrange("a p c -> p a c").bitcast(I32))
+        load_w3(1)
 
         nc.scalar.activation(rough[:], trust_t[:], ACT.Abs_reciprocal_sqrt)
         nc.vector.tensor_tensor(root0[:], rough[:], trust_t[:], ALU.mult)
         nc.vector.scalar_tensor_tensor(defect[:], root0[:], -0.5 * math.sqrt(2.0), rough[:], ALU.mult, ALU.mult)
         nc.vector.scalar_tensor_tensor(root[:], defect[:], 1.5 * math.sqrt(2.0), root0[:], ALU.add, ALU.mult)
-
-        for r in range(4):
-            nc.sync.dma_start(w2_s[r:P:32, :].bitcast(I32), w2_scales[0, r:SCALE_ROWS:4, :].bitcast(I32))
-        nc.sync.dma_start(w2_w[:], w2_words[0].rearrange("p c i -> p (c i)").bitcast(I32))
-        load_w3(0)
-        load_tab(0)
-        load_tab(1)
-        nc.sync.dma_start(w1_first[:].bitcast(I32), w1_rows[:, :, 0 : P // 2])
-        for r in range(4):
-            nc.sync.dma_start(w1_s[r:P:32, :, :].bitcast(I32),
-                              w1_scales[:, r:SCALE_ROWS:4, :].rearrange("a q c -> q a c").bitcast(I32))
-
-        nc.vector.tensor_copy(v2_s[:], tab2_s[:].indirect(list2[:]))
-        nc.vector.tensor_copy(v2_w[0][:], tab2_w[:].indirect(half_list(list2, 0)))
-        nc.vector.tensor_copy(v2_w[1][:], tab2_w[:].indirect(half_list(list2, 1)))
-        nc.vector.tensor_copy(picked_s[:], tab_s[:].indirect(list1[:]))
-        nc.sync.dma_start(lifted_s[0:LIVE_ROWS, :].bitcast(I32), picked_s[PASS1_ROW : PASS1_ROW + LIVE_ROWS, :].bitcast(I32))
-        load_w3(1)
-        nc.sync.dma_start(w1_rest[:].bitcast(I32), w1_rows[:, :, P // 2 : H // 2])
-        v_s = [picked_s, lifted_s]
 
         steps = [((0, 0), (0, 1))]
         for rt in range(1, R_TILES - 1, 2):
@@ -191,17 +191,24 @@ def tile_list_moisture_downscaling_kernel(
         load_w3(3)
         for h in range(HALVES):
             nc.sync.dma_start(grid_raw[h][:], grid[h * HALF : (h + 1) * HALF, :].rearrange("(p j) n -> p j n", j=PACK))
-        w3_first = placed("w3_first", [P, P, PACK], BF16, TAB2 + 2048)
+        w3_first = placed("w3_first", [P, P, PACK], BF16, V1)
         nc.vector.tensor_copy(*weave(w3_first[:], w3_raw[0][:]))
-        v1_w = placed("v1_w", [P, S], U32, TAB2 + 2048)
+        v1_w = placed("v1_w", [P, S], U32, V1)
         quantize(w3_w[0][:], w3_s[0][:], w3_first[:])
         for h in range(HALVES):
             nc.vector.tensor_copy(v1_w[:, h * HALF : (h + 1) * HALF], tab_w[1][:].bitcast(U32).indirect(half_list(list1, h)))
 
         v_w = [[words[:, h * HALF : (h + 1) * HALF] for h in range(HALVES)] for words in (v0_w, v1_w)]
         a_bank, num, den, rsq, num_t, rsq_t, factor, z_bf, z_w, z_s, rounded, out_bank = ({} for i in range(12))
-        for c in range(1, len(w3_cols)):
+        FACTOR_BYTES = 4 * PACK * 2 * P
+
+        def staged(name, shape, dtype, offset):
+            return stage.tile(shape, dtype, name=name, align_bytes=64, offset=offset)
+
+        for c in range(1, len(w3_cols) - 1):
             w3_w[c] = held("w3_w%d" % c, [P, w3_cols[c].stop - w3_cols[c].start], U32)
+        w3_w[3] = staged("w3_last", [P, P], U32, 4 * F)
+        grid_w = [staged("grid_w%d" % h, [P, F], U32, h * FACTOR_BYTES) for h in range(HALVES)]
 
         a_names = list(A_BANKS) + [OUT_BANK] + [A_BANKS[u % len(A_BANKS)] for u in range(count - 4)]
 
@@ -211,7 +218,7 @@ def tile_list_moisture_downscaling_kernel(
             c = max(c for c, cols in enumerate(w3_cols) if cols.start <= rt * P)
             off = rt * P - w3_cols[c].start
             pixels = slice(h * HALF, (h + 1) * HALF)
-            w1_cols = w1_first[:] if rt == 0 else w1_rest[:, :, 2 * (rt - 1) * P : 2 * rt * P]
+            w1_cols = w1_w[:, :, 2 * rt * P : 2 * (rt + 1) * P]
             from_tab = [(w1_cols[:, a, :].bitcast(FP4X4), w1_s[:, a, rt * P : (rt + 1) * P],
                          v_w[a][h].bitcast(FP8X4), v_s[a][:, pixels]) for a in range(2)]
             from_tab2 = [(w3_w[c][:, off : off + P].bitcast(FP8X4), w3_s[c][:, off : off + P],
@@ -255,7 +262,7 @@ def tile_list_moisture_downscaling_kernel(
 
         def make_factors(s, k):
             if k == 0:
-                factor[s] = ring.tile([P, PACK, 2, P], F32, name="factor", bufs=3)
+                factor[s] = staged("factor%d" % s, [P, PACK, 2, P], F32, (s if s < 2 else 2 + s % 3) * FACTOR_BYTES)
             together = 2 if one_half(s) else 1
             for place in range(0, PACK, together):
                 e, t = root_blocks(s, k)[place]
@@ -345,10 +352,10 @@ def tile_list_moisture_downscaling_kernel(
                 quantize_z(s - LAG, slice(0, 2 * P))
             if s < 2:
                 quantize_w3(s + 1)
-            if s in (3, 4):
-                quantize_grid(s - 3)
             if s == 3:
                 quantize_w3(3)
+            if s in (3, 4):
+                quantize_grid(s - 3)
             if s in (1, 3):
                 round_grid(s // 2)
             if s == 0:

@@ -210,7 +210,12 @@ def tile_list_moisture_downscaling_kernel(
         w3_w[3] = staged("w3_last", [P, P], U32, 4 * F)
         grid_w = [staged("grid_w%d" % h, [P, F], U32, h * FACTOR_BYTES) for h in range(HALVES)]
 
-        a_names = list(A_BANKS) + [OUT_BANK] + [A_BANKS[u % len(A_BANKS)] for u in range(count - 4)]
+        a_names = [A_BANKS[0], A_BANKS[1], A_BANKS[2], OUT_BANK, A_BANKS[0], A_BANKS[1], OUT_BANK, A_BANKS[0]]
+        num_names = list(NUM_BANKS)
+        for s in range(LAG, last + 1):
+            num_names.extend((a_names[2 * s - 1], num_names[2 * (s - LAG) + 1]))
+            a_names.extend((num_names[2 * (s - LAG)], a_names[2 * s]))
+        out_name = A_BANKS[2]
 
         def make_a(u):
             rt, h = units[u]
@@ -328,9 +333,8 @@ def tile_list_moisture_downscaling_kernel(
             if s >= 1:
                 make_root(early - 2)
                 make_root(late - 2)
-            if 1 <= s < last:
-                make_a(early + 2)
             if s == 1:
+                make_a(early + 2)
                 make_a(late + 2)
             for u in (early, late) if s == 0 else (late, early):
                 make_num(u)
@@ -345,9 +349,11 @@ def tile_list_moisture_downscaling_kernel(
                     turn_roots(s - 1, k)
                 for k in range(2):
                     make_factors(s - 1, k)
+            if 2 <= s < last:
+                make_a(early + 2)
             if s >= 2:
-                for e in range(2):
-                    turn_num(early - 4 + e, NUM_BANKS[e])
+                for u in (early - 4, late - 4):
+                    turn_num(u, num_names[u])
             if s >= LAG:
                 quantize_z(s - LAG, slice(0, 2 * P))
             if s < 2:
@@ -362,7 +368,7 @@ def tile_list_moisture_downscaling_kernel(
                 make_a(2)
                 make_a(3)
             for rt in outs_at.get(s, ()):
-                make_out(rt, OUT_BANK)
+                make_out(rt, out_name)
             make_den(early)
             if 2 <= s < last:
                 make_a(late + 2)
@@ -373,17 +379,18 @@ def tile_list_moisture_downscaling_kernel(
         make_root(late)
         for e in (1, 0):
             make_z(last - 2, e)
-        turn_num(early - 2, a_names[early - 1])
+        free_names = a_names[count:]
+        for e in range(2):
+            turn_num(early - 2 + e, free_names[e])
         for k in range(2):
             turn_roots(last, k)
-        turn_num(late - 2, NUM_BANKS[1])
-        turn_num(early, NUM_BANKS[0])
-        turn_num(late, a_names[early])
+        turn_num(early, a_names[late])
+        turn_num(late, num_names[late - 4])
         store_out(1)
         for k in range(2):
             make_factors(last, k)
         quantize_z(last - 2, slice(0, 2 * P))
-        make_out(2, OUT_BANK)
+        make_out(2, out_name)
         store_out(2)
         for e in range(2):
             make_z(last - 1, e)
@@ -392,11 +399,11 @@ def tile_list_moisture_downscaling_kernel(
         make_z(last, 1)
         for e in range(2):
             quantize_z(last, slice(e * P, (e + 1) * P))
-        for rt, name in ((3, ROOT_BANKS[0]), (4, OUT_BANK)):
+        for rt, name in ((3, ROOT_BANKS[0]), (4, num_names[early - 4])):
             make_out(rt, name)
             store_out(rt)
         sides = [slice(0, F // 2), slice(F // 2, F)]
-        last_banks = [bank(name, [P, HALF]) for name in (a_names[early - 1], a_names[late])]
+        last_banks = [bank(name, [P, HALF]) for name in free_names]
         for h in range(HALVES):
             for side, cols in enumerate(sides):
                 out_pass(last_banks[side][:, 0 : F // 2], R_TILES - 1, h, cols)

@@ -67,7 +67,9 @@ def tile_list_moisture_downscaling_kernel(
         tab_w = [held("tab_w0", [P, T], I32), placed("tab_w1", [P, T], I32, TAB1)]
         tab_s = held("tab_s", [P, T], U8)
         tab2_s = held("tab2_s", [P, T], U8)
-        w1_w = held("w1_w", [P, 2, 2 * H], U8)
+        w1_near = [held("w1_near%d" % a, [P, H], U8) for a in range(2)]
+        w1_far = held("w1_far", [P, 2, H], U8)
+        w1_rows = w1_words.rearrange("a p c -> p a c").bitcast(I32)
         w3_cuts = (0, P, 3 * P, 5 * P, H)
         w3_cols = [slice(c0, c1) for c0, c1 in zip(w3_cuts, w3_cuts[1:])]
         w3_raw = [held("w3_raw%d" % c, [P, PACK, cols.stop - cols.start], F32) for c, cols in enumerate(w3_cols)]
@@ -98,6 +100,9 @@ def tile_list_moisture_downscaling_kernel(
         def load_w3(c):
             nc.sync.dma_start(w3_raw[c][:], w3[:, w3_cols[c]].rearrange("(p j) r -> p j r", j=PACK))
 
+        def load_grid(h):
+            nc.sync.dma_start(grid_raw[h][:], grid[h * HALF : (h + 1) * HALF, :].rearrange("(p j) n -> p j n", j=PACK))
+
         def load_part(tile, rows, c0, c1):
             cols = slice(c0 * rows.shape[1] // 8, c1 * rows.shape[1] // 8)
             nc.sync.dma_start(tile[:, cols], rows[:, cols])
@@ -112,14 +117,14 @@ def tile_list_moisture_downscaling_kernel(
         tab_rows = [tab_words[a].rearrange("p t i -> p (t i)").bitcast(I32) for a in range(2)]
         tab2_rows = tab2_words[0].bitcast(I32)
 
-        for scale_tile in (tab2_s[:], tab_s[:], w2_s[:], v2_s[:], w1_s[:].rearrange("p a c -> p (a c)"),
-                           v_both[:].rearrange("p a c -> p (a c)")):
+        for scale_tile in (tab2_s[:], tab_s[:], w2_s[:], v2_s[:], v_both[:].rearrange("p a c -> p (a c)")):
             nc.vector.memset(scale_tile.bitcast(I32), 0)
 
-        nc.gpsimd.dma_start(trust_t[:].rearrange("p (h t) -> p h t", t=PACK),
-                            trust.rearrange("(h p t) -> p h t", h=HALVES, t=PACK))
+        nc.gpsimd.memset(w1_s[:].rearrange("p a c -> p (a c)").bitcast(I32), 0)
+        for r in range(4):
+            nc.gpsimd.dma_start(w1_s[r:P:32, :, :].bitcast(I32),
+                                w1_scales[:, r:SCALE_ROWS:4, :].rearrange("a q c -> q a c").bitcast(I32))
         nc.gpsimd.memset(const_rows[0 : P - R_TILES, :], 0.0)
-        nc.gpsimd.dma_start(const_rows[P - R_TILES : P, :], const.rearrange("(t p) -> t p", p=P))
         make_identity(nc, ident[:])
 
         nc.sync.dma_start(list2[:], offs2)
@@ -128,6 +133,8 @@ def tile_list_moisture_downscaling_kernel(
         load_part(tab2_w[:].bitcast(I32), tab2_rows, 4, 8)
         nc.sync.dma_start(list1[:], offs)
         nc.sync.dma_start(tab_s[0:P:4, :].bitcast(I32), tab_scales.rearrange("a g t -> g a t").bitcast(I32))
+        nc.sync.dma_start(trust_t[:].rearrange("p (h t) -> p h t", t=PACK),
+                          trust.rearrange("(h p t) -> p h t", h=HALVES, t=PACK))
         load_part(tab_w[0][:], tab_rows[0], 0, 4)
         for r in range(4):
             nc.sync.dma_start(w2_s[r:P:32, :].bitcast(I32), w2_scales[0, r:SCALE_ROWS:4, :].bitcast(I32))
@@ -139,16 +146,14 @@ def tile_list_moisture_downscaling_kernel(
         for h in range(HALVES):
             nc.vector.tensor_copy(v2_w[h][:], tab2_w[:].indirect(half_list(list2, h)))
         nc.vector.tensor_copy(picked_s[:], tab_s[:].indirect(list1[:]))
-        load_part(tab_w[1][:], tab_rows[1], 0, 3)
-        for r in range(4):
-            nc.sync.dma_start(w1_s[r:P:32, :, :].bitcast(I32),
-                              w1_scales[:, r:SCALE_ROWS:4, :].rearrange("a q c -> q a c").bitcast(I32))
-        load_part(tab_w[1][:], tab_rows[1], 3, 6)
+        load_part(tab_w[1][:], tab_rows[1], 0, 4)
         load_w3(0)
+        nc.sync.dma_start(w1_near[0][:].bitcast(I32), w1_rows[:, 0, 0 : H // 4])
         lift(v_s[0], picked_s, 0)
-        load_part(tab_w[1][:], tab_rows[1], 6, 8)
+        load_part(tab_w[1][:], tab_rows[1], 4, 8)
+        nc.sync.dma_start(w1_near[1][:].bitcast(I32), w1_rows[:, 1, 0 : H // 4])
         lift(v_s[1], picked_s, 4)
-        nc.sync.dma_start(w1_w[:].bitcast(I32), w1_words.rearrange("a p c -> p a c").bitcast(I32))
+        nc.sync.dma_start(const_rows[P - R_TILES : P, :], const.rearrange("(t p) -> t p", p=P))
         load_w3(1)
 
         nc.scalar.activation(rough[:], trust_t[:], ACT.Abs_reciprocal_sqrt)
@@ -181,16 +186,17 @@ def tile_list_moisture_downscaling_kernel(
         def quantize(codes, scales, grouped):
             nc.vector.quantize_mx(out=codes.bitcast(FP8X4), scales=scales, in_=grouped.rearrange("p c t -> p (c t)"))
 
-        all_banks = NUM_BANKS + ROOT_BANKS + A_BANKS + (OUT_BANK,)
+        b_names = ROOT_BANKS + NUM_BANKS + A_BANKS + (OUT_BANK,) + ROOT_BANKS + NUM_BANKS
         b_order = [u for h in range(HALVES) for u in range(count) if units[u][1] == h]
         for i, u in enumerate(b_order):
-            make_b(u, all_banks[i % len(all_banks)])
+            make_b(u, b_names[i])
 
         nc.vector.tensor_copy(v0_w[:], tab_w[0][:].bitcast(U32).indirect(list1[:]))
         load_w3(2)
+        load_grid(0)
+        nc.sync.dma_start(w1_far[:].bitcast(I32), w1_rows[:, :, H // 4 : H // 2])
         load_w3(3)
-        for h in range(HALVES):
-            nc.sync.dma_start(grid_raw[h][:], grid[h * HALF : (h + 1) * HALF, :].rearrange("(p j) n -> p j n", j=PACK))
+        load_grid(1)
         w3_first = placed("w3_first", [P, P, PACK], BF16, V1)
         nc.vector.tensor_copy(*weave(w3_first[:], w3_raw[0][:]))
         v1_w = placed("v1_w", [P, S], U32, V1)
@@ -210,8 +216,8 @@ def tile_list_moisture_downscaling_kernel(
         w3_w[3] = staged("w3_last", [P, P], U32, 4 * F)
         grid_w = [staged("grid_w%d" % h, [P, F], U32, h * FACTOR_BYTES) for h in range(HALVES)]
 
-        a_names = [A_BANKS[0], A_BANKS[1], A_BANKS[2], OUT_BANK, A_BANKS[0], A_BANKS[1], OUT_BANK, A_BANKS[0]]
-        num_names = list(NUM_BANKS)
+        a_names = list(A_BANKS) + [OUT_BANK] + list(NUM_BANKS) + [OUT_BANK, NUM_BANKS[0]]
+        num_names = list(A_BANKS[0:2])
         for s in range(LAG, last + 1):
             num_names.extend((a_names[2 * s - 1], num_names[2 * (s - LAG) + 1]))
             a_names.extend((num_names[2 * (s - LAG)], a_names[2 * s]))
@@ -223,8 +229,9 @@ def tile_list_moisture_downscaling_kernel(
             c = max(c for c, cols in enumerate(w3_cols) if cols.start <= rt * P)
             off = rt * P - w3_cols[c].start
             pixels = slice(h * HALF, (h + 1) * HALF)
-            w1_cols = w1_w[:, :, 2 * rt * P : 2 * (rt + 1) * P]
-            from_tab = [(w1_cols[:, a, :].bitcast(FP4X4), w1_s[:, a, rt * P : (rt + 1) * P],
+            near, first = rt < R_TILES // 2, 2 * (rt % (R_TILES // 2)) * P
+            w1_cols = [(w1_near[a][:] if near else w1_far[:, a, :])[:, first : first + 2 * P] for a in range(2)]
+            from_tab = [(w1_cols[a].bitcast(FP4X4), w1_s[:, a, rt * P : (rt + 1) * P],
                          v_w[a][h].bitcast(FP8X4), v_s[a][:, pixels]) for a in range(2)]
             from_tab2 = [(w3_w[c][:, off : off + P].bitcast(FP8X4), w3_s[c][:, off : off + P],
                           v2_w[h][:].bitcast(FP4X4), v2_s[:, pixels])]
@@ -310,7 +317,11 @@ def tile_list_moisture_downscaling_kernel(
 
         def round_grid(h):
             rounded["grid", h] = held("in_turn", [P, F, PACK], BF16)
-            nc.gpsimd.tensor_scalar(rounded["grid", h][:], grid_raw[h][:].rearrange("p t c -> p c t"), 1.0, 0.0, ALU.mult, ALU.add)
+            shared = F if h == 0 else F // 2
+            nc.gpsimd.tensor_scalar(rounded["grid", h][:, 0:shared, :], grid_raw[h][:, :, 0:shared].rearrange("p t c -> p c t"),
+                                    1.0, 0.0, ALU.mult, ALU.add)
+            if shared < F:
+                nc.scalar.copy(*weave(rounded["grid", h][:, shared:F, :], grid_raw[h][:, :, shared:F]))
 
         def quantize_w3(c):
             quantize(w3_w[c][:], w3_s[c][:], rounded["w3", c][:])
@@ -320,7 +331,7 @@ def tile_list_moisture_downscaling_kernel(
 
         make_a(0)
         make_a(1)
-        const_turned = bank(NUM_BANKS[0], [P, P])
+        const_turned = bank(ROOT_BANKS[0], [P, P])
         nc.tensor.transpose(const_turned[:], const_rows[:], ident[:])
         nc.scalar.copy(const_t[:], const_turned[:, P - R_TILES : P])
         round_w3(1, "w3_second")
@@ -351,25 +362,26 @@ def tile_list_moisture_downscaling_kernel(
                     make_factors(s - 1, k)
             if 2 <= s < last:
                 make_a(early + 2)
-            if s >= 2:
-                for u in (early - 4, late - 4):
+            if s == 1 or s >= LAG:
+                for u in (0, 1) if s == 1 else (early - 4, late - 4):
                     turn_num(u, num_names[u])
             if s >= LAG:
                 quantize_z(s - LAG, slice(0, 2 * P))
-            if s < 2:
-                quantize_w3(s + 1)
+            if s == 1:
+                quantize_w3(2)
             if s == 3:
                 quantize_w3(3)
             if s in (3, 4):
                 quantize_grid(s - 3)
             if s in (1, 3):
                 round_grid(s // 2)
-            if s == 0:
-                make_a(2)
-                make_a(3)
             for rt in outs_at.get(s, ()):
                 make_out(rt, out_name)
             make_den(early)
+            if s == 0:
+                quantize_w3(1)
+                make_a(2)
+                make_a(3)
             if 2 <= s < last:
                 make_a(late + 2)
             make_den(late)

@@ -120,12 +120,12 @@ def tile_list_moisture_downscaling_kernel(
         for scale_tile in (tab2_s[:], tab_s[:], w2_s[:], v2_s[:], v_both[:].rearrange("p a c -> p (a c)")):
             nc.vector.memset(scale_tile.bitcast(I32), 0)
 
+        nc.vector.memset(const_rows[0 : P - R_TILES, :], 0.0)
+        make_identity(nc, ident[:])
         nc.gpsimd.memset(w1_s[:].rearrange("p a c -> p (a c)").bitcast(I32), 0)
         for r in range(4):
             nc.gpsimd.dma_start(w1_s[r:P:32, :, :].bitcast(I32),
                                 w1_scales[:, r:SCALE_ROWS:4, :].rearrange("a q c -> q a c").bitcast(I32))
-        nc.gpsimd.memset(const_rows[0 : P - R_TILES, :], 0.0)
-        make_identity(nc, ident[:])
 
         nc.sync.dma_start(list2[:], offs2)
         load_part(tab2_w[:].bitcast(I32), tab2_rows, 0, 4)
@@ -315,19 +315,13 @@ def tile_list_moisture_downscaling_kernel(
             rounded["w3", c] = held(name, [P, w3_cols[c].stop - w3_cols[c].start, PACK], BF16)
             nc.scalar.copy(*weave(rounded["w3", c][:], w3_raw[c][:]))
 
-        def round_grid(h):
-            rounded["grid", h] = held("in_turn", [P, F, PACK], BF16)
-            shared = F if h == 0 else F // 2
-            nc.gpsimd.tensor_scalar(rounded["grid", h][:, 0:shared, :], grid_raw[h][:, :, 0:shared].rearrange("p t c -> p c t"),
-                                    1.0, 0.0, ALU.mult, ALU.add)
-            if shared < F:
-                nc.scalar.copy(*weave(rounded["grid", h][:, shared:F, :], grid_raw[h][:, :, shared:F]))
+        def round_on_gpsimd(grouped, raw):
+            nc.gpsimd.tensor_scalar(grouped, raw.rearrange("p t c -> p c t"), 1.0, 0.0, ALU.mult, ALU.add)
+
+        sides = [slice(0, F // 2), slice(F // 2, F)]
 
         def quantize_w3(c):
             quantize(w3_w[c][:], w3_s[c][:], rounded["w3", c][:])
-
-        def quantize_grid(h):
-            quantize(grid_w[h][:], grid_s[h][:], rounded["grid", h][:])
 
         make_a(0)
         make_a(1)
@@ -351,8 +345,11 @@ def tile_list_moisture_downscaling_kernel(
                 make_num(u)
             if s == 0:
                 round_w3(2, "in_turn")
-            if s == 2:
+            if s == 1:
                 round_w3(3, "w3_second")
+            if s == 2:
+                second_half = [held("grid_left", [P, F // 2, PACK], BF16)]
+                nc.scalar.copy(*weave(second_half[0][:], grid_raw[1][:, :, sides[0]]))
             for rt in outs_at.get(s - 1, ()):
                 store_out(rt)
             if s >= 1:
@@ -371,10 +368,16 @@ def tile_list_moisture_downscaling_kernel(
                 quantize_w3(2)
             if s == 3:
                 quantize_w3(3)
-            if s in (3, 4):
-                quantize_grid(s - 3)
-            if s in (1, 3):
-                round_grid(s // 2)
+            if s == 1:
+                first_half = held("in_turn", [P, F, PACK], BF16)
+                round_on_gpsimd(first_half[:], grid_raw[0][:])
+            if s == 3:
+                quantize(grid_w[0][:], grid_s[0][:], first_half[:])
+                second_half.append(held("in_turn", [P, F // 2, PACK], BF16))
+                round_on_gpsimd(second_half[1][:], grid_raw[1][:, :, sides[1]])
+            if s == 4:
+                for grouped, cols in zip(second_half, sides):
+                    quantize(grid_w[1][:, cols], grid_s[1][:, cols], grouped[:])
             for rt in outs_at.get(s, ()):
                 make_out(rt, out_name)
             make_den(early)
@@ -414,7 +417,6 @@ def tile_list_moisture_downscaling_kernel(
         for rt, name in ((3, ROOT_BANKS[0]), (4, num_names[early - 4])):
             make_out(rt, name)
             store_out(rt)
-        sides = [slice(0, F // 2), slice(F // 2, F)]
         last_banks = [bank(name, [P, HALF]) for name in free_names]
         for h in range(HALVES):
             for side, cols in enumerate(sides):

@@ -23,6 +23,7 @@ PACK = 4
 HALF = P * PACK
 HALVES = S // HALF
 R_TILES = H // P
+SHARED = 4
 SCALE_ROWS = 16
 LAG = 3
 
@@ -205,7 +206,7 @@ def tile_list_moisture_downscaling_kernel(
             nc.vector.tensor_copy(v1_w[:, h * HALF : (h + 1) * HALF], tab_w[1][:].bitcast(U32).indirect(half_list(list1, h)))
 
         v_w = [[words[:, h * HALF : (h + 1) * HALF] for h in range(HALVES)] for words in (v0_w, v1_w)]
-        a_bank, num, den, rsq, num_t, rsq_t, factor, z_bf, z_w, z_s, rounded, out_bank = ({} for i in range(12))
+        a_bank, num, den, rsq, num_t, rsq_t, factor, z_bf, z_w, z_s, rounded, out_bank, positive = ({} for i in range(13))
         FACTOR_BYTES = 4 * PACK * 2 * P
 
         def staged(name, shape, dtype, offset):
@@ -216,11 +217,11 @@ def tile_list_moisture_downscaling_kernel(
         w3_w[3] = staged("w3_last", [P, P], U32, 4 * F)
         grid_w = [staged("grid_w%d" % h, [P, F], U32, h * FACTOR_BYTES) for h in range(HALVES)]
 
-        a_names = list(A_BANKS) + [OUT_BANK] + list(NUM_BANKS) + [OUT_BANK, NUM_BANKS[0]]
+        a_names = list(A_BANKS) + [OUT_BANK] + list(NUM_BANKS) + [OUT_BANK, NUM_BANKS[1]]
         num_names = list(A_BANKS[0:2])
         for s in range(LAG, last + 1):
-            num_names.extend((a_names[2 * s - 1], num_names[2 * (s - LAG) + 1]))
-            a_names.extend((num_names[2 * (s - LAG)], a_names[2 * s]))
+            num_names.extend((a_names[2 * s - (2 if s - 1 in (2, SHARED) else 1)], num_names[2 * (s - LAG) + 1]))
+            a_names.extend((num_names[2 * (s - LAG)], a_names[2 * s + (1 if s == SHARED else 0)]))
         out_name = A_BANKS[2]
 
         def make_a(u):
@@ -249,6 +250,14 @@ def tile_list_moisture_downscaling_kernel(
             den[u] = held("half_b%d" % u, [P, PACK, P], F32)
             nc.vector.scalar_tensor_tensor(den[u][:], by_slot(a_bank[u]), 0.0, num[u][:], ALU.max, ALU.subtract)
 
+        def make_positive(u):
+            positive[u] = held("positive%d" % u, [P, PACK, P], F32)
+            nc.scalar.activation(positive[u][:], by_slot(a_bank[u]), ACT.Relu)
+
+        def subtract_den(u):
+            den[u] = held("half_b%d" % u, [P, PACK, P], F32)
+            nc.gpsimd.tensor_tensor(den[u][:], positive[u][:], num[u][:], ALU.subtract)
+
         def make_root(u):
             rt, h = units[u]
             rsq[u] = ring.tile([P, PACK, P], F32, name="rsq", bufs=4)
@@ -273,7 +282,7 @@ def tile_list_moisture_downscaling_kernel(
                 nc.tensor.transpose(rsq_t[s, k][:, place, :], rsq[2 * s + e][:, t, :], ident[:])
 
         def make_factors(s, k):
-            if k == 0:
+            if s not in factor:
                 factor[s] = staged("factor%d" % s, [P, PACK, 2, P], F32, (s if s < 2 else 2 + s % 3) * FACTOR_BYTES)
             together = 2 if one_half(s) else 1
             for place in range(0, PACK, together):
@@ -294,21 +303,21 @@ def tile_list_moisture_downscaling_kernel(
         def quantize_z(s, cols):
             quantize(z_w[s][:, cols], z_s[s][:, cols], z_bf[s][:, cols, :])
 
-        def out_pass(acc, rt, h, cols):
+        def out_pass(acc, rt, h, cols, first=0):
             s, e = divmod(units.index((rt, h)), 2)
             nc.tensor.matmul_mx(acc, lhsT=z_w[s][:, e * P : (e + 1) * P].bitcast(FP8X4),
                                 lhsT_scale=z_s[s][:, e * P : (e + 1) * P],
                                 rhs=grid_w[h][:, cols].bitcast(FP8X4), rhs_scale=grid_s[h][:, cols],
-                                start=(h == 0), stop=(h == HALVES - 1))
+                                start=(h == first), stop=(h != first))
 
         def make_out(rt, name):
             out_bank[rt] = bank(name, [P, F])
             for h in range(HALVES):
                 out_pass(out_bank[rt][:], rt, h, slice(0, F))
 
-        def store_out(rt):
+        def store_out(rt, empty=nc.scalar.copy):
             result = ring.tile([P, F], F32, name="result", bufs=5)
-            nc.scalar.copy(result[:], out_bank[rt][:])
+            empty(result[:], out_bank[rt][:])
             nc.sync.dma_start(out[rt * P : (rt + 1) * P, :], result[:])
 
         def round_w3(c, name):
@@ -336,13 +345,16 @@ def tile_list_moisture_downscaling_kernel(
                 make_z(s - LAG, 1)
                 make_z(s - LAG, 0)
             if s >= 1:
-                make_root(early - 2)
-                make_root(late - 2)
+                for u in (late - 2, early - 2) if s - 1 == 2 else (early - 2, late - 2):
+                    make_root(u)
+            if s >= SHARED:
+                make_positive(late if s == SHARED else early)
             if s == 1:
                 make_a(early + 2)
                 make_a(late + 2)
-            for u in (early, late) if s == 0 else (late, early):
-                make_num(u)
+            make_num(early if s in (0, SHARED) else late)
+            if s < SHARED:
+                make_num(late if s == 0 else early)
             if s == 0:
                 round_w3(2, "in_turn")
             if s == 1:
@@ -380,47 +392,52 @@ def tile_list_moisture_downscaling_kernel(
                     quantize(grid_w[1][:, cols], grid_s[1][:, cols], grouped[:])
             for rt in outs_at.get(s, ()):
                 make_out(rt, out_name)
-            make_den(early)
+            if s >= SHARED:
+                make_num(late if s == SHARED else early)
+                subtract_den(late if s == SHARED else early)
+            else:
+                make_den(late if s == 2 else early)
             if s == 0:
                 quantize_w3(1)
                 make_a(2)
                 make_a(3)
             if 2 <= s < last:
                 make_a(late + 2)
-            make_den(late)
+            make_den(early if s in (2, SHARED) else late)
 
         early, late = 2 * last, 2 * last + 1
-        make_root(early)
         make_root(late)
+        make_root(early)
         for e in (1, 0):
             make_z(last - 2, e)
         free_names = a_names[count:]
         for e in range(2):
             turn_num(early - 2 + e, free_names[e])
-        for k in range(2):
+        for k in (1, 0):
             turn_roots(last, k)
-        turn_num(early, a_names[late])
-        turn_num(late, num_names[late - 4])
+        turn_num(late, a_names[late])
+        turn_num(early, num_names[late - 4])
         store_out(1)
-        for k in range(2):
+        for k in (1, 0):
             make_factors(last, k)
+        make_z(last - 1, 0)
         quantize_z(last - 2, slice(0, 2 * P))
         make_out(2, out_name)
         store_out(2)
-        for e in range(2):
-            make_z(last - 1, e)
-        make_z(last, 0)
-        quantize_z(last - 1, slice(0, 2 * P))
+        make_z(last - 1, 1)
         make_z(last, 1)
-        for e in range(2):
+        quantize_z(last - 1, slice(0, 2 * P))
+        make_z(last, 0)
+        for e in (1, 0):
             quantize_z(last, slice(e * P, (e + 1) * P))
-        for rt, name in ((3, ROOT_BANKS[0]), (4, num_names[early - 4])):
-            make_out(rt, name)
-            store_out(rt)
+        make_out(3, ROOT_BANKS[0])
+        store_out(3)
+        make_out(4, num_names[early - 4])
+        store_out(4, nc.vector.tensor_copy)
         last_banks = [bank(name, [P, HALF]) for name in free_names]
-        for h in range(HALVES):
+        for h in (1, 0):
             for side, cols in enumerate(sides):
-                out_pass(last_banks[side][:, 0 : F // 2], R_TILES - 1, h, cols)
+                out_pass(last_banks[side][:, 0 : F // 2], R_TILES - 1, h, cols, first=1)
         for side, empty in enumerate((nc.scalar.copy, nc.vector.tensor_copy)):
             part = ring.tile([P, F // 2], F32, name="part", bufs=2)
             empty(part[:], last_banks[side][:, 0 : F // 2])

@@ -127,6 +127,7 @@ def tile_list_moisture_downscaling_kernel(
         for r in range(4):
             nc.gpsimd.dma_start(w1_s[r:P:32, :, :].bitcast(I32),
                                 w1_scales[:, r:SCALE_ROWS:4, :].rearrange("a q c -> q a c").bitcast(I32))
+        nc.gpsimd.dma_start(const_rows[P - R_TILES : P, :], const.rearrange("(t p) -> t p", p=P))
 
         nc.sync.dma_start(list2[:], offs2)
         load_part(tab2_w[:].bitcast(I32), tab2_rows, 0, 4)
@@ -154,7 +155,6 @@ def tile_list_moisture_downscaling_kernel(
         load_part(tab_w[1][:], tab_rows[1], 4, 8)
         nc.sync.dma_start(w1_near[1][:].bitcast(I32), w1_rows[:, 1, 0 : H // 4])
         lift(v_s[1], picked_s, 4)
-        nc.sync.dma_start(const_rows[P - R_TILES : P, :], const.rearrange("(t p) -> t p", p=P))
         load_w3(1)
 
         nc.scalar.activation(rough[:], trust_t[:], ACT.Abs_reciprocal_sqrt)
@@ -337,7 +337,14 @@ def tile_list_moisture_downscaling_kernel(
         const_turned = bank(ROOT_BANKS[0], [P, P])
         nc.tensor.transpose(const_turned[:], const_rows[:], ident[:])
         nc.scalar.copy(const_t[:], const_turned[:, P - R_TILES : P])
-        round_w3(1, "w3_second")
+        second = [held("w3_second%d" % e, [P, P, PACK], BF16) for e in range(2)]
+        for e in range(2):
+            nc.scalar.copy(*weave(second[e][:], w3_raw[1][:, :, e * P : (e + 1) * P]))
+
+        def finish_second(e):
+            quantize(w3_w[1][:, e * P : (e + 1) * P], w3_s[1][:, e * P : (e + 1) * P], second[e][:])
+            make_a(2 + e)
+
         outs_at = {4: (0,), 5: (1,)}
         for s in range(last + 1):
             early, late = 2 * s, 2 * s + 1
@@ -352,13 +359,13 @@ def tile_list_moisture_downscaling_kernel(
             if s == 1:
                 make_a(early + 2)
                 make_a(late + 2)
-            make_num(early if s in (0, SHARED) else late)
+            make_num(early if s in (0, 1, SHARED) else late)
             if s < SHARED:
-                make_num(late if s == 0 else early)
+                make_num(late if s < 2 else early)
             if s == 0:
                 round_w3(2, "in_turn")
             if s == 1:
-                round_w3(3, "w3_second")
+                round_w3(3, "w3_second1")
             if s == 2:
                 second_half = [held("grid_left", [P, F // 2, PACK], BF16)]
                 nc.scalar.copy(*weave(second_half[0][:], grid_raw[1][:, :, sides[0]]))
@@ -398,12 +405,12 @@ def tile_list_moisture_downscaling_kernel(
             else:
                 make_den(late if s == 2 else early)
             if s == 0:
-                quantize_w3(1)
-                make_a(2)
-                make_a(3)
+                finish_second(0)
             if 2 <= s < last:
                 make_a(late + 2)
             make_den(early if s in (2, SHARED) else late)
+            if s == 0:
+                finish_second(1)
 
         early, late = 2 * last, 2 * last + 1
         make_root(late)

@@ -127,7 +127,6 @@ def tile_list_moisture_downscaling_kernel(
         for r in range(4):
             nc.gpsimd.dma_start(w1_s[r:P:32, :, :].bitcast(I32),
                                 w1_scales[:, r:SCALE_ROWS:4, :].rearrange("a q c -> q a c").bitcast(I32))
-        nc.gpsimd.dma_start(const_rows[P - R_TILES : P, :], const.rearrange("(t p) -> t p", p=P))
 
         nc.sync.dma_start(list2[:], offs2)
         load_part(tab2_w[:].bitcast(I32), tab2_rows, 0, 4)
@@ -137,14 +136,15 @@ def tile_list_moisture_downscaling_kernel(
         nc.sync.dma_start(tab_s[0:P:4, :].bitcast(I32), tab_scales.rearrange("a g t -> g a t").bitcast(I32))
         nc.sync.dma_start(trust_t[:].rearrange("p (h t) -> p h t", t=PACK),
                           trust.rearrange("(h p t) -> p h t", h=HALVES, t=PACK))
-        load_part(tab_w[0][:], tab_rows[0], 0, 4)
+        load_part(tab_w[0][:], tab_rows[0], 0, 3)
         for r in range(4):
             nc.sync.dma_start(w2_s[r:P:32, :].bitcast(I32), w2_scales[0, r:SCALE_ROWS:4, :].bitcast(I32))
-        load_part(tab_w[0][:], tab_rows[0], 4, 8)
         nc.sync.dma_start(w2_w[:], w2_words[0].rearrange("p c i -> p (c i)").bitcast(I32))
+        load_part(tab_w[0][:], tab_rows[0], 3, 6)
 
         nc.vector.tensor_copy(picked2_s[:], tab2_s[:].indirect(list2[:]))
         lift(v2_s, picked2_s, 0)
+        load_part(tab_w[0][:], tab_rows[0], 6, 8)
         for h in range(HALVES):
             nc.vector.tensor_copy(v2_w[h][:], tab2_w[:].indirect(half_list(list2, h)))
         nc.vector.tensor_copy(picked_s[:], tab_s[:].indirect(list1[:]))
@@ -194,6 +194,7 @@ def tile_list_moisture_downscaling_kernel(
 
         nc.vector.tensor_copy(v0_w[:], tab_w[0][:].bitcast(U32).indirect(list1[:]))
         load_w3(2)
+        nc.sync.dma_start(const_rows[P - R_TILES : P, :], const.rearrange("(t p) -> t p", p=P))
         load_grid(0)
         nc.sync.dma_start(w1_far[:].bitcast(I32), w1_rows[:, :, H // 4 : H // 2])
         load_w3(3)

import math
from contextlib import ExitStack

import concourse.mybir as mybir
from concourse.masks import make_identity

K, K2, T, S, H, F = 1024, 512, 4096, 1024, 768, 512
FLOPS = 2 * S * H * (K + 2 * K2) + 2 * S * H * F

F32 = mybir.dt.float32
BF16 = mybir.dt.bfloat16
I32 = mybir.dt.int32
U32 = mybir.dt.uint32
U16 = mybir.dt.uint16
U8 = mybir.dt.uint8
FP8X4 = mybir.dt.float8_e4m3fn_x4
FP4X4 = mybir.dt.float4_e2m1fn_x4
ALU = mybir.AluOpType
ACT = mybir.ActivationFunctionType

P = 128
PACK = 4
HALF = P * PACK
HALVES = S // HALF
R_TILES = H // P
SHARED = 4
SCALE_ROWS = 16
LAG = 3


def weave(grouped, slots):
    return (
        grouped.rearrange("p (c i) t -> p c t i", i=2),
        slots.rearrange("p t (c i) -> p c t i", i=2),
    )


def tile_list_moisture_downscaling_kernel(
    tc, tab_words, tab_scales, tab2_words, tab2_scales, offs, offs2, w1_words, w1_scales,
    w2_words, w2_scales, w3, const, trust, grid, out,
):
    nc = tc.nc
    with ExitStack() as ctx:
        keep = ctx.enter_context(tc.tile_pool(name="keep", bufs=1))
        loads = ctx.enter_context(tc.tile_pool(name="loads", bufs=1))
        ring = ctx.enter_context(tc.tile_pool(name="ring", bufs=1))
        stage = ctx.enter_context(tc.tile_pool(name="stage", bufs=1))
        psum = ctx.enter_context(tc.psum_pool(name="psum", bufs=1))

        def held(name, shape, dtype):
            return keep.tile(shape, dtype, name=name, align_bytes=64)

        def placed(name, shape, dtype, offset):
            return loads.tile(shape, dtype, name=name, align_bytes=64, offset=offset)

        def bank(name, shape):
            return psum.tile(shape, F32, name=name)

        A_BANKS = ("a0", "a1", "a2")
        NUM_BANKS = ("num0", "num1")
        ROOT_BANKS = ("root0", "root1")
        OUT_BANK = "o"

        TAB1, V1 = 0, 4 * T
        list1 = held("list1", [P, S // 16], U16)
        list2 = held("list2", [P, S // 16], U16)
        tab2_w = held("tab2_w", [P, T], U16)
        tab_w = [held("tab_w0", [P, T], I32), placed("tab_w1", [P, T], I32, TAB1)]
        tab_s = held("tab_s", [P, T], U8)
        tab2_s = held("tab2_s", [P, T], U8)
        w1_near = [held("w1_near%d" % a, [P, H], U8) for a in range(2)]
        w1_far = held("w1_far", [P, 2, H], U8)
        w1_rows = w1_words.rearrange("a p c -> p a c").bitcast(I32)
        w3_cuts = (0, P, 3 * P, 5 * P, H)
        w3_cols = [slice(c0, c1) for c0, c1 in zip(w3_cuts, w3_cuts[1:])]
        w3_raw = [held("w3_raw%d" % c, [P, PACK, cols.stop - cols.start], F32) for c, cols in enumerate(w3_cols)]
        grid_raw = [held("grid_raw%d" % h, [P, PACK, F], F32) for h in range(HALVES)]
        v2_w = [held("v2_w%d" % h, [P, HALF], U16) for h in range(HALVES)]
        w1_s = held("w1_s", [P, 2, H], U8)
        picked_s = held("picked_s", [P, S], U8)
        picked2_s = held("picked2_s", [P, S], U8)
        v_both = held("v_both", [P, 2, S], U8)
        v_s = [v_both[:, a, :] for a in range(2)]
        const_rows = held("const_rows", [P, P], F32)
        const_t = held("const_t", [P, R_TILES], F32)
        v0_w = held("v0_w", [P, S], U32)
        trust_t = held("trust_t", [P, HALVES * PACK], F32)
        rough = held("rough", [P, HALVES * PACK], F32)
        defect = held("defect", [P, HALVES * PACK], F32)
        root0 = held("root0", [P, HALVES * PACK], F32)
        root = held("root", [P, HALVES * PACK], F32)
        v2_s = held("v2_s", [P, S], U8)
        w2_w = held("w2_w", [P, H], I32)
        w2_s = held("w2_s", [P, H], U8)
        w3_w = {0: held("w3_w0", [P, P], U32)}
        w3_s = [held("w3_s%d" % c, [P, cols.stop - cols.start], U8) if c != 1 else None for c, cols in enumerate(w3_cols)]
        w3_s[1] = placed("w3_s_second", [P, 2 * P], U8, TAB1)
        grid_s = [held("grid_s%d" % h, [P, F], U8) for h in range(HALVES)]
        ident = held("ident", [P, P], F32)

        def load_w3(c):
            nc.sync.dma_start(w3_raw[c][:], w3[:, w3_cols[c]].rearrange("(p j) r -> p j r", j=PACK))

        def load_grid(h):
            nc.sync.dma_start(grid_raw[h][:], grid[h * HALF : (h + 1) * HALF, :].rearrange("(p j) n -> p j n", j=PACK))

        def load_part(tile, rows, c0, c1):
            cols = slice(c0 * rows.shape[1] // 8, c1 * rows.shape[1] // 8)
            nc.sync.dma_start(tile[:, cols], rows[:, cols])

        def lift(scale_tile, picked, first):
            for r in range(4):
                nc.sync.dma_start(scale_tile[r:P:32, :].bitcast(I32), picked[8 * r + first : P : 32, :].bitcast(I32))

        def half_list(offsets, h):
            return offsets[:, h * (HALF // 16) : (h + 1) * (HALF // 16)]

        tab_rows = [tab_words[a].rearrange("p t i -> p (t i)").bitcast(I32) for a in range(2)]
        tab2_rows = tab2_words[0].bitcast(I32)

        for scale_tile in (tab2_s[:], tab_s[:], w2_s[:], v2_s[:], v_both[:].rearrange("p a c -> p (a c)")):
            nc.vector.memset(scale_tile.bitcast(I32), 0)

        nc.vector.memset(const_rows[0 : P - R_TILES, :], 0.0)
        make_identity(nc, ident[:])
        nc.gpsimd.memset(w1_s[:].rearrange("p a c -> p (a c)").bitcast(I32), 0)
        for r in range(4):
            nc.gpsimd.dma_start(w1_s[r:P:32, :, :].bitcast(I32),
                                w1_scales[:, r:SCALE_ROWS:4, :].rearrange("a q c -> q a c").bitcast(I32))

        nc.sync.dma_start(list2[:], offs2)
        load_part(tab2_w[:].bitcast(I32), tab2_rows, 0, 4)
        nc.sync.dma_start(tab2_s[0:P:8, :].bitcast(I32), tab2_scales[0].bitcast(I32))
        load_part(tab2_w[:].bitcast(I32), tab2_rows, 4, 8)
        nc.sync.dma_start(list1[:], offs)
        nc.sync.dma_start(tab_s[0:P:4, :].bitcast(I32), tab_scales.rearrange("a g t -> g a t").bitcast(I32))
        nc.sync.dma_start(trust_t[:].rearrange("p (h t) -> p h t", t=PACK),
                          trust.rearrange("(h p t) -> p h t", h=HALVES, t=PACK))
        load_part(tab_w[0][:], tab_rows[0], 0, 3)
        for r in range(4):
            nc.sync.dma_start(w2_s[r:P:32, :].bitcast(I32), w2_scales[0, r:SCALE_ROWS:4, :].bitcast(I32))
        nc.sync.dma_start(w2_w[:], w2_words[0].rearrange("p c i -> p (c i)").bitcast(I32))
        load_part(tab_w[0][:], tab_rows[0], 3, 6)

        nc.vector.tensor_copy(picked2_s[:], tab2_s[:].indirect(list2[:]))
        lift(v2_s, picked2_s, 0)
        load_part(tab_w[0][:], tab_rows[0], 6, 8)
        for h in range(HALVES):
            nc.vector.tensor_copy(v2_w[h][:], tab2_w[:].indirect(half_list(list2, h)))
        nc.vector.tensor_copy(picked_s[:], tab_s[:].indirect(list1[:]))
        load_part(tab_w[1][:], tab_rows[1], 0, 4)
        load_w3(0)
        nc.sync.dma_start(w1_near[0][:].bitcast(I32), w1_rows[:, 0, 0 : H // 4])
        lift(v_s[0], picked_s, 0)
        load_part(tab_w[1][:], tab_rows[1], 4, 8)
        nc.sync.dma_start(w1_near[1][:].bitcast(I32), w1_rows[:, 1, 0 : H // 4])
        lift(v_s[1], picked_s, 4)
        load_w3(1)

        nc.scalar.activation(rough[:], trust_t[:], ACT.Abs_reciprocal_sqrt)
        nc.vector.tensor_tensor(root0[:], rough[:], trust_t[:], ALU.mult)
        nc.vector.scalar_tensor_tensor(defect[:], root0[:], -0.5 * math.sqrt(2.0), rough[:], ALU.mult, ALU.mult)
        nc.vector.scalar_tensor_tensor(root[:], defect[:], 1.5 * math.sqrt(2.0), root0[:], ALU.add, ALU.mult)

        steps = [((0, 0), (0, 1))]
        for rt in range(1, R_TILES - 1, 2):
            steps.extend(((rt, h), (rt + 1, h)) for h in range(HALVES))
        steps.append(((R_TILES - 1, 0), (R_TILES - 1, 1)))
        units = [unit for step in steps for unit in step]
        count, last = len(units), len(steps) - 1

        def by_slot(tile):
            return tile[:].rearrange("p (q t) -> p t q", t=PACK)

        half_b = {}

        def make_b(u, name):
            rt, h = units[u]
            acc = bank(name, [P, HALF])
            nc.tensor.matmul_mx(acc[:], lhsT=w2_w[:, rt * P : (rt + 1) * P].bitcast(FP8X4),
                                lhsT_scale=w2_s[:, rt * P : (rt + 1) * P],
                                rhs=v2_w[h][:].bitcast(FP4X4), rhs_scale=v2_s[:, h * HALF : (h + 1) * HALF],
                                start=True, stop=True)
            half_b[u] = held("half_b%d" % u, [P, PACK, P], F32)
            nc.scalar.activation(half_b[u][:], by_slot(acc), ACT.Copy, scale=0.5)

        def quantize(codes, scales, grouped):
            nc.vector.quantize_mx(out=codes.bitcast(FP8X4), scales=scales, in_=grouped.rearrange("p c t -> p (c t)"))

        b_names = ROOT_BANKS + NUM_BANKS + A_BANKS + (OUT_BANK,) + ROOT_BANKS + NUM_BANKS
        b_order = [u for h in range(HALVES) for u in range(count) if units[u][1] == h]
        for i, u in enumerate(b_order):
            make_b(u, b_names[i])

        nc.vector.tensor_copy(v0_w[:], tab_w[0][:].bitcast(U32).indirect(list1[:]))
        load_w3(2)
        nc.sync.dma_start(const_rows[P - R_TILES : P, :], const.rearrange("(t p) -> t p", p=P))
        load_grid(0)
        nc.sync.dma_start(w1_far[:].bitcast(I32), w1_rows[:, :, H // 4 : H // 2])
        load_w3(3)
        load_grid(1)
        w3_first = placed("w3_first", [P, P, PACK], BF16, V1)
        nc.vector.tensor_copy(*weave(w3_first[:], w3_raw[0][:]))
        v1_w = placed("v1_w", [P, S], U32, V1)
        quantize(w3_w[0][:], w3_s[0][:], w3_first[:])
        for h in range(HALVES):
            nc.vector.tensor_copy(v1_w[:, h * HALF : (h + 1) * HALF], tab_w[1][:].bitcast(U32).indirect(half_list(list1, h)))

        v_w = [[words[:, h * HALF : (h + 1) * HALF] for h in range(HALVES)] for words in (v0_w, v1_w)]
        a_bank, num, den, rsq, num_t, rsq_t, factor, z_bf, z_w, z_s, rounded, out_bank, positive = ({} for i in range(13))
        FACTOR_BYTES = 4 * PACK * 2 * P

        def staged(name, shape, dtype, offset):
            return stage.tile(shape, dtype, name=name, align_bytes=64, offset=offset)

        for c in range(1, len(w3_cols) - 1):
            w3_w[c] = held("w3_w%d" % c, [P, w3_cols[c].stop - w3_cols[c].start], U32)
        w3_w[3] = staged("w3_last", [P, P], U32, 4 * F)
        grid_w = [staged("grid_w%d" % h, [P, F], U32, h * FACTOR_BYTES) for h in range(HALVES)]

        a_names = list(A_BANKS) + [OUT_BANK] + list(NUM_BANKS) + [OUT_BANK, NUM_BANKS[1]]
        num_names = list(A_BANKS[0:2])
        for s in range(LAG, last + 1):
            num_names.extend((a_names[2 * s - (2 if s - 1 in (2, SHARED) else 1)], num_names[2 * (s - LAG) + 1]))
            a_names.extend((num_names[2 * (s - LAG)], a_names[2 * s + (1 if s == SHARED else 0)]))
        out_name = A_BANKS[2]

        def make_a(u):
            rt, h = units[u]
            acc = bank(a_names[u], [P, HALF])
            c = max(c for c, cols in enumerate(w3_cols) if cols.start <= rt * P)
            off = rt * P - w3_cols[c].start
            pixels = slice(h * HALF, (h + 1) * HALF)
            near, first = rt < R_TILES // 2, 2 * (rt % (R_TILES // 2)) * P
            w1_cols = [(w1_near[a][:] if near else w1_far[:, a, :])[:, first : first + 2 * P] for a in range(2)]
            from_tab = [(w1_cols[a].bitcast(FP4X4), w1_s[:, a, rt * P : (rt + 1) * P],
                         v_w[a][h].bitcast(FP8X4), v_s[a][:, pixels]) for a in range(2)]
            from_tab2 = [(w3_w[c][:, off : off + P].bitcast(FP8X4), w3_s[c][:, off : off + P],
                          v2_w[h][:].bitcast(FP4X4), v2_s[:, pixels])]
            passes = from_tab2 + from_tab if rt == 0 else from_tab + from_tab2
            for k, (weights, weight_scales, moving, moving_scales) in enumerate(passes):
                nc.tensor.matmul_mx(acc[:], lhsT=weights, lhsT_scale=weight_scales, rhs=moving, rhs_scale=moving_scales,
                                    start=(k == 0), stop=(k == len(passes) - 1))
            a_bank[u] = acc

        def make_num(u):
            num[u] = ring.tile([P, PACK, P], F32, name="num", bufs=6)
            nc.vector.scalar_tensor_tensor(num[u][:], by_slot(a_bank[u]), 0.5, half_b[u][:], ALU.mult, ALU.subtract)

        def make_den(u):
            den[u] = held("half_b%d" % u, [P, PACK, P], F32)
            nc.vector.scalar_tensor_tensor(den[u][:], by_slot(a_bank[u]), 0.0, num[u][:], ALU.max, ALU.subtract)

        def make_positive(u):
            positive[u] = held("positive%d" % u, [P, PACK, P], F32)
            nc.scalar.activation(positive[u][:], by_slot(a_bank[u]), ACT.Relu)

        def subtract_den(u):
            den[u] = held("half_b%d" % u, [P, PACK, P], F32)
            nc.gpsimd.tensor_tensor(den[u][:], positive[u][:], num[u][:], ALU.subtract)

        def make_root(u):
            rt, h = units[u]
            rsq[u] = ring.tile([P, PACK, P], F32, name="rsq", bufs=4)
            nc.scalar.activation(rsq[u][:], den[u][:], ACT.Abs_reciprocal_sqrt, bias=const_t[:, rt : rt + 1], scale=2.0)

        def turn_num(u, name):
            num_t[u] = bank(name, [P, PACK, P])
            for t in range(PACK):
                nc.tensor.transpose(num_t[u][:, t, :], num[u][:, t, :], ident[:])

        def one_half(s):
            return steps[s][0][1] == steps[s][1][1]

        def root_blocks(s, k):
            if one_half(s):
                return [(e, t) for t in (2 * k, 2 * k + 1) for e in range(2)]
            return [(k, t) for t in range(PACK)]

        def turn_roots(s, k):
            rsq_t[s, k] = bank(ROOT_BANKS[k], [P, PACK, P])
            for place, (e, t) in enumerate(root_blocks(s, k)):
                nc.tensor.transpose(rsq_t[s, k][:, place, :], rsq[2 * s + e][:, t, :], ident[:])

        def make_factors(s, k):
            if s not in factor:
                factor[s] = staged("factor%d" % s, [P, PACK, 2, P], F32, (s if s < 2 else 2 + s % 3) * FACTOR_BYTES)
            together = 2 if one_half(s) else 1
            for place in range(0, PACK, together):
                e, t = root_blocks(s, k)[place]
                slot = steps[s][e][1] * PACK + t
                nc.scalar.activation(factor[s][:, t, e : e + together, :], rsq_t[s, k][:, place : place + together, :],
                                     ACT.Square, scale=root[:, slot : slot + 1])

        def make_z(s, e):
            if s not in z_bf:
                z_bf[s] = held("z_bf%d" % s, [P, 2 * P, PACK], BF16)
                z_w[s] = held("z_w%d" % s, [P, 2 * P], U32)
                z_s[s] = held("z_s%d" % s, [P, 2 * P], U8)
            grouped = z_bf[s][:, e * P : (e + 1) * P, :]
            dst, src = weave(grouped, num_t[2 * s + e][:])
            nc.vector.tensor_tensor(dst, src, weave(grouped, factor[s][:, :, e, :])[1], ALU.mult)

        def quantize_z(s, cols):
            quantize(z_w[s][:, cols], z_s[s][:, cols], z_bf[s][:, cols, :])

        def out_pass(acc, rt, h, cols, first=0):
            s, e = divmod(units.index((rt, h)), 2)
            nc.tensor.matmul_mx(acc, lhsT=z_w[s][:, e * P : (e + 1) * P].bitcast(FP8X4),
                                lhsT_scale=z_s[s][:, e * P : (e + 1) * P],
                                rhs=grid_w[h][:, cols].bitcast(FP8X4), rhs_scale=grid_s[h][:, cols],
                                start=(h == first), stop=(h != first))

        def make_out(rt, name):
            out_bank[rt] = bank(name, [P, F])
            for h in range(HALVES):
                out_pass(out_bank[rt][:], rt, h, slice(0, F))

        def store_out(rt, empty=nc.scalar.copy):
            result = ring.tile([P, F], F32, name="result", bufs=5)
            empty(result[:], out_bank[rt][:])
            nc.sync.dma_start(out[rt * P : (rt + 1) * P, :], result[:])

        def round_w3(c, name):
            rounded["w3", c] = held(name, [P, w3_cols[c].stop - w3_cols[c].start, PACK], BF16)
            nc.scalar.copy(*weave(rounded["w3", c][:], w3_raw[c][:]))

        def round_on_gpsimd(grouped, raw):
            nc.gpsimd.tensor_scalar(grouped, raw.rearrange("p t c -> p c t"), 1.0, 0.0, ALU.mult, ALU.add)

        sides = [slice(0, F // 2), slice(F // 2, F)]

        def quantize_w3(c):
            quantize(w3_w[c][:], w3_s[c][:], rounded["w3", c][:])

        make_a(0)
        make_a(1)
        const_turned = bank(ROOT_BANKS[0], [P, P])
        nc.tensor.transpose(const_turned[:], const_rows[:], ident[:])
        nc.scalar.copy(const_t[:], const_turned[:, P - R_TILES : P])
        second = [held("w3_second%d" % e, [P, P, PACK], BF16) for e in range(2)]
        for e in range(2):
            nc.scalar.copy(*weave(second[e][:], w3_raw[1][:, :, e * P : (e + 1) * P]))

        def finish_second(e):
            quantize(w3_w[1][:, e * P : (e + 1) * P], w3_s[1][:, e * P : (e + 1) * P], second[e][:])
            make_a(2 + e)

        outs_at = {4: (0,), 5: (1,)}
        for s in range(last + 1):
            early, late = 2 * s, 2 * s + 1
            if s >= LAG:
                make_z(s - LAG, 1)
                make_z(s - LAG, 0)
            if s >= 1:
                for u in (late - 2, early - 2) if s - 1 == 2 else (early - 2, late - 2):
                    make_root(u)
            if s >= SHARED:
                make_positive(late if s == SHARED else early)
            if s == 1:
                make_a(early + 2)
                make_a(late + 2)
            make_num(early if s in (0, 1, SHARED) else late)
            if s < SHARED:
                make_num(late if s < 2 else early)
            if s == 0:
                round_w3(2, "in_turn")
            if s == 1:
                round_w3(3, "w3_second1")
            if s == 2:
                second_half = [held("grid_left", [P, F // 2, PACK], BF16)]
                nc.scalar.copy(*weave(second_half[0][:], grid_raw[1][:, :, sides[0]]))
            for rt in outs_at.get(s - 1, ()):
                store_out(rt)
            if s >= 1:
                for k in range(2):
                    turn_roots(s - 1, k)
                for k in range(2):
                    make_factors(s - 1, k)
            if 2 <= s < last:
                make_a(early + 2)
            if s == 1 or s >= LAG:
                for u in (0, 1) if s == 1 else (early - 4, late - 4):
                    turn_num(u, num_names[u])
            if s >= LAG:
                quantize_z(s - LAG, slice(0, 2 * P))
            if s == 1:
                quantize_w3(2)
            if s == 3:
                quantize_w3(3)
            if s == 1:
                first_half = held("in_turn", [P, F, PACK], BF16)
                round_on_gpsimd(first_half[:], grid_raw[0][:])
            if s == 3:
                quantize(grid_w[0][:], grid_s[0][:], first_half[:])
                second_half.append(held("in_turn", [P, F // 2, PACK], BF16))
                round_on_gpsimd(second_half[1][:], grid_raw[1][:, :, sides[1]])
            if s == 4:
                for grouped, cols in zip(second_half, sides):
                    quantize(grid_w[1][:, cols], grid_s[1][:, cols], grouped[:])
            for rt in outs_at.get(s, ()):
                make_out(rt, out_name)
            if s >= SHARED:
                make_num(late if s == SHARED else early)
                subtract_den(late if s == SHARED else early)
            else:
                make_den(late if s == 2 else early)
            if s == 0:
                finish_second(0)
            if 2 <= s < last:
                make_a(late + 2)
            make_den(early if s in (2, SHARED) else late)
            if s == 0:
                finish_second(1)

        early, late = 2 * last, 2 * last + 1
        make_root(late)
        make_root(early)
        for e in (1, 0):
            make_z(last - 2, e)
        free_names = a_names[count:]
        for e in range(2):
            turn_num(early - 2 + e, free_names[e])
        for k in (1, 0):
            turn_roots(last, k)
        turn_num(late, a_names[late])
        turn_num(early, num_names[late - 4])
        store_out(1)
        for k in (1, 0):
            make_factors(last, k)
        make_z(last - 1, 0)
        quantize_z(last - 2, slice(0, 2 * P))
        make_out(2, out_name)
        store_out(2)
        make_z(last - 1, 1)
        make_z(last, 1)
        quantize_z(last - 1, slice(0, 2 * P))
        make_z(last, 0)
        for e in (1, 0):
            quantize_z(last, slice(e * P, (e + 1) * P))
        make_out(3, ROOT_BANKS[0])
        store_out(3)
        make_out(4, num_names[early - 4])
        store_out(4, nc.vector.tensor_copy)
        last_banks = [bank(name, [P, HALF]) for name in free_names]
        for h in (1, 0):
            for side, cols in enumerate(sides):
                out_pass(last_banks[side][:, 0 : F // 2], R_TILES - 1, h, cols, first=1)
        for side, empty in enumerate((nc.scalar.copy, nc.vector.tensor_copy)):
            part = ring.tile([P, F // 2], F32, name="part", bufs=2)
            empty(part[:], last_banks[side][:, 0 : F // 2])
            nc.sync.dma_start(out[H - P : H, sides[side]], part[:])
